import numpy as np
import ml_dtypes


def mxq(x, axis, fmt="e4m3"):
    dtype, down = {"e4m3": (ml_dtypes.float8_e4m3fn, 7), "e5m2": (ml_dtypes.float8_e5m2, 14)}[fmt]
    v = np.moveaxis(np.asarray(x, np.float32).astype(ml_dtypes.bfloat16).astype(np.float64), axis, -1)
    blocks = v.reshape(v.shape[:-1] + (-1, 32))
    amax = np.abs(blocks).max(-1, keepdims=True)
    byte = np.maximum(np.where(amax > 0, np.frexp(amax)[1] - 1 + 127, 0) - down, 1)
    scale = np.exp2(byte - 127.0)
    codes = (blocks / scale).astype(np.float32).astype(dtype).astype(np.float64)
    return np.moveaxis((codes * scale).reshape(v.shape), -1, axis)


WIDE = False


def mx_kscale(k):
    if not WIDE:
        return np.ones(k)
    levels = np.array([18, -18])
    if k % 512:
        return np.exp2(np.random.permutation(np.resize(levels, k // 32))).repeat(32)
    a = np.empty((k // 512, 16))
    for p in range(k // 512):
        a[p, :8] = np.random.permutation(np.resize(levels, 8))
        for g in range(8):
            far = levels[np.abs(levels - a[p, g]) >= 10]
            a[p, g + 8] = far[np.random.randint(len(far))]
    return np.exp2(a.ravel()).repeat(32)


def f64(x):
    return np.asarray(x).astype(np.float64)


def striped(idx):
    return np.tile(np.asarray(idx).reshape(-1, 16).T, (8, 1)).astype(np.uint16)


def unstriped(offs):
    return offs[:16].T.reshape(-1).astype(np.int64)


E2M1 = np.array([0.0, 0.5, 1.0, 1.5, 2.0, 3.0, 4.0, 6.0, -0.0, -0.5, -1.0, -1.5, -2.0, -3.0, -4.0, -6.0])


def pack_weight(w, fmt):
    k, n = w.shape
    w = f64(np.asarray(w, np.float32).astype(ml_dtypes.bfloat16)).reshape(k // 32, 32, n)
    amax = np.abs(w).max(1)
    if fmt == "e4m3":
        byte = np.frexp(amax)[1] - 1 + 127 - 7
    else:
        mant, ex = np.frexp(amax / 6.0)
        byte = np.where(mant > 0.5, ex, ex - 1) + 127
    byte = np.clip(np.where(amax > 0, byte, 1), 1, 254)
    scaled = (w * np.exp2(127.0 - byte)[:, None, :]).reshape(k, n).astype(np.float32)
    by_word = np.ascontiguousarray(scaled.reshape(k // 512, 128, 4, n).transpose(0, 1, 3, 2))
    if fmt == "e4m3":
        words = by_word.astype(ml_dtypes.float8_e4m3fn).view(np.uint8)
    else:
        c = by_word.astype(ml_dtypes.float4_e2m1fn).view(np.uint8) & 0xF
        words = (c[..., 0::2] | (c[..., 1::2] << 4)).reshape(k // 512, 128, 2 * n)
    return np.ascontiguousarray(words), np.ascontiguousarray(byte.astype(np.uint8).reshape(k // 512, 16, n))


def unpack_weight(words, scales, fmt):
    g, _, n = scales.shape
    words = np.ascontiguousarray(words).reshape(g, 128, n, -1)
    if fmt == "e4m3":
        vals = words.view(ml_dtypes.float8_e4m3fn).astype(np.float64)
    else:
        nib = np.empty((g, 128, n, 4), np.uint8)
        nib[..., 0::2] = words & 0xF
        nib[..., 1::2] = words >> 4
        vals = E2M1[nib]
    vals = vals * np.repeat(np.exp2(scales.astype(np.float64) - 127.0), 8, axis=1)[..., None]
    return vals.transpose(0, 1, 3, 2).reshape(g * 512, n)


B, N, T, D, DV, R = 2, 512, 2048, 512, 512, 512


def setup_inputs():
    n = np.random.standard_normal
    idx = np.random.permutation(T)[:B * N]
    s = mx_kscale(D)[:, None]
    z = mx_kscale(R)[:, None]
    v = mx_kscale(DV)[:, None]
    q = n((B, D, R))
    do = n((B, DV, R))
    kp = pack_weight(n((D, T)) * (0.50 / np.sqrt(D)) / s, "e4m3")
    vp = pack_weight(n((DV, T)) / np.sqrt(DV) / v, "e4m3")
    return {
        "qT": (q * s).astype(np.float32),
        "k_words": kp[0],
        "k_scales": kp[1],
        "v_words": vp[0],
        "v_scales": vp[1],
        "doT": (do * v).astype(np.float32),
        "lse": (np.log(N) + 0.12 + 0.1 * n((B, R, 1))).astype(np.float32),
        "delta": (0.3 * n((B, R, 1))).astype(np.float32),
        "rw": (np.random.uniform(0.5, 1.5, (B, R, 1)) * N / np.sqrt(R) * z).astype(np.float32),
        "qm": (q.transpose(0, 2, 1) / z).astype(np.float32),
        "dom": (do.transpose(0, 2, 1) / z).astype(np.float32),
        "offs": striped(idx),
    }


def reference(qT, k_words, k_scales, v_words, v_scales, doT, lse, delta, rw, qm, dom, offs):
    idx = unstriped(offs)
    v = unpack_weight(v_words, v_scales, "e4m3")
    k = unpack_weight(k_words, k_scales, "e4m3")
    pick = lambda x: x[:, idx].reshape(x.shape[0], B, N).transpose(1, 0, 2)
    a = mxq(f64(qT), 1, "e4m3").transpose(0, 2, 1) @ pick(k)
    p = np.exp(a - f64(lse))
    dp = mxq(f64(doT), 1, "e5m2").transpose(0, 2, 1) @ pick(v)
    ds = f64(rw) * p * (dp - f64(delta))
    dk = mxq(f64(qm), 1, "e4m3").transpose(0, 2, 1) @ mxq(ds, 1, "e5m2")
    dv = mxq(f64(dom), 1, "e5m2").transpose(0, 2, 1) @ mxq(f64(rw) * p, 1, "e4m3")
    gk = np.zeros((D, T))
    gk[:, idx] = dk.transpose(1, 0, 2).reshape(D, B * N)
    gv = np.zeros((DV, T))
    gv[:, idx] = dv.transpose(1, 0, 2).reshape(DV, B * N)
    return gk, gv

@@ -1,0 +1,200 @@
+from contextlib import ExitStack
+
+import concourse.mybir as mybir
+
+B, N, T, D, DV, R = 2, 512, 2048, 512, 512, 512
+FLOPS = 4 * 2 * B * R * N * D
+
+F32 = mybir.dt.float32
+BF16 = mybir.dt.bfloat16
+I32 = mybir.dt.int32
+U32 = mybir.dt.uint32
+U16 = mybir.dt.uint16
+U8 = mybir.dt.uint8
+E4M3 = mybir.dt.float8_e4m3fn_x4
+E5M2 = mybir.dt.float8_e5m2_x4
+ACT = mybir.ActivationFunctionType
+ALU = mybir.AluOpType
+
+P = 128
+PACK = 4
+LIST_COLS = N // 16
+
+
+def tile_attend_gat_lse_kv_kernel(
+    tc, qT, k_words, k_scales, v_words, v_scales, doT, lse, delta, rw, qm, dom, offs, out_0, out_1
+):
+    nc = tc.nc
+    with ExitStack() as ctx:
+        held = ctx.enter_context(tc.tile_pool(name="held", bufs=1))
+        raws = ctx.enter_context(tc.tile_pool(name="raws", bufs=5))
+        groups = ctx.enter_context(tc.tile_pool(name="groups", bufs=6))
+        score_banks = ctx.enter_context(tc.psum_pool(name="score_banks", bufs=4))
+        grad_banks = ctx.enter_context(tc.psum_pool(name="grad_banks", bufs=4))
+
+        offsets = held.tile([P, B * LIST_COLS], U16, name="offsets")
+        nc.sync.dma_start(offsets[:], offs)
+
+        def load_rows(rows):
+            raw = raws.tile([P, PACK, 512], F32, name="raw")
+            nc.sync.dma_start(out=raw[:], in_=rows.rearrange("(p j) w -> p j w", j=PACK))
+            return raw
+
+        def load_words(words, name):
+            pool_words = held.tile([P, T], U32, name=name)
+            nc.sync.dma_start(out=pool_words[:].bitcast(I32), in_=words[0].rearrange("p n t -> p (n t)").bitcast(I32))
+            return pool_words
+
+        def load_scales(scales, name):
+            pool_scales = held.tile([P, T], U8, name=name)
+            nc.vector.memset(pool_scales[:].bitcast(I32), 0)
+            for quad in range(4):
+                nc.sync.dma_start(
+                    out=pool_scales[32 * quad : 32 * quad + 4, :].bitcast(I32),
+                    in_=scales[0, 4 * quad : 4 * quad + 4, :].bitcast(I32),
+                )
+            return pool_scales
+
+        def load_per_query(vec, name):
+            col = held.tile([P, B, PACK], F32, name=name)
+            nc.scalar.dma_start(out=col[:], in_=vec.rearrange("b (p t) o -> p b (t o)", t=PACK))
+            return col
+
+        lse_sb = load_per_query(lse, "lse_sb")
+        rw_sb = load_per_query(rw, "rw_sb")
+        delta_sb = load_per_query(delta, "delta_sb")
+
+        warm = held.tile([P, 1], F32, name="warm")
+        nc.vector.memset(warm[:], 0.0)
+        warm_out = held.tile([P, 1], F32, name="warm_out")
+        nc.scalar.activation(warm_out[:], warm[:], ACT.Exp)
+
+        q_raw = [load_rows(qT[0])]
+        k_pool_scales = load_scales(k_scales, "k_pool_scales")
+        k_pool_words = load_words(k_words, "k_pool_words")
+        dom_raw = [load_rows(dom[0])]
+        q_raw.append(load_rows(qT[1]))
+        v_pool_scales = load_scales(v_scales, "v_pool_scales")
+        dom_raw.append(load_rows(dom[1]))
+        v_pool_words = load_words(v_words, "v_pool_words")
+
+        neg_lse = held.tile([P, B, PACK], F32, name="neg_lse")
+        nc.vector.tensor_scalar_mul(neg_lse[:], lse_sb[:], -1.0)
+        neg_rw_delta = held.tile([P, B * PACK], F32, name="neg_rw_delta")
+        nc.vector.scalar_tensor_tensor(
+            neg_rw_delta[:], delta_sb[:].rearrange("p b t -> p (b t)"), -1.0, rw_sb[:].rearrange("p b t -> p (b t)"), ALU.mult, ALU.mult
+        )
+
+        def gather(pool_tile, b, dtype, name):
+            picked = held.tile([P, N], dtype, name=name, align_bytes=64)
+            nc.vector.tensor_copy(picked[:], pool_tile[:].indirect(offsets[:, b * LIST_COLS : (b + 1) * LIST_COLS]))
+            return picked
+
+        def quantize(grouped, fmt, name):
+            codes = held.tile([P, 512], U32, name=name + "_codes", align_bytes=64)
+            scales = held.tile([P, 512], U8, name=name + "_scales", align_bytes=64)
+            nc.vector.quantize_mx(out=codes[:].bitcast(fmt), scales=scales[:], in_=grouped[:])
+            return codes, scales, fmt
+
+        def new_grouped():
+            return groups.tile([P, 512 * PACK], BF16, name="grouped", align_bytes=64)
+
+        def interleaved(grouped):
+            return grouped[:].rearrange("p (c i t) -> p c t i", i=4, t=PACK)
+
+        def by_fours(planes):
+            return planes[:].rearrange("p t (c i) -> p c t i", i=4)
+
+        def cast_plain(raw):
+            grouped = new_grouped()
+            nc.scalar.copy(interleaved(grouped), by_fours(raw))
+            return grouped
+
+        def cast_by_query(raw):
+            grouped = new_grouped()
+            nc.scalar.copy(
+                grouped[:].rearrange("p (t m j) -> p m j t", t=PACK, j=PACK),
+                raw[:].rearrange("p j (m t) -> p m j t", t=PACK),
+            )
+            return grouped
+
+        def product(banks, stationary, c, moving):
+            bank = banks.tile([P, 512], F32, name="bank")
+            cols = slice(c * P, (c + 1) * P)
+            nc.tensor.matmul_mx(
+                out=bank[:],
+                lhsT=stationary[0][:, cols].bitcast(stationary[2]),
+                lhsT_scale=stationary[1][:, cols],
+                rhs=moving[0][:].bitcast(moving[2]),
+                rhs_scale=moving[1][:],
+                start=True,
+                stop=True,
+            )
+            return bank
+
+        p_planes, dv_staged = [], []
+        for b in range(B):
+            q_mx = quantize(cast_by_query(q_raw[b]), E4M3, f"q{b}")
+            k_s = gather(k_pool_scales, b, U8, f"k_s{b}")
+            k_w = gather(k_pool_words, b, U32, f"k_w{b}")
+            p = held.tile([P, PACK, N], F32, name=f"p{b}")
+            for t in range(PACK):
+                bank = product(score_banks, q_mx, t, (k_w, k_s, E4M3))
+                nc.scalar.activation(p[:, t, :], bank[:], ACT.Exp, bias=neg_lse[:, b, t : t + 1])
+            p_planes.append(p)
+            pw = new_grouped()
+            if b == 0:
+                gate = rw_sb[:, b, :].unsqueeze(1).unsqueeze(3).broadcast_to([P, N // 4, PACK, 4])
+                nc.vector.tensor_tensor(interleaved(pw), by_fours(p), gate, ALU.mult)
+            else:
+                pw_planes = held.tile([P, PACK, N], F32, name="pw_planes")
+                for t in range(PACK):
+                    nc.scalar.activation(pw_planes[:, t, :], p[:, t, :], ACT.Copy, scale=rw_sb[:, b, t : t + 1])
+                nc.scalar.copy(interleaved(pw), by_fours(pw_planes))
+            dom_mx = quantize(cast_plain(dom_raw[b]), E5M2, f"dom{b}")
+            pw_mx = quantize(pw, E4M3, f"pw{b}")
+            staged = []
+            for c in range(DV // P):
+                bank = product(grad_banks, dom_mx, c, pw_mx)
+                st = held.tile([P, N], F32, name=f"dv{b}_{c}")
+                nc.scalar.copy(st[:], bank[:])
+                staged.append(st)
+            dv_staged.append(staged)
+
+        do_raw = [load_rows(doT[b]) for b in range(B)]
+        qm_raw = [load_rows(qm[b]) for b in range(B)]
+        dk_staged = []
+        for b in range(B):
+            do_mx = quantize(cast_by_query(do_raw[b]), E5M2, f"do{b}")
+            v_s = gather(v_pool_scales, b, U8, f"v_s{b}")
+            v_w = gather(v_pool_words, b, U32, f"v_w{b}")
+            g = held.tile([P, PACK, N], F32, name=f"g{b}")
+            for t in range(PACK):
+                bank = product(score_banks, do_mx, t, (v_w, v_s, E4M3))
+                col = b * PACK + t
+                nc.scalar.activation(
+                    g[:, t, :], bank[:], ACT.Identity, bias=neg_rw_delta[:, col : col + 1], scale=rw_sb[:, b, t : t + 1]
+                )
+            ds = new_grouped()
+            nc.vector.tensor_tensor(interleaved(ds), by_fours(p_planes[b]), by_fours(g), ALU.mult)
+            qm_mx = quantize(cast_plain(qm_raw[b]), E4M3, f"qm{b}")
+            ds_mx = quantize(ds, E5M2, f"ds{b}")
+            staged = []
+            for c in range(D // P):
+                bank = product(grad_banks, qm_mx, c, ds_mx)
+                st = held.tile([P, N], F32, name=f"dk{b}_{c}")
+                nc.scalar.copy(st[:], bank[:])
+                staged.append(st)
+            dk_staged.append(staged)
+
+        windows = [held.tile([P, T], F32, name=f"window{c}") for c in range(DV // P)]
+        for window in windows:
+            nc.vector.memset(window[:].bitcast(I32), 0)
+        for staged, out in ((dv_staged, out_1), (dk_staged, out_0)):
+            for b in range(B):
+                for c in range(DV // P):
+                    nc.vector.tensor_copy(
+                        windows[c][:].indirect(offsets[:, b * LIST_COLS : (b + 1) * LIST_COLS]), staged[b][c][:]
+                    )
+                    if b == B - 1:
+                        nc.sync.dma_start(out=out[c * P : (c + 1) * P, :], in_=windows[c][:])

@@ -27,71 +27,71 @@ def tile_attend_gat_lse_kv_kernel(
     nc = tc.nc
     with ExitStack() as ctx:
         held = ctx.enter_context(tc.tile_pool(name="held", bufs=1))
-        raws = ctx.enter_context(tc.tile_pool(name="raws", bufs=5))
         groups = ctx.enter_context(tc.tile_pool(name="groups", bufs=6))
-        score_banks = ctx.enter_context(tc.psum_pool(name="score_banks", bufs=4))
-        grad_banks = ctx.enter_context(tc.psum_pool(name="grad_banks", bufs=4))
+        psum = ctx.enter_context(tc.psum_pool(name="psum", bufs=1))
+        banks = [psum.tile([P, 512], F32, name=f"bank{n}") for n in range(8)]
 
         offsets = held.tile([P, B * LIST_COLS], U16, name="offsets")
         nc.sync.dma_start(offsets[:], offs)
 
-        def load_rows(rows):
-            raw = raws.tile([P, PACK, 512], F32, name="raw")
+        def load_rows(raw, rows):
             nc.sync.dma_start(out=raw[:], in_=rows.rearrange("(p j) w -> p j w", j=PACK))
-            return raw
 
-        def load_words(words, name):
-            pool_words = held.tile([P, T], U32, name=name)
+        def load_words(words):
+            pool_words = held.tile([P, T], U32, name="pool_words", tag="pool_words")
             nc.sync.dma_start(out=pool_words[:].bitcast(I32), in_=words[0].rearrange("p n t -> p (n t)").bitcast(I32))
             return pool_words
 
-        def load_scales(scales, name):
-            pool_scales = held.tile([P, T], U8, name=name)
-            nc.vector.memset(pool_scales[:].bitcast(I32), 0)
+        def load_scales(queue, scales, name):
+            pool_scales = held.tile([P, T], U8, name=name, tag=name, align_bytes=64)
+            nc.gpsimd.memset(pool_scales[:].bitcast(I32), 0)
             for quad in range(4):
-                nc.sync.dma_start(
+                queue.dma_start(
                     out=pool_scales[32 * quad : 32 * quad + 4, :].bitcast(I32),
                     in_=scales[0, 4 * quad : 4 * quad + 4, :].bitcast(I32),
                 )
             return pool_scales
 
-        def load_per_query(vec, name):
+        def load_per_query(queue, vec, name):
             col = held.tile([P, B, PACK], F32, name=name)
-            nc.scalar.dma_start(out=col[:], in_=vec.rearrange("b (p t) o -> p b (t o)", t=PACK))
+            queue.dma_start(out=col[:], in_=vec.rearrange("b (p t) o -> p b (t o)", t=PACK))
             return col
 
-        lse_sb = load_per_query(lse, "lse_sb")
-        rw_sb = load_per_query(rw, "rw_sb")
-        delta_sb = load_per_query(delta, "delta_sb")
-
-        warm = held.tile([P, 1], F32, name="warm")
-        nc.vector.memset(warm[:], 0.0)
-        warm_out = held.tile([P, 1], F32, name="warm_out")
+        k_pool_scales = load_scales(nc.sync, k_scales, "k_pool_scales")
+        warm = held.tile([P, 1], F32, name="warm", tag="pool_words")
+        nc.gpsimd.memset(warm[:], 0.0)
+        warm_out = held.tile([P, 1], F32, name="warm_out", tag="query_rows")
         nc.scalar.activation(warm_out[:], warm[:], ACT.Exp)
 
-        q_raw = [load_rows(qT[0])]
-        k_pool_scales = load_scales(k_scales, "k_pool_scales")
-        k_pool_words = load_words(k_words, "k_pool_words")
-        dom_raw = [load_rows(dom[0])]
-        q_raw.append(load_rows(qT[1]))
-        v_pool_scales = load_scales(v_scales, "v_pool_scales")
-        dom_raw.append(load_rows(dom[1]))
-        v_pool_words = load_words(v_words, "v_pool_words")
+        feature_rows = held.tile([P, PACK, 512], F32, name="feature_rows")
+        query_rows = held.tile([P, PACK, 512], F32, name="query_rows", tag="query_rows")
+        load_rows(feature_rows, qT[0])
+        k_pool_words = load_words(k_words)
+        load_rows(query_rows, dom[0])
+        lse_sb = load_per_query(nc.sync, lse, "lse_sb")
+        v_pool_scales = load_scales(nc.sync, v_scales, "v_pool_scales")
+        rw_sb = load_per_query(nc.gpsimd, rw, "rw_sb")
+        delta_sb = load_per_query(nc.gpsimd, delta, "delta_sb")
 
         neg_lse = held.tile([P, B, PACK], F32, name="neg_lse")
-        nc.vector.tensor_scalar_mul(neg_lse[:], lse_sb[:], -1.0)
-        neg_rw_delta = held.tile([P, B * PACK], F32, name="neg_rw_delta")
-        nc.vector.scalar_tensor_tensor(
-            neg_rw_delta[:], delta_sb[:].rearrange("p b t -> p (b t)"), -1.0, rw_sb[:].rearrange("p b t -> p (b t)"), ALU.mult, ALU.mult
-        )
+        nc.gpsimd.tensor_scalar_mul(neg_lse[:], lse_sb[:], -1.0)
+        neg_delta = held.tile([P, B, PACK], F32, name="neg_delta")
+        nc.gpsimd.tensor_scalar_mul(neg_delta[:], delta_sb[:], -1.0)
+        neg_rw_delta = held.tile([P, B, PACK], F32, name="neg_rw_delta")
+        nc.gpsimd.tensor_tensor(neg_rw_delta[:], neg_delta[:], rw_sb[:], ALU.mult)
+
+        windows = [held.tile([P, T], F32, name=f"window{c}") for c in range(DV // P)]
+        for window in windows:
+            for first in range(0, T, 512):
+                nc.gpsimd.memset(window[:, first : first + 512], 0.0)
 
         def gather(pool_tile, b, dtype, name):
             picked = held.tile([P, N], dtype, name=name, align_bytes=64)
             nc.vector.tensor_copy(picked[:], pool_tile[:].indirect(offsets[:, b * LIST_COLS : (b + 1) * LIST_COLS]))
             return picked
 
-        def quantize(grouped, fmt, name):
-            codes = held.tile([P, 512], U32, name=name + "_codes", align_bytes=64)
+        def quantize(grouped, fmt, name, tag=None):
+            codes = held.tile([P, 512], U32, name=name + "_codes", tag=tag or name + "_codes", align_bytes=64)
             scales = held.tile([P, 512], U8, name=name + "_scales", align_bytes=64)
             nc.vector.quantize_mx(out=codes[:].bitcast(fmt), scales=scales[:], in_=grouped[:])
             return codes, scales, fmt
@@ -118,8 +118,7 @@ def tile_attend_gat_lse_kv_kernel(
             )
             return grouped
 
-        def product(banks, stationary, c, moving):
-            bank = banks.tile([P, 512], F32, name="bank")
+        def product(bank, stationary, c, moving):
             cols = slice(c * P, (c + 1) * P)
             nc.tensor.matmul_mx(
                 out=bank[:],
@@ -130,71 +129,91 @@ def tile_attend_gat_lse_kv_kernel(
                 start=True,
                 stop=True,
             )
-            return bank
 
-        p_planes, dv_staged = [], []
-        for b in range(B):
-            q_mx = quantize(cast_by_query(q_raw[b]), E4M3, f"q{b}")
-            k_s = gather(k_pool_scales, b, U8, f"k_s{b}")
-            k_w = gather(k_pool_words, b, U32, f"k_w{b}")
+        def gathered(pool_words, pool_scales, b, name):
+            scales = gather(pool_scales, b, U8, name + "_scales")
+            return gather(pool_words, b, U32, name + "_codes"), scales, E4M3
+
+        def weights(b, q_mx, k_mx):
             p = held.tile([P, PACK, N], F32, name=f"p{b}")
             for t in range(PACK):
-                bank = product(score_banks, q_mx, t, (k_w, k_s, E4M3))
-                nc.scalar.activation(p[:, t, :], bank[:], ACT.Exp, bias=neg_lse[:, b, t : t + 1])
-            p_planes.append(p)
-            pw = new_grouped()
-            if b == 0:
-                gate = rw_sb[:, b, :].unsqueeze(1).unsqueeze(3).broadcast_to([P, N // 4, PACK, 4])
-                nc.vector.tensor_tensor(interleaved(pw), by_fours(p), gate, ALU.mult)
-            else:
-                pw_planes = held.tile([P, PACK, N], F32, name="pw_planes")
-                for t in range(PACK):
-                    nc.scalar.activation(pw_planes[:, t, :], p[:, t, :], ACT.Copy, scale=rw_sb[:, b, t : t + 1])
-                nc.scalar.copy(interleaved(pw), by_fours(pw_planes))
-            dom_mx = quantize(cast_plain(dom_raw[b]), E5M2, f"dom{b}")
-            pw_mx = quantize(pw, E4M3, f"pw{b}")
-            staged = []
-            for c in range(DV // P):
-                bank = product(grad_banks, dom_mx, c, pw_mx)
-                st = held.tile([P, N], F32, name=f"dv{b}_{c}")
-                nc.scalar.copy(st[:], bank[:])
-                staged.append(st)
-            dv_staged.append(staged)
+                product(banks[t], q_mx, t, k_mx)
+                nc.scalar.activation(p[:, t, :], banks[t][:], ACT.Exp, bias=neg_lse[:, b, t : t + 1])
+            return p
 
-        do_raw = [load_rows(doT[b]) for b in range(B)]
-        qm_raw = [load_rows(qm[b]) for b in range(B)]
-        dk_staged = []
-        for b in range(B):
-            do_mx = quantize(cast_by_query(do_raw[b]), E5M2, f"do{b}")
-            v_s = gather(v_pool_scales, b, U8, f"v_s{b}")
-            v_w = gather(v_pool_words, b, U32, f"v_w{b}")
+        def gated_dp(b, do_mx, v_mx, dp_banks):
             g = held.tile([P, PACK, N], F32, name=f"g{b}")
-            for t in range(PACK):
-                bank = product(score_banks, do_mx, t, (v_w, v_s, E4M3))
-                col = b * PACK + t
+            for t, bank in enumerate(dp_banks):
+                product(bank, do_mx, t, v_mx)
                 nc.scalar.activation(
-                    g[:, t, :], bank[:], ACT.Identity, bias=neg_rw_delta[:, col : col + 1], scale=rw_sb[:, b, t : t + 1]
+                    g[:, t, :], bank[:], ACT.Identity, bias=neg_rw_delta[:, b, t : t + 1], scale=rw_sb[:, b, t : t + 1]
                 )
-            ds = new_grouped()
-            nc.vector.tensor_tensor(interleaved(ds), by_fours(p_planes[b]), by_fours(g), ALU.mult)
-            qm_mx = quantize(cast_plain(qm_raw[b]), E4M3, f"qm{b}")
-            ds_mx = quantize(ds, E5M2, f"ds{b}")
-            staged = []
-            for c in range(D // P):
-                bank = product(grad_banks, qm_mx, c, ds_mx)
-                st = held.tile([P, N], F32, name=f"dk{b}_{c}")
-                nc.scalar.copy(st[:], bank[:])
-                staged.append(st)
-            dk_staged.append(staged)
+            return g
 
-        windows = [held.tile([P, T], F32, name=f"window{c}") for c in range(DV // P)]
-        for window in windows:
-            nc.vector.memset(window[:].bitcast(I32), 0)
-        for staged, out in ((dv_staged, out_1), (dk_staged, out_0)):
+        def score_grad(p, g):
+            ds = new_grouped()
+            nc.vector.tensor_tensor(interleaved(ds), by_fours(p), by_fours(g), ALU.mult)
+            return ds
+
+        def gradient(bank, stationary, c, moving, staged):
+            product(bank, stationary, c, moving)
+            nc.scalar.copy(staged, bank[:])
+            return staged
+
+        def fresh_stage(name):
+            return held.tile([P, N], F32, name=name)[:]
+
+        k_picked_scales = [gather(k_pool_scales, b, U8, f"k{b}_scales") for b in range(B)]
+        q0_mx = quantize(cast_by_query(feature_rows), E4M3, "q0", tag="k_pool_scales")
+        load_rows(feature_rows, qT[1])
+        k0_mx = gather(k_pool_words, 0, U32, "k0_codes"), k_picked_scales[0], E4M3
+        p0 = weights(0, q0_mx, k0_mx)
+        pw0 = new_grouped()
+        gate = rw_sb[:, 0, :].unsqueeze(1).unsqueeze(3).broadcast_to([P, N // 4, PACK, 4])
+        nc.vector.tensor_tensor(interleaved(pw0), by_fours(p0), gate, ALU.mult)
+        dom0_mx = quantize(cast_plain(query_rows), E5M2, "dom0")
+        pw0_mx = quantize(pw0, E4M3, "pw0")
+        k1_mx = gather(k_pool_words, 1, U32, "k1_codes"), k_picked_scales[1], E4M3
+        v_pool_words = load_words(v_words)
+        load_rows(query_rows, dom[1])
+        q1_mx = quantize(cast_by_query(feature_rows), E4M3, "q1")
+        load_rows(feature_rows, doT[0])
+        dv0 = [gradient(banks[4 + c], dom0_mx, c, pw0_mx, fresh_stage(f"dv0_{c}")) for c in (0, 1, 2)]
+
+        p1 = weights(1, q1_mx, k1_mx)
+        pw1_planes = held.tile([P, PACK, N], F32, name="pw1_planes")
+        for t in range(PACK):
+            nc.scalar.activation(pw1_planes[:, t, :], p1[:, t, :], ACT.Copy, scale=rw_sb[:, 1, t : t + 1])
+        pw1 = cast_plain(pw1_planes)
+        dom1_mx = quantize(cast_plain(query_rows), E5M2, "dom1")
+        load_rows(query_rows, qm[0])
+        pw1_mx = quantize(pw1, E4M3, "pw1")
+        dv0.append(gradient(banks[7], dom0_mx, 3, pw0_mx, pw1_planes[:, 3, :]))
+
+        do0_mx = quantize(cast_by_query(feature_rows), E5M2, "do0")
+        load_rows(feature_rows, doT[1])
+        v0_mx = gathered(v_pool_words, v_pool_scales, 0, "v0")
+        v1_mx = gathered(v_pool_words, v_pool_scales, 1, "v1")
+        dv1 = [gradient(banks[4 + c], dom1_mx, c, pw1_mx, fresh_stage(f"dv1_{c}")) for c in (0, 1)]
+
+        g0 = gated_dp(0, do0_mx, v0_mx, banks[0:4])
+        ds0 = score_grad(p0, g0)
+        qm0_mx = quantize(cast_plain(query_rows), E4M3, "qm0")
+        load_rows(query_rows, qm[1])
+        ds0_mx = quantize(ds0, E5M2, "ds0")
+        do1_mx = quantize(cast_by_query(feature_rows), E5M2, "do1")
+        dv1 += [gradient(banks[c], dom1_mx, c, pw1_mx, feature_rows[:, c, :]) for c in (2, 3)]
+
+        g1 = gated_dp(1, do1_mx, v1_mx, [banks[n] for n in (0, 1, 6, 7)])
+        ds1 = score_grad(p1, g1)
+        qm1_mx = quantize(cast_plain(query_rows), E4M3, "qm1")
+        ds1_mx = quantize(ds1, E5M2, "ds1")
+        dk0 = [gradient(banks[n], qm0_mx, c, ds0_mx, g0[:, c, :]) for c, n in enumerate((4, 5, 2, 3))]
+        dk1 = [gradient(banks[n], qm1_mx, c, ds1_mx, g1[:, c, :]) for c, n in enumerate((0, 1, 6, 7))]
+
+        for staged, out in (((dv0, dv1), out_1), ((dk0, dk1), out_0)):
             for b in range(B):
-                for c in range(DV // P):
-                    nc.vector.tensor_copy(
-                        windows[c][:].indirect(offsets[:, b * LIST_COLS : (b + 1) * LIST_COLS]), staged[b][c][:]
-                    )
+                for c, window in enumerate(windows):
+                    nc.vector.tensor_copy(window[:].indirect(offsets[:, b * LIST_COLS : (b + 1) * LIST_COLS]), staged[b][c])
                     if b == B - 1:
-                        nc.sync.dma_start(out=out[c * P : (c + 1) * P, :], in_=windows[c][:])
+                        nc.sync.dma_start(out=out[c * P : (c + 1) * P, :], in_=window[:])

@@ -27,76 +27,95 @@ def tile_attend_gat_lse_kv_kernel(
     nc = tc.nc
     with ExitStack() as ctx:
         held = ctx.enter_context(tc.tile_pool(name="held", bufs=1))
-        groups = ctx.enter_context(tc.tile_pool(name="groups", bufs=6))
+        groups = ctx.enter_context(tc.tile_pool(name="groups", bufs=4))
         psum = ctx.enter_context(tc.psum_pool(name="psum", bufs=1))
         banks = [psum.tile([P, 512], F32, name=f"bank{n}") for n in range(8)]
 
         offsets = held.tile([P, B * LIST_COLS], U16, name="offsets")
         nc.sync.dma_start(offsets[:], offs)
 
-        def load_rows(raw, rows):
+        def load_rows(rows, name):
+            raw = held.tile([P, PACK, 512], F32, name=name)
             nc.sync.dma_start(out=raw[:], in_=rows.rearrange("(p j) w -> p j w", j=PACK))
+            return raw
 
-        def load_words(words):
-            pool_words = held.tile([P, T], U32, name="pool_words", tag="pool_words")
+        def load_words(words, name):
+            pool_words = held.tile([P, T], U32, name=name)
             nc.sync.dma_start(out=pool_words[:].bitcast(I32), in_=words[0].rearrange("p n t -> p (n t)").bitcast(I32))
             return pool_words
 
-        def load_scales(queue, scales, name):
-            pool_scales = held.tile([P, T], U8, name=name, tag=name, align_bytes=64)
-            nc.gpsimd.memset(pool_scales[:].bitcast(I32), 0)
+        def load_scales(clear, scales, name):
+            pool_scales = held.tile([P, T], U8, name=name, align_bytes=64)
+            clear.memset(pool_scales[:].bitcast(I32), 0)
             for quad in range(4):
-                queue.dma_start(
+                nc.sync.dma_start(
                     out=pool_scales[32 * quad : 32 * quad + 4, :].bitcast(I32),
                     in_=scales[0, 4 * quad : 4 * quad + 4, :].bitcast(I32),
                 )
             return pool_scales
 
-        def load_per_query(queue, vec, name):
+        def load_per_query(vec, name):
             col = held.tile([P, B, PACK], F32, name=name)
-            queue.dma_start(out=col[:], in_=vec.rearrange("b (p t) o -> p b (t o)", t=PACK))
+            nc.sync.dma_start(out=col[:], in_=vec.rearrange("b (p t) o -> p b (t o)", t=PACK))
             return col
 
-        k_pool_scales = load_scales(nc.sync, k_scales, "k_pool_scales")
-        warm = held.tile([P, 1], F32, name="warm", tag="pool_words")
-        nc.gpsimd.memset(warm[:], 0.0)
-        warm_out = held.tile([P, 1], F32, name="warm_out", tag="query_rows")
+        warm = held.tile([P, 1], F32, name="warm")
+        nc.vector.memset(warm[:], 0.0)
+        warm_out = held.tile([P, 1], F32, name="warm_out")
         nc.scalar.activation(warm_out[:], warm[:], ACT.Exp)
 
-        feature_rows = held.tile([P, PACK, 512], F32, name="feature_rows")
-        query_rows = held.tile([P, PACK, 512], F32, name="query_rows", tag="query_rows")
-        load_rows(feature_rows, qT[0])
-        k_pool_words = load_words(k_words)
-        load_rows(query_rows, dom[0])
-        lse_sb = load_per_query(nc.sync, lse, "lse_sb")
-        v_pool_scales = load_scales(nc.sync, v_scales, "v_pool_scales")
-        rw_sb = load_per_query(nc.gpsimd, rw, "rw_sb")
-        delta_sb = load_per_query(nc.gpsimd, delta, "delta_sb")
+        lse_sb = load_per_query(lse, "lse_sb")
+        rw_sb = load_per_query(rw, "rw_sb")
+        k_pool_scales = load_scales(nc.gpsimd, k_scales, "k_pool_scales")
+        q0_raw = load_rows(qT[0], "q0_raw")
+        v_pool_scales = load_scales(nc.gpsimd, v_scales, "v_pool_scales")
+        k_pool_words = load_words(k_words, "k_pool_words")
+        v_pool_words = load_words(v_words, "v_pool_words")
+        dom0_raw = load_rows(dom[0], "dom0_raw")
+        do0_raw = load_rows(doT[0], "do0_raw")
+        delta_sb = load_per_query(delta, "delta_sb")
+        qm0_raw = load_rows(qm[0], "qm0_raw")
+        q1_raw = load_rows(qT[1], "q1_raw")
+        dom1_raw = load_rows(dom[1], "dom1_raw")
+        do1_raw = load_rows(doT[1], "do1_raw")
+        qm1_raw = load_rows(qm[1], "qm1_raw")
 
         neg_lse = held.tile([P, B, PACK], F32, name="neg_lse")
-        nc.gpsimd.tensor_scalar_mul(neg_lse[:], lse_sb[:], -1.0)
-        neg_delta = held.tile([P, B, PACK], F32, name="neg_delta")
-        nc.gpsimd.tensor_scalar_mul(neg_delta[:], delta_sb[:], -1.0)
-        neg_rw_delta = held.tile([P, B, PACK], F32, name="neg_rw_delta")
-        nc.gpsimd.tensor_tensor(neg_rw_delta[:], neg_delta[:], rw_sb[:], ALU.mult)
+        nc.scalar.mul(neg_lse[:], lse_sb[:], -1.0)
 
-        windows = [held.tile([P, T], F32, name=f"window{c}") for c in range(DV // P)]
-        for window in windows:
+        dv_windows = [held.tile([P, T], F32, name=f"dv_window{c}") for c in range(DV // P)]
+        dk_windows = [held.tile([P, T], F32, name=f"dk_window{c}") for c in range(D // P)]
+        nc.vector.memset(dv_windows[0][:, :1023], 0.0)
+        nc.vector.memset(dv_windows[0][:, 1023:], 0.0)
+        for window in dv_windows[1:] + dk_windows:
             for first in range(0, T, 512):
                 nc.gpsimd.memset(window[:, first : first + 512], 0.0)
 
-        def gather(pool_tile, b, dtype, name):
-            picked = held.tile([P, N], dtype, name=name, align_bytes=64)
-            nc.vector.tensor_copy(picked[:], pool_tile[:].indirect(offsets[:, b * LIST_COLS : (b + 1) * LIST_COLS]))
+        def gather(pool_tile, b, dtype, name, tag=None, parts=1):
+            picked = held.tile([P, N], dtype, name=name, tag=tag or name, align_bytes=64)
+            for h in range(parts):
+                entries = slice((b * parts + h) * LIST_COLS // parts, (b * parts + h + 1) * LIST_COLS // parts)
+                nc.vector.tensor_copy(picked[:, h * N // parts : (h + 1) * N // parts], pool_tile[:].indirect(offsets[:, entries]))
             return picked
 
-        def quantize(grouped, fmt, name, tag=None):
+        def new_mx(name, fmt, tag=None):
             codes = held.tile([P, 512], U32, name=name + "_codes", tag=tag or name + "_codes", align_bytes=64)
             scales = held.tile([P, 512], U8, name=name + "_scales", align_bytes=64)
-            nc.vector.quantize_mx(out=codes[:].bitcast(fmt), scales=scales[:], in_=grouped[:])
             return codes, scales, fmt
 
-        def new_grouped():
+        def quantize_cols(mx, grouped, cols):
+            nc.vector.quantize_mx(
+                out=mx[0][:, cols].bitcast(mx[2]), scales=mx[1][:, cols], in_=grouped[:, PACK * cols.start : PACK * cols.stop]
+            )
+
+        def quantize(grouped, fmt, name, tag=None):
+            mx = new_mx(name, fmt, tag)
+            quantize_cols(mx, grouped, slice(0, 512))
+            return mx
+
+        def new_grouped(tag=None):
+            if tag:
+                return held.tile([P, 512 * PACK], BF16, name=tag, align_bytes=64)
             return groups.tile([P, 512 * PACK], BF16, name="grouped", align_bytes=64)
 
         def interleaved(grouped):
@@ -105,34 +124,37 @@ def tile_attend_gat_lse_kv_kernel(
         def by_fours(planes):
             return planes[:].rearrange("p t (c i) -> p c t i", i=4)
 
+        def cast_plain_cols(grouped, raw, cols):
+            fours = slice(cols.start // 4, cols.stop // 4)
+            nc.scalar.copy(interleaved(grouped)[:, fours], by_fours(raw)[:, fours])
+
         def cast_plain(raw):
             grouped = new_grouped()
-            nc.scalar.copy(interleaved(grouped), by_fours(raw))
+            cast_plain_cols(grouped, raw, slice(0, 512))
             return grouped
+
+        def cast_by_query_rows(grouped, raw, rows):
+            nc.scalar.copy(
+                grouped[:].rearrange("p (t m j) -> p m j t", t=PACK, j=PACK)[:, rows],
+                raw[:].rearrange("p j (m t) -> p m j t", t=PACK)[:, rows],
+            )
 
         def cast_by_query(raw):
             grouped = new_grouped()
-            nc.scalar.copy(
-                grouped[:].rearrange("p (t m j) -> p m j t", t=PACK, j=PACK),
-                raw[:].rearrange("p j (m t) -> p m j t", t=PACK),
-            )
+            cast_by_query_rows(grouped, raw, slice(0, P))
             return grouped
 
-        def product(bank, stationary, c, moving):
+        def product(bank, stationary, c, moving, slots=slice(0, N)):
             cols = slice(c * P, (c + 1) * P)
             nc.tensor.matmul_mx(
-                out=bank[:],
+                out=bank[:, slots],
                 lhsT=stationary[0][:, cols].bitcast(stationary[2]),
                 lhsT_scale=stationary[1][:, cols],
-                rhs=moving[0][:].bitcast(moving[2]),
-                rhs_scale=moving[1][:],
+                rhs=moving[0][:, slots].bitcast(moving[2]),
+                rhs_scale=moving[1][:, slots],
                 start=True,
                 stop=True,
             )
-
-        def gathered(pool_words, pool_scales, b, name):
-            scales = gather(pool_scales, b, U8, name + "_scales")
-            return gather(pool_words, b, U32, name + "_codes"), scales, E4M3
 
         def weights(b, q_mx, k_mx):
             p = held.tile([P, PACK, N], F32, name=f"p{b}")
@@ -141,8 +163,7 @@ def tile_attend_gat_lse_kv_kernel(
                 nc.scalar.activation(p[:, t, :], banks[t][:], ACT.Exp, bias=neg_lse[:, b, t : t + 1])
             return p
 
-        def gated_dp(b, do_mx, v_mx, dp_banks):
-            g = held.tile([P, PACK, N], F32, name=f"g{b}")
+        def gated_dp(b, do_mx, v_mx, dp_banks, g):
             for t, bank in enumerate(dp_banks):
                 product(bank, do_mx, t, v_mx)
                 nc.scalar.activation(
@@ -155,65 +176,73 @@ def tile_attend_gat_lse_kv_kernel(
             nc.vector.tensor_tensor(interleaved(ds), by_fours(p), by_fours(g), ALU.mult)
             return ds
 
-        def gradient(bank, stationary, c, moving, staged):
+        def place(out, windows, b, c, bank, stationary, moving, staged):
             product(bank, stationary, c, moving)
             nc.scalar.copy(staged, bank[:])
-            return staged
-
-        def fresh_stage(name):
-            return held.tile([P, N], F32, name=name)[:]
+            nc.vector.tensor_copy(windows[c][:].indirect(offsets[:, b * LIST_COLS : (b + 1) * LIST_COLS]), staged)
+            if b == B - 1:
+                nc.sync.dma_start(out=out[c * P : (c + 1) * P, :], in_=windows[c][:])
 
         k_picked_scales = [gather(k_pool_scales, b, U8, f"k{b}_scales") for b in range(B)]
-        q0_mx = quantize(cast_by_query(feature_rows), E4M3, "q0", tag="k_pool_scales")
-        load_rows(feature_rows, qT[1])
-        k0_mx = gather(k_pool_words, 0, U32, "k0_codes"), k_picked_scales[0], E4M3
-        p0 = weights(0, q0_mx, k0_mx)
-        pw0 = new_grouped()
-        gate = rw_sb[:, 0, :].unsqueeze(1).unsqueeze(3).broadcast_to([P, N // 4, PACK, 4])
-        nc.vector.tensor_tensor(interleaved(pw0), by_fours(p0), gate, ALU.mult)
-        dom0_mx = quantize(cast_plain(query_rows), E5M2, "dom0")
-        pw0_mx = quantize(pw0, E4M3, "pw0")
+        v_picked_scales = [gather(v_pool_scales, b, U8, f"v{b}_scales") for b in range(B)]
+        q0_mx = quantize(cast_by_query(q0_raw), E4M3, "q0", tag="v_pool_scales")
+        k0_mx = gather(k_pool_words, 0, U32, "k0_codes", parts=2), k_picked_scales[0], E4M3
         k1_mx = gather(k_pool_words, 1, U32, "k1_codes"), k_picked_scales[1], E4M3
-        v_pool_words = load_words(v_words)
-        load_rows(query_rows, dom[1])
-        q1_mx = quantize(cast_by_query(feature_rows), E4M3, "q1")
-        load_rows(feature_rows, doT[0])
-        dv0 = [gradient(banks[4 + c], dom0_mx, c, pw0_mx, fresh_stage(f"dv0_{c}")) for c in (0, 1, 2)]
+        v0_mx = gather(v_pool_words, 0, U32, "v0_codes"), v_picked_scales[0], E4M3
+        halves = (slice(0, 256), slice(256, 512))
+        p0 = held.tile([P, PACK, N], F32, name="p0")
+        pw0 = new_grouped("pw0_grouped")
+        gate = rw_sb[:, 0, :].unsqueeze(1).unsqueeze(3).broadcast_to([P, N // 8, PACK, 4])
+        for h, slots in enumerate(halves):
+            for t in range(PACK):
+                product(banks[4 * h + t], q0_mx, t, k0_mx, slots)
+                nc.scalar.activation(p0[:, t, slots], banks[4 * h + t][:, slots], ACT.Exp, bias=neg_lse[:, 0, t : t + 1])
+            fours = slice(slots.start // 4, slots.stop // 4)
+            nc.vector.tensor_tensor(interleaved(pw0)[:, fours], by_fours(p0)[:, fours], gate, ALU.mult)
+        dom0_low, dom0_high = new_grouped("dom0_low"), new_grouped()
+        dom0_mx = new_mx("dom0", E5M2)
+        cast_plain_cols(dom0_low, dom0_raw, halves[0])
+        quantize_cols(dom0_mx, dom0_low, halves[0])
+        pw0_mx = quantize(pw0, E4M3, "pw0", tag="dom0_low")
+        cast_plain_cols(dom0_high, dom0_raw, halves[1])
+        quantize_cols(dom0_mx, dom0_high, halves[1])
+        v1_mx = gather(v_pool_words, 1, U32, "v1_codes", tag="pw0_grouped"), v_picked_scales[1], E4M3
+        do0 = new_grouped()
+        cast_by_query_rows(do0, do0_raw, slice(0, 64))
+        place(out_1, dv_windows, 0, 0, banks[4], dom0_mx, pw0_mx, q0_raw[:, 0, :])
+        cast_by_query_rows(do0, do0_raw, slice(64, P))
+        do0_mx = quantize(do0, E5M2, "do0")
+        neg_rw_delta = held.tile([P, B, PACK], F32, name="neg_rw_delta")
+        nc.vector.scalar_tensor_tensor(neg_rw_delta[:], delta_sb[:], -1.0, rw_sb[:], ALU.mult, ALU.mult)
+        place(out_1, dv_windows, 0, 1, banks[5], dom0_mx, pw0_mx, q0_raw[:, 1, :])
+        g0 = gated_dp(0, do0_mx, v0_mx, banks[0:4], dom0_raw)
+        qm0_mx = quantize(cast_plain(qm0_raw), E4M3, "qm0")
+        place(out_1, dv_windows, 0, 2, banks[0], dom0_mx, pw0_mx, qm0_raw[:, 2, :])
+        ds0 = score_grad(p0, g0)
+        q1_mx = quantize(cast_by_query(q1_raw), E4M3, "q1")
+        ds0_mx = quantize(ds0, E5M2, "ds0")
+        place(out_1, dv_windows, 0, 3, banks[1], dom0_mx, pw0_mx, q1_raw[:, 3, :])
 
+        dom1_mx = quantize(cast_plain(dom1_raw), E5M2, "dom1")
+        place(out_0, dk_windows, 0, 0, banks[4], qm0_mx, ds0_mx, g0[:, 0, :])
         p1 = weights(1, q1_mx, k1_mx)
-        pw1_planes = held.tile([P, PACK, N], F32, name="pw1_planes")
+        place(out_0, dk_windows, 0, 1, banks[0], qm0_mx, ds0_mx, g0[:, 1, :])
+        pw1_planes = do0_raw
         for t in range(PACK):
             nc.scalar.activation(pw1_planes[:, t, :], p1[:, t, :], ACT.Copy, scale=rw_sb[:, 1, t : t + 1])
+        place(out_0, dk_windows, 0, 2, banks[1], qm0_mx, ds0_mx, g0[:, 2, :])
         pw1 = cast_plain(pw1_planes)
-        dom1_mx = quantize(cast_plain(query_rows), E5M2, "dom1")
-        load_rows(query_rows, qm[0])
         pw1_mx = quantize(pw1, E4M3, "pw1")
-        dv0.append(gradient(banks[7], dom0_mx, 3, pw0_mx, pw1_planes[:, 3, :]))
+        do1_mx = quantize(cast_by_query(do1_raw), E5M2, "do1")
+        place(out_0, dk_windows, 0, 3, banks[2], qm0_mx, ds0_mx, do1_raw[:, 3, :])
 
-        do0_mx = quantize(cast_by_query(feature_rows), E5M2, "do0")
-        load_rows(feature_rows, doT[1])
-        v0_mx = gathered(v_pool_words, v_pool_scales, 0, "v0")
-        v1_mx = gathered(v_pool_words, v_pool_scales, 1, "v1")
-        dv1 = [gradient(banks[4 + c], dom1_mx, c, pw1_mx, fresh_stage(f"dv1_{c}")) for c in (0, 1)]
-
-        g0 = gated_dp(0, do0_mx, v0_mx, banks[0:4])
-        ds0 = score_grad(p0, g0)
-        qm0_mx = quantize(cast_plain(query_rows), E4M3, "qm0")
-        load_rows(query_rows, qm[1])
-        ds0_mx = quantize(ds0, E5M2, "ds0")
-        do1_mx = quantize(cast_by_query(feature_rows), E5M2, "do1")
-        dv1 += [gradient(banks[c], dom1_mx, c, pw1_mx, feature_rows[:, c, :]) for c in (2, 3)]
-
-        g1 = gated_dp(1, do1_mx, v1_mx, [banks[n] for n in (0, 1, 6, 7)])
+        place(out_1, dv_windows, 1, 0, banks[2], dom1_mx, pw1_mx, dom1_raw[:, 0, :])
+        g1 = gated_dp(1, do1_mx, v1_mx, banks[4:8], q0_raw)
+        place(out_1, dv_windows, 1, 1, banks[4], dom1_mx, pw1_mx, dom1_raw[:, 1, :])
         ds1 = score_grad(p1, g1)
-        qm1_mx = quantize(cast_plain(query_rows), E4M3, "qm1")
+        qm1_mx = quantize(cast_plain(qm1_raw), E4M3, "qm1")
+        place(out_1, dv_windows, 1, 2, banks[1], dom1_mx, pw1_mx, g1[:, 2, :])
         ds1_mx = quantize(ds1, E5M2, "ds1")
-        dk0 = [gradient(banks[n], qm0_mx, c, ds0_mx, g0[:, c, :]) for c, n in enumerate((4, 5, 2, 3))]
-        dk1 = [gradient(banks[n], qm1_mx, c, ds1_mx, g1[:, c, :]) for c, n in enumerate((0, 1, 6, 7))]
-
-        for staged, out in (((dv0, dv1), out_1), ((dk0, dk1), out_0)):
-            for b in range(B):
-                for c, window in enumerate(windows):
-                    nc.vector.tensor_copy(window[:].indirect(offsets[:, b * LIST_COLS : (b + 1) * LIST_COLS]), staged[b][c])
-                    if b == B - 1:
-                        nc.sync.dma_start(out=out[c * P : (c + 1) * P, :], in_=window[:])
+        place(out_1, dv_windows, 1, 3, banks[2], dom1_mx, pw1_mx, qm1_raw[:, 3, :])
+        for c in range(4):
+            place(out_0, dk_windows, 1, c, banks[(3, 0, 5, 6)[c]], qm1_mx, ds1_mx, dom0_raw[:, c, :])

@@ -40,7 +40,7 @@ def tile_attend_gat_lse_kv_kernel(
             return raw
 
         def load_words(words, name):
-            pool_words = held.tile([P, T], U32, name=name)
+            pool_words = held.tile([P, T], U32, name=name, align_bytes=64)
             nc.sync.dma_start(out=pool_words[:].bitcast(I32), in_=words[0].rearrange("p n t -> p (n t)").bitcast(I32))
             return pool_words
 
@@ -65,31 +65,30 @@ def tile_attend_gat_lse_kv_kernel(
         nc.scalar.activation(warm_out[:], warm[:], ACT.Exp)
 
         lse_sb = load_per_query(lse, "lse_sb")
-        rw_sb = load_per_query(rw, "rw_sb")
-        k_pool_scales = load_scales(nc.gpsimd, k_scales, "k_pool_scales")
+        k_pool_scales = load_scales(nc.vector, k_scales, "k_pool_scales")
         q0_raw = load_rows(qT[0], "q0_raw")
-        v_pool_scales = load_scales(nc.gpsimd, v_scales, "v_pool_scales")
-        k_pool_words = load_words(k_words, "k_pool_words")
-        v_pool_words = load_words(v_words, "v_pool_words")
+        v_pool_scales = load_scales(nc.vector, v_scales, "v_pool_scales")
         dom0_raw = load_rows(dom[0], "dom0_raw")
-        do0_raw = load_rows(doT[0], "do0_raw")
-        delta_sb = load_per_query(delta, "delta_sb")
-        qm0_raw = load_rows(qm[0], "qm0_raw")
+        k_pool_words = load_words(k_words, "k_pool_words")
+        rw_sb = load_per_query(rw, "rw_sb")
         q1_raw = load_rows(qT[1], "q1_raw")
+        v_pool_words = load_words(v_words, "v_pool_words")
         dom1_raw = load_rows(dom[1], "dom1_raw")
+        delta_sb = load_per_query(delta, "delta_sb")
+        do0_raw = load_rows(doT[0], "do0_raw")
+        qm0_raw = load_rows(qm[0], "qm0_raw")
         do1_raw = load_rows(doT[1], "do1_raw")
         qm1_raw = load_rows(qm[1], "qm1_raw")
 
         neg_lse = held.tile([P, B, PACK], F32, name="neg_lse")
         nc.scalar.mul(neg_lse[:], lse_sb[:], -1.0)
 
-        dv_windows = [held.tile([P, T], F32, name=f"dv_window{c}") for c in range(DV // P)]
-        dk_windows = [held.tile([P, T], F32, name=f"dk_window{c}") for c in range(D // P)]
-        nc.vector.memset(dv_windows[0][:, :1023], 0.0)
-        nc.vector.memset(dv_windows[0][:, 1023:], 0.0)
-        for window in dv_windows[1:] + dk_windows:
-            for first in range(0, T, 512):
-                nc.gpsimd.memset(window[:, first : first + 512], 0.0)
+        def new_window(c, tag=None):
+            window = held.tile([P, T], F32, name=f"window{c}", tag=tag or f"window{c}", align_bytes=64)
+            nc.vector.memset(window[:].bitcast(I32), 0)
+            return window
+
+        windows = [new_window(c) for c in range(3)]
 
         def gather(pool_tile, b, dtype, name, tag=None, parts=1):
             picked = held.tile([P, N], dtype, name=name, tag=tag or name, align_bytes=64)
@@ -176,7 +175,7 @@ def tile_attend_gat_lse_kv_kernel(
             nc.vector.tensor_tensor(interleaved(ds), by_fours(p), by_fours(g), ALU.mult)
             return ds
 
-        def place(out, windows, b, c, bank, stationary, moving, staged):
+        def place(out, b, c, bank, stationary, moving, staged):
             product(bank, stationary, c, moving)
             nc.scalar.copy(staged, bank[:])
             nc.vector.tensor_copy(windows[c][:].indirect(offsets[:, b * LIST_COLS : (b + 1) * LIST_COLS]), staged)
@@ -184,14 +183,15 @@ def tile_attend_gat_lse_kv_kernel(
                 nc.sync.dma_start(out=out[c * P : (c + 1) * P, :], in_=windows[c][:])
 
         k_picked_scales = [gather(k_pool_scales, b, U8, f"k{b}_scales") for b in range(B)]
+        windows.append(new_window(3, tag="k_pool_scales"))
         v_picked_scales = [gather(v_pool_scales, b, U8, f"v{b}_scales") for b in range(B)]
         q0_mx = quantize(cast_by_query(q0_raw), E4M3, "q0", tag="v_pool_scales")
         k0_mx = gather(k_pool_words, 0, U32, "k0_codes", parts=2), k_picked_scales[0], E4M3
         k1_mx = gather(k_pool_words, 1, U32, "k1_codes"), k_picked_scales[1], E4M3
-        v0_mx = gather(v_pool_words, 0, U32, "v0_codes"), v_picked_scales[0], E4M3
+        dom0_mx = quantize(cast_plain(dom0_raw), E5M2, "dom0", tag="k_pool_words")
         halves = (slice(0, 256), slice(256, 512))
         p0 = held.tile([P, PACK, N], F32, name="p0")
-        pw0 = new_grouped("pw0_grouped")
+        pw0 = new_grouped()
         gate = rw_sb[:, 0, :].unsqueeze(1).unsqueeze(3).broadcast_to([P, N // 8, PACK, 4])
         for h, slots in enumerate(halves):
             for t in range(PACK):
@@ -199,50 +199,43 @@ def tile_attend_gat_lse_kv_kernel(
                 nc.scalar.activation(p0[:, t, slots], banks[4 * h + t][:, slots], ACT.Exp, bias=neg_lse[:, 0, t : t + 1])
             fours = slice(slots.start // 4, slots.stop // 4)
             nc.vector.tensor_tensor(interleaved(pw0)[:, fours], by_fours(p0)[:, fours], gate, ALU.mult)
-        dom0_low, dom0_high = new_grouped("dom0_low"), new_grouped()
-        dom0_mx = new_mx("dom0", E5M2)
-        cast_plain_cols(dom0_low, dom0_raw, halves[0])
-        quantize_cols(dom0_mx, dom0_low, halves[0])
-        pw0_mx = quantize(pw0, E4M3, "pw0", tag="dom0_low")
-        cast_plain_cols(dom0_high, dom0_raw, halves[1])
-        quantize_cols(dom0_mx, dom0_high, halves[1])
-        v1_mx = gather(v_pool_words, 1, U32, "v1_codes", tag="pw0_grouped"), v_picked_scales[1], E4M3
-        do0 = new_grouped()
-        cast_by_query_rows(do0, do0_raw, slice(0, 64))
-        place(out_1, dv_windows, 0, 0, banks[4], dom0_mx, pw0_mx, q0_raw[:, 0, :])
-        cast_by_query_rows(do0, do0_raw, slice(64, P))
-        do0_mx = quantize(do0, E5M2, "do0")
-        neg_rw_delta = held.tile([P, B, PACK], F32, name="neg_rw_delta")
-        nc.vector.scalar_tensor_tensor(neg_rw_delta[:], delta_sb[:], -1.0, rw_sb[:], ALU.mult, ALU.mult)
-        place(out_1, dv_windows, 0, 1, banks[5], dom0_mx, pw0_mx, q0_raw[:, 1, :])
-        g0 = gated_dp(0, do0_mx, v0_mx, banks[0:4], dom0_raw)
-        qm0_mx = quantize(cast_plain(qm0_raw), E4M3, "qm0")
-        place(out_1, dv_windows, 0, 2, banks[0], dom0_mx, pw0_mx, qm0_raw[:, 2, :])
-        ds0 = score_grad(p0, g0)
+        pw0_mx = quantize(pw0, E4M3, "pw0")
+        v0_mx = gather(v_pool_words, 0, U32, "v0_codes"), v_picked_scales[0], E4M3
         q1_mx = quantize(cast_by_query(q1_raw), E4M3, "q1")
-        ds0_mx = quantize(ds0, E5M2, "ds0")
-        place(out_1, dv_windows, 0, 3, banks[1], dom0_mx, pw0_mx, q1_raw[:, 3, :])
+        v1_mx = gather(v_pool_words, 1, U32, "v1_codes"), v_picked_scales[1], E4M3
+        for c in (0, 1):
+            place(out_1, 0, c, banks[4 + c], dom0_mx, pw0_mx, q0_raw[:, c, :])
 
-        dom1_mx = quantize(cast_plain(dom1_raw), E5M2, "dom1")
-        place(out_0, dk_windows, 0, 0, banks[4], qm0_mx, ds0_mx, g0[:, 0, :])
         p1 = weights(1, q1_mx, k1_mx)
-        place(out_0, dk_windows, 0, 1, banks[0], qm0_mx, ds0_mx, g0[:, 1, :])
-        pw1_planes = do0_raw
+        pw1_planes = q1_raw
         for t in range(PACK):
             nc.scalar.activation(pw1_planes[:, t, :], p1[:, t, :], ACT.Copy, scale=rw_sb[:, 1, t : t + 1])
-        place(out_0, dk_windows, 0, 2, banks[1], qm0_mx, ds0_mx, g0[:, 2, :])
+        place(out_1, 0, 2, banks[0], dom0_mx, pw0_mx, q0_raw[:, 2, :])
         pw1 = cast_plain(pw1_planes)
         pw1_mx = quantize(pw1, E4M3, "pw1")
-        do1_mx = quantize(cast_by_query(do1_raw), E5M2, "do1")
-        place(out_0, dk_windows, 0, 3, banks[2], qm0_mx, ds0_mx, do1_raw[:, 3, :])
+        dom1_mx = quantize(cast_plain(dom1_raw), E5M2, "dom1")
+        place(out_1, 0, 3, banks[1], dom0_mx, pw0_mx, q0_raw[:, 3, :])
+        do0_mx = quantize(cast_by_query(do0_raw), E5M2, "do0")
+        neg_rw_delta = held.tile([P, B, PACK], F32, name="neg_rw_delta")
+        nc.vector.scalar_tensor_tensor(neg_rw_delta[:], delta_sb[:], -1.0, rw_sb[:], ALU.mult, ALU.mult)
+        for c in (0, 1):
+            place(out_1, 1, c, banks[1], dom1_mx, pw1_mx, dom1_raw[:, c, :])
 
-        place(out_1, dv_windows, 1, 0, banks[2], dom1_mx, pw1_mx, dom1_raw[:, 0, :])
-        g1 = gated_dp(1, do1_mx, v1_mx, banks[4:8], q0_raw)
-        place(out_1, dv_windows, 1, 1, banks[4], dom1_mx, pw1_mx, dom1_raw[:, 1, :])
+        g0 = gated_dp(0, do0_mx, v0_mx, banks[4:8], dom0_raw)
+        qm0_mx = quantize(cast_plain(qm0_raw), E4M3, "qm0")
+        ds0 = score_grad(p0, g0)
+        place(out_1, 1, 2, banks[4], dom1_mx, pw1_mx, g0[:, 2, :])
+        ds0_mx = quantize(ds0, E5M2, "ds0")
+        do1_mx = quantize(cast_by_query(do1_raw), E5M2, "do1")
+        place(out_1, 1, 3, banks[5], dom1_mx, pw1_mx, do1_raw[:, 3, :])
+        place(out_0, 0, 0, banks[5], qm0_mx, ds0_mx, g0[:, 0, :])
+
+        g1 = gated_dp(1, do1_mx, v1_mx, banks[0:4], do0_raw)
+        place(out_0, 0, 1, banks[0], qm0_mx, ds0_mx, g0[:, 1, :])
         ds1 = score_grad(p1, g1)
         qm1_mx = quantize(cast_plain(qm1_raw), E4M3, "qm1")
-        place(out_1, dv_windows, 1, 2, banks[1], dom1_mx, pw1_mx, g1[:, 2, :])
+        place(out_0, 0, 2, banks[1], qm0_mx, ds0_mx, g1[:, 2, :])
         ds1_mx = quantize(ds1, E5M2, "ds1")
-        place(out_1, dv_windows, 1, 3, banks[2], dom1_mx, pw1_mx, qm1_raw[:, 3, :])
+        place(out_0, 0, 3, banks[2], qm0_mx, ds0_mx, qm1_raw[:, 3, :])
         for c in range(4):
-            place(out_0, dk_windows, 1, c, banks[(3, 0, 5, 6)[c]], qm1_mx, ds1_mx, dom0_raw[:, c, :])
+            place(out_0, 1, c, banks[4 + c], qm1_mx, ds1_mx, q0_raw[:, c, :])

@@ -35,7 +35,7 @@ def tile_attend_gat_lse_kv_kernel(
         nc.sync.dma_start(offsets[:], offs)
 
         def load_rows(rows, name):
-            raw = held.tile([P, PACK, 512], F32, name=name)
+            raw = held.tile([P, PACK, rows.shape[1]], F32, name=name)
             nc.sync.dma_start(out=raw[:], in_=rows.rearrange("(p j) w -> p j w", j=PACK))
             return raw
 
@@ -68,11 +68,12 @@ def tile_attend_gat_lse_kv_kernel(
         k_pool_scales = load_scales(nc.vector, k_scales, "k_pool_scales")
         q0_raw = load_rows(qT[0], "q0_raw")
         v_pool_scales = load_scales(nc.vector, v_scales, "v_pool_scales")
-        dom0_raw = load_rows(dom[0], "dom0_raw")
+        dom0_low_raw = load_rows(dom[0][:, :256], "dom0_low_raw")
         k_pool_words = load_words(k_words, "k_pool_words")
         rw_sb = load_per_query(rw, "rw_sb")
-        q1_raw = load_rows(qT[1], "q1_raw")
         v_pool_words = load_words(v_words, "v_pool_words")
+        dom0_high_raw = load_rows(dom[0][:, 256:], "dom0_high_raw")
+        q1_raw = load_rows(qT[1], "q1_raw")
         dom1_raw = load_rows(dom[1], "dom1_raw")
         delta_sb = load_per_query(delta, "delta_sb")
         do0_raw = load_rows(doT[0], "do0_raw")
@@ -83,9 +84,9 @@ def tile_attend_gat_lse_kv_kernel(
         neg_lse = held.tile([P, B, PACK], F32, name="neg_lse")
         nc.scalar.mul(neg_lse[:], lse_sb[:], -1.0)
 
-        def new_window(c, tag=None):
+        def new_window(c, clear=nc.vector, tag=None):
             window = held.tile([P, T], F32, name=f"window{c}", tag=tag or f"window{c}", align_bytes=64)
-            nc.vector.memset(window[:].bitcast(I32), 0)
+            clear.memset(window[:].bitcast(I32), 0)
             return window
 
         windows = [new_window(c) for c in range(3)]
@@ -106,6 +107,9 @@ def tile_attend_gat_lse_kv_kernel(
             nc.vector.quantize_mx(
                 out=mx[0][:, cols].bitcast(mx[2]), scales=mx[1][:, cols], in_=grouped[:, PACK * cols.start : PACK * cols.stop]
             )
+
+        def quantize_half(mx, grouped, cols):
+            nc.vector.quantize_mx(out=mx[0][:, cols].bitcast(mx[2]), scales=mx[1][:, cols], in_=grouped[:])
 
         def quantize(grouped, fmt, name, tag=None):
             mx = new_mx(name, fmt, tag)
@@ -183,15 +187,18 @@ def tile_attend_gat_lse_kv_kernel(
                 nc.sync.dma_start(out=out[c * P : (c + 1) * P, :], in_=windows[c][:])
 
         k_picked_scales = [gather(k_pool_scales, b, U8, f"k{b}_scales") for b in range(B)]
-        windows.append(new_window(3, tag="k_pool_scales"))
         v_picked_scales = [gather(v_pool_scales, b, U8, f"v{b}_scales") for b in range(B)]
         q0_mx = quantize(cast_by_query(q0_raw), E4M3, "q0", tag="v_pool_scales")
         k0_mx = gather(k_pool_words, 0, U32, "k0_codes", parts=2), k_picked_scales[0], E4M3
         k1_mx = gather(k_pool_words, 1, U32, "k1_codes"), k_picked_scales[1], E4M3
-        dom0_mx = quantize(cast_plain(dom0_raw), E5M2, "dom0", tag="k_pool_words")
         halves = (slice(0, 256), slice(256, 512))
+        dom0_mx = new_mx("dom0", E5M2, tag="k_pool_words")
+        dom0_low = held.tile([P, 256 * PACK], BF16, name="dom0_low", align_bytes=64)
+        nc.scalar.copy(interleaved(dom0_low), by_fours(dom0_low_raw))
+        quantize_half(dom0_mx, dom0_low, halves[0])
+        windows.append(new_window(3, clear=nc.gpsimd, tag="dom0_low"))
         p0 = held.tile([P, PACK, N], F32, name="p0")
-        pw0 = new_grouped()
+        pw0 = new_grouped("pw0_grouped")
         gate = rw_sb[:, 0, :].unsqueeze(1).unsqueeze(3).broadcast_to([P, N // 8, PACK, 4])
         for h, slots in enumerate(halves):
             for t in range(PACK):
@@ -199,21 +206,28 @@ def tile_attend_gat_lse_kv_kernel(
                 nc.scalar.activation(p0[:, t, slots], banks[4 * h + t][:, slots], ACT.Exp, bias=neg_lse[:, 0, t : t + 1])
             fours = slice(slots.start // 4, slots.stop // 4)
             nc.vector.tensor_tensor(interleaved(pw0)[:, fours], by_fours(p0)[:, fours], gate, ALU.mult)
-        pw0_mx = quantize(pw0, E4M3, "pw0")
-        v0_mx = gather(v_pool_words, 0, U32, "v0_codes"), v_picked_scales[0], E4M3
+        dom0_high = held.tile([P, 256 * PACK], BF16, name="dom0_high", align_bytes=64)
+        nc.scalar.copy(interleaved(dom0_high), by_fours(dom0_high_raw))
+        quantize_half(dom0_mx, dom0_high, halves[1])
+        pw0_mx = quantize(pw0, E4M3, "pw0", tag="dom0_high")
+        v_codes = held.tile([P, B * N], U32, name="v_codes", tag="pw0_grouped", align_bytes=64)
+        nc.vector.tensor_copy(v_codes[:], v_pool_words[:].indirect(offsets[:]))
+        v0_mx, v1_mx = [(v_codes[:, b * N : (b + 1) * N], v_picked_scales[b], E4M3) for b in range(B)]
         q1_mx = quantize(cast_by_query(q1_raw), E4M3, "q1")
-        v1_mx = gather(v_pool_words, 1, U32, "v1_codes"), v_picked_scales[1], E4M3
-        for c in (0, 1):
-            place(out_1, 0, c, banks[4 + c], dom0_mx, pw0_mx, q0_raw[:, c, :])
+        place(out_1, 0, 0, banks[4], dom0_mx, pw0_mx, q1_raw[:, 0, :])
+        place(out_1, 0, 1, banks[4], dom0_mx, pw0_mx, q0_raw[:, 1, :])
 
+        dom1 = new_grouped("dom1_grouped")
+        cast_plain_cols(dom1, dom1_raw, halves[0])
         p1 = weights(1, q1_mx, k1_mx)
-        pw1_planes = q1_raw
+        place(out_1, 0, 2, banks[0], dom0_mx, pw0_mx, q0_raw[:, 2, :])
+        pw1_planes = held.tile([P, PACK, N], F32, name="pw1_planes")
         for t in range(PACK):
             nc.scalar.activation(pw1_planes[:, t, :], p1[:, t, :], ACT.Copy, scale=rw_sb[:, 1, t : t + 1])
-        place(out_1, 0, 2, banks[0], dom0_mx, pw0_mx, q0_raw[:, 2, :])
+        cast_plain_cols(dom1, dom1_raw, halves[1])
         pw1 = cast_plain(pw1_planes)
+        dom1_mx = quantize(dom1, E5M2, "dom1")
         pw1_mx = quantize(pw1, E4M3, "pw1")
-        dom1_mx = quantize(cast_plain(dom1_raw), E5M2, "dom1")
         place(out_1, 0, 3, banks[1], dom0_mx, pw0_mx, q0_raw[:, 3, :])
         do0_mx = quantize(cast_by_query(do0_raw), E5M2, "do0")
         neg_rw_delta = held.tile([P, B, PACK], F32, name="neg_rw_delta")
@@ -221,7 +235,7 @@ def tile_attend_gat_lse_kv_kernel(
         for c in (0, 1):
             place(out_1, 1, c, banks[1], dom1_mx, pw1_mx, dom1_raw[:, c, :])
 
-        g0 = gated_dp(0, do0_mx, v0_mx, banks[4:8], dom0_raw)
+        g0 = gated_dp(0, do0_mx, v0_mx, banks[4:8], held.tile([P, PACK, N], F32, name="g0"))
         qm0_mx = quantize(cast_plain(qm0_raw), E4M3, "qm0")
         ds0 = score_grad(p0, g0)
         place(out_1, 1, 2, banks[4], dom1_mx, pw1_mx, g0[:, 2, :])

@@ -44,36 +44,35 @@ def tile_attend_gat_lse_kv_kernel(
             nc.sync.dma_start(out=pool_words[:].bitcast(I32), in_=words[0].rearrange("p n t -> p (n t)").bitcast(I32))
             return pool_words
 
-        def load_scales(clear, scales, name):
+        def new_scales(name):
             pool_scales = held.tile([P, T], U8, name=name, align_bytes=64)
-            clear.memset(pool_scales[:].bitcast(I32), 0)
-            for quad in range(4):
+            nc.vector.memset(pool_scales[:].bitcast(I32), 0)
+            return pool_scales
+
+        def load_scales(pool_scales, scales, quads):
+            for quad in quads:
                 nc.sync.dma_start(
                     out=pool_scales[32 * quad : 32 * quad + 4, :].bitcast(I32),
                     in_=scales[0, 4 * quad : 4 * quad + 4, :].bitcast(I32),
                 )
-            return pool_scales
 
         def load_per_query(vec, name):
             col = held.tile([P, B, PACK], F32, name=name)
             nc.sync.dma_start(out=col[:], in_=vec.rearrange("b (p t) o -> p b (t o)", t=PACK))
             return col
 
-        warm = held.tile([P, 1], F32, name="warm")
-        nc.vector.memset(warm[:], 0.0)
-        warm_out = held.tile([P, 1], F32, name="warm_out")
-        nc.scalar.activation(warm_out[:], warm[:], ACT.Exp)
-
         lse_sb = load_per_query(lse, "lse_sb")
-        k_pool_scales = load_scales(nc.vector, k_scales, "k_pool_scales")
+        k_pool_scales, v_pool_scales = new_scales("k_pool_scales"), new_scales("v_pool_scales")
+        load_scales(k_pool_scales, k_scales, range(4))
+        load_scales(v_pool_scales, v_scales, range(1))
         q0_raw = load_rows(qT[0], "q0_raw")
-        v_pool_scales = load_scales(nc.vector, v_scales, "v_pool_scales")
+        load_scales(v_pool_scales, v_scales, range(1, 4))
+        rw_sb = load_per_query(rw, "rw_sb")
         dom0_low_raw = load_rows(dom[0][:, :256], "dom0_low_raw")
         k_pool_words = load_words(k_words, "k_pool_words")
-        rw_sb = load_per_query(rw, "rw_sb")
+        q1_raw = load_rows(qT[1], "q1_raw")
         v_pool_words = load_words(v_words, "v_pool_words")
         dom0_high_raw = load_rows(dom[0][:, 256:], "dom0_high_raw")
-        q1_raw = load_rows(qT[1], "q1_raw")
         dom1_raw = load_rows(dom[1], "dom1_raw")
         delta_sb = load_per_query(delta, "delta_sb")
         do0_raw = load_rows(doT[0], "do0_raw")
@@ -89,7 +88,7 @@ def tile_attend_gat_lse_kv_kernel(
             clear.memset(window[:].bitcast(I32), 0)
             return window
 
-        windows = [new_window(c) for c in range(3)]
+        windows = [new_window(c) for c in range(4)]
 
         def gather(pool_tile, b, dtype, name, tag=None, parts=1):
             picked = held.tile([P, N], dtype, name=name, tag=tag or name, align_bytes=64)
@@ -97,6 +96,11 @@ def tile_attend_gat_lse_kv_kernel(
                 entries = slice((b * parts + h) * LIST_COLS // parts, (b * parts + h + 1) * LIST_COLS // parts)
                 nc.vector.tensor_copy(picked[:, h * N // parts : (h + 1) * N // parts], pool_tile[:].indirect(offsets[:, entries]))
             return picked
+
+        def gather_scales(pool_scales, name):
+            picked = held.tile([P, B * N], U8, name=name, align_bytes=64)
+            nc.vector.tensor_copy(picked[:], pool_scales[:].indirect(offsets[:]))
+            return [picked[:, b * N : (b + 1) * N] for b in range(B)]
 
         def new_mx(name, fmt, tag=None):
             codes = held.tile([P, 512], U32, name=name + "_codes", tag=tag or name + "_codes", align_bytes=64)
@@ -186,9 +190,9 @@ def tile_attend_gat_lse_kv_kernel(
             if b == B - 1:
                 nc.sync.dma_start(out=out[c * P : (c + 1) * P, :], in_=windows[c][:])
 
-        k_picked_scales = [gather(k_pool_scales, b, U8, f"k{b}_scales") for b in range(B)]
-        v_picked_scales = [gather(v_pool_scales, b, U8, f"v{b}_scales") for b in range(B)]
-        q0_mx = quantize(cast_by_query(q0_raw), E4M3, "q0", tag="v_pool_scales")
+        k_picked_scales = gather_scales(k_pool_scales, "k_scales")
+        v_picked_scales = gather_scales(v_pool_scales, "v_scales")
+        q0_mx = quantize(cast_by_query(q0_raw), E4M3, "q0")
         k0_mx = gather(k_pool_words, 0, U32, "k0_codes", parts=2), k_picked_scales[0], E4M3
         k1_mx = gather(k_pool_words, 1, U32, "k1_codes"), k_picked_scales[1], E4M3
         halves = (slice(0, 256), slice(256, 512))
@@ -196,9 +200,8 @@ def tile_attend_gat_lse_kv_kernel(
         dom0_low = held.tile([P, 256 * PACK], BF16, name="dom0_low", align_bytes=64)
         nc.scalar.copy(interleaved(dom0_low), by_fours(dom0_low_raw))
         quantize_half(dom0_mx, dom0_low, halves[0])
-        windows.append(new_window(3, clear=nc.gpsimd, tag="dom0_low"))
         p0 = held.tile([P, PACK, N], F32, name="p0")
-        pw0 = new_grouped("pw0_grouped")
+        pw0 = new_grouped()
         gate = rw_sb[:, 0, :].unsqueeze(1).unsqueeze(3).broadcast_to([P, N // 8, PACK, 4])
         for h, slots in enumerate(halves):
             for t in range(PACK):
@@ -206,34 +209,35 @@ def tile_attend_gat_lse_kv_kernel(
                 nc.scalar.activation(p0[:, t, slots], banks[4 * h + t][:, slots], ACT.Exp, bias=neg_lse[:, 0, t : t + 1])
             fours = slice(slots.start // 4, slots.stop // 4)
             nc.vector.tensor_tensor(interleaved(pw0)[:, fours], by_fours(p0)[:, fours], gate, ALU.mult)
+        pw0_mx = quantize(pw0, E4M3, "pw0")
+        v0_mx = gather(v_pool_words, 0, U32, "v0_codes"), v_picked_scales[0], E4M3
+        q1_mx = quantize(cast_by_query(q1_raw), E4M3, "q1")
+        place(out_1, 0, 0, banks[4], dom0_mx, pw0_mx, q0_raw[:, 0, :])
         dom0_high = held.tile([P, 256 * PACK], BF16, name="dom0_high", align_bytes=64)
         nc.scalar.copy(interleaved(dom0_high), by_fours(dom0_high_raw))
         quantize_half(dom0_mx, dom0_high, halves[1])
-        pw0_mx = quantize(pw0, E4M3, "pw0", tag="dom0_high")
-        v_codes = held.tile([P, B * N], U32, name="v_codes", tag="pw0_grouped", align_bytes=64)
-        nc.vector.tensor_copy(v_codes[:], v_pool_words[:].indirect(offsets[:]))
-        v0_mx, v1_mx = [(v_codes[:, b * N : (b + 1) * N], v_picked_scales[b], E4M3) for b in range(B)]
-        q1_mx = quantize(cast_by_query(q1_raw), E4M3, "q1")
-        place(out_1, 0, 0, banks[4], dom0_mx, pw0_mx, q1_raw[:, 0, :])
         place(out_1, 0, 1, banks[4], dom0_mx, pw0_mx, q0_raw[:, 1, :])
 
-        dom1 = new_grouped("dom1_grouped")
-        cast_plain_cols(dom1, dom1_raw, halves[0])
         p1 = weights(1, q1_mx, k1_mx)
         place(out_1, 0, 2, banks[0], dom0_mx, pw0_mx, q0_raw[:, 2, :])
         pw1_planes = held.tile([P, PACK, N], F32, name="pw1_planes")
         for t in range(PACK):
             nc.scalar.activation(pw1_planes[:, t, :], p1[:, t, :], ACT.Copy, scale=rw_sb[:, 1, t : t + 1])
-        cast_plain_cols(dom1, dom1_raw, halves[1])
-        pw1 = cast_plain(pw1_planes)
-        dom1_mx = quantize(dom1, E5M2, "dom1")
-        pw1_mx = quantize(pw1, E4M3, "pw1")
         place(out_1, 0, 3, banks[1], dom0_mx, pw0_mx, q0_raw[:, 3, :])
+        dom1, dom1_mx = new_grouped("dom1_grouped"), new_mx("dom1", E5M2)
+        cast_plain_cols(dom1, dom1_raw, halves[0])
+        quantize_cols(dom1_mx, dom1, halves[0])
+        pw1 = new_grouped("pw1_grouped")
+        cast_plain_cols(pw1, pw1_planes, slice(0, 512))
+        pw1_mx = quantize(pw1, E4M3, "pw1")
+        v1_mx = gather(v_pool_words, 1, U32, "v1_codes", tag="pw1_grouped"), v_picked_scales[1], E4M3
         do0_mx = quantize(cast_by_query(do0_raw), E5M2, "do0")
         neg_rw_delta = held.tile([P, B, PACK], F32, name="neg_rw_delta")
         nc.vector.scalar_tensor_tensor(neg_rw_delta[:], delta_sb[:], -1.0, rw_sb[:], ALU.mult, ALU.mult)
-        for c in (0, 1):
-            place(out_1, 1, c, banks[1], dom1_mx, pw1_mx, dom1_raw[:, c, :])
+        place(out_1, 1, 0, banks[1], dom1_mx, pw1_mx, q1_raw[:, 0, :])
+        cast_plain_cols(dom1, dom1_raw, halves[1])
+        quantize_cols(dom1_mx, dom1, halves[1])
+        place(out_1, 1, 1, banks[1], dom1_mx, pw1_mx, q1_raw[:, 1, :])
 
         g0 = gated_dp(0, do0_mx, v0_mx, banks[4:8], held.tile([P, PACK, N], F32, name="g0"))
         qm0_mx = quantize(cast_plain(qm0_raw), E4M3, "qm0")

@@ -179,9 +179,8 @@ def tile_attend_gat_lse_kv_kernel(
             return g
 
         def score_grad(p, g):
-            ds = new_grouped()
-            nc.vector.tensor_tensor(interleaved(ds), by_fours(p), by_fours(g), ALU.mult)
-            return ds
+            nc.vector.tensor_tensor(p[:], p[:], g[:], ALU.mult)
+            return p
 
         def place(out, b, c, bank, stationary, moving, staged):
             product(bank, stationary, c, moving)
@@ -240,20 +239,21 @@ def tile_attend_gat_lse_kv_kernel(
         place(out_1, 1, 1, banks[1], dom1_mx, pw1_mx, q1_raw[:, 1, :])
 
         g0 = gated_dp(0, do0_mx, v0_mx, banks[4:8], held.tile([P, PACK, N], F32, name="g0"))
-        qm0_mx = quantize(cast_plain(qm0_raw), E4M3, "qm0")
         ds0 = score_grad(p0, g0)
-        place(out_1, 1, 2, banks[4], dom1_mx, pw1_mx, g0[:, 2, :])
-        ds0_mx = quantize(ds0, E5M2, "ds0")
         do1_mx = quantize(cast_by_query(do1_raw), E5M2, "do1")
-        place(out_1, 1, 3, banks[5], dom1_mx, pw1_mx, do1_raw[:, 3, :])
-        place(out_0, 0, 0, banks[5], qm0_mx, ds0_mx, g0[:, 0, :])
+        qm0_mx = quantize(cast_plain(qm0_raw), E4M3, "qm0")
+        place(out_1, 1, 2, banks[0], dom1_mx, pw1_mx, g0[:, 2, :])
+        ds0_mx = quantize(cast_plain(ds0), E5M2, "ds0")
+        place(out_1, 1, 3, banks[0], dom1_mx, pw1_mx, ds0[:, 3, :])
 
-        g1 = gated_dp(1, do1_mx, v1_mx, banks[0:4], do0_raw)
-        place(out_0, 0, 1, banks[0], qm0_mx, ds0_mx, g0[:, 1, :])
-        ds1 = score_grad(p1, g1)
+        g1 = gated_dp(1, do1_mx, v1_mx, banks[4:8], do0_raw)
+        place(out_0, 0, 0, banks[7], qm0_mx, ds0_mx, g0[:, 0, :])
         qm1_mx = quantize(cast_plain(qm1_raw), E4M3, "qm1")
+        ds1 = score_grad(p1, g1)
+        place(out_0, 0, 1, banks[0], qm0_mx, ds0_mx, g1[:, 1, :])
+        ds1 = cast_plain(ds1)
         place(out_0, 0, 2, banks[1], qm0_mx, ds0_mx, g1[:, 2, :])
         ds1_mx = quantize(ds1, E5M2, "ds1")
-        place(out_0, 0, 3, banks[2], qm0_mx, ds0_mx, qm1_raw[:, 3, :])
+        place(out_0, 0, 3, banks[2], qm0_mx, ds0_mx, p1[:, 3, :])
         for c in range(4):
             place(out_0, 1, c, banks[4 + c], qm1_mx, ds1_mx, q0_raw[:, c, :])

@@ -88,7 +88,7 @@ def tile_attend_gat_lse_kv_kernel(
             clear.memset(window[:].bitcast(I32), 0)
             return window
 
-        windows = [new_window(c) for c in range(4)]
+        windows = [new_window(c) for c in range(3)]
 
         def gather(pool_tile, b, dtype, name, tag=None, parts=1):
             picked = held.tile([P, N], dtype, name=name, tag=tag or name, align_bytes=64)
@@ -199,6 +199,7 @@ def tile_attend_gat_lse_kv_kernel(
         dom0_low = held.tile([P, 256 * PACK], BF16, name="dom0_low", align_bytes=64)
         nc.scalar.copy(interleaved(dom0_low), by_fours(dom0_low_raw))
         quantize_half(dom0_mx, dom0_low, halves[0])
+        windows.append(new_window(3, clear=nc.gpsimd, tag="dom0_low"))
         p0 = held.tile([P, PACK, N], F32, name="p0")
         pw0 = new_grouped()
         gate = rw_sb[:, 0, :].unsqueeze(1).unsqueeze(3).broadcast_to([P, N // 8, PACK, 4])

@@ -49,12 +49,9 @@ def tile_attend_gat_lse_kv_kernel(
             nc.vector.memset(pool_scales[:].bitcast(I32), 0)
             return pool_scales
 
-        def load_scales(pool_scales, scales, quads):
-            for quad in quads:
-                nc.sync.dma_start(
-                    out=pool_scales[32 * quad : 32 * quad + 4, :].bitcast(I32),
-                    in_=scales[0, 4 * quad : 4 * quad + 4, :].bitcast(I32),
-                )
+        def load_scales(pool_scales, scales, rows):
+            for row in rows:
+                nc.sync.dma_start(out=pool_scales[row:P:32, :].bitcast(I32), in_=scales[0, row:16:4, :].bitcast(I32))
 
         def load_per_query(vec, name):
             col = held.tile([P, B, PACK], F32, name=name)

@@ -85,7 +85,9 @@ def tile_attend_gat_lse_kv_kernel(
             clear.memset(window[:].bitcast(I32), 0)
             return window
 
-        windows = [new_window(c) for c in range(3)]
+        windows = [new_window(c) for c in range(2)]
+        ones = held.tile([P, N], F32, name="ones")
+        nc.vector.memset(ones[:], 1.0)
 
         def gather(pool_tile, b, dtype, name, tag=None, parts=1):
             picked = held.tile([P, N], dtype, name=name, tag=tag or name, align_bytes=64)
@@ -143,8 +145,8 @@ def tile_attend_gat_lse_kv_kernel(
                 raw[:].rearrange("p j (m t) -> p m j t", t=PACK)[:, rows],
             )
 
-        def cast_by_query(raw):
-            grouped = new_grouped()
+        def cast_by_query(raw, tag=None):
+            grouped = new_grouped(tag)
             cast_by_query_rows(grouped, raw, slice(0, P))
             return grouped
 
@@ -179,10 +181,14 @@ def tile_attend_gat_lse_kv_kernel(
             nc.vector.tensor_tensor(p[:], p[:], g[:], ALU.mult)
             return p
 
-        def place(out, b, c, bank, stationary, moving, staged):
+        def place(out, b, c, bank, stationary, moving, staged, two_inputs=False):
             product(bank, stationary, c, moving)
             nc.scalar.copy(staged, bank[:])
-            nc.vector.tensor_copy(windows[c][:].indirect(offsets[:, b * LIST_COLS : (b + 1) * LIST_COLS]), staged)
+            listed = windows[c][:].indirect(offsets[:, b * LIST_COLS : (b + 1) * LIST_COLS])
+            if two_inputs:
+                nc.vector.tensor_tensor(listed, staged, ones[:], ALU.mult)
+            else:
+                nc.vector.tensor_copy(listed, staged)
             if b == B - 1:
                 nc.sync.dma_start(out=out[c * P : (c + 1) * P, :], in_=windows[c][:])
 
@@ -196,7 +202,6 @@ def tile_attend_gat_lse_kv_kernel(
         dom0_low = held.tile([P, 256 * PACK], BF16, name="dom0_low", align_bytes=64)
         nc.scalar.copy(interleaved(dom0_low), by_fours(dom0_low_raw))
         quantize_half(dom0_mx, dom0_low, halves[0])
-        windows.append(new_window(3, clear=nc.gpsimd, tag="dom0_low"))
         p0 = held.tile([P, PACK, N], F32, name="p0")
         pw0 = new_grouped()
         gate = rw_sb[:, 0, :].unsqueeze(1).unsqueeze(3).broadcast_to([P, N // 8, PACK, 4])
@@ -208,11 +213,13 @@ def tile_attend_gat_lse_kv_kernel(
             nc.vector.tensor_tensor(interleaved(pw0)[:, fours], by_fours(p0)[:, fours], gate, ALU.mult)
         pw0_mx = quantize(pw0, E4M3, "pw0")
         v0_mx = gather(v_pool_words, 0, U32, "v0_codes"), v_picked_scales[0], E4M3
-        q1_mx = quantize(cast_by_query(q1_raw), E4M3, "q1")
-        place(out_1, 0, 0, banks[4], dom0_mx, pw0_mx, q0_raw[:, 0, :])
+        q1_mx = quantize(cast_by_query(q1_raw, "q1_grouped"), E4M3, "q1")
+        windows.append(new_window(2, clear=nc.gpsimd, tag="q1_grouped"))
+        place(out_1, 0, 0, banks[4], dom0_mx, pw0_mx, q0_raw[:, 0, :], two_inputs=True)
         dom0_high = held.tile([P, 256 * PACK], BF16, name="dom0_high", align_bytes=64)
         nc.scalar.copy(interleaved(dom0_high), by_fours(dom0_high_raw))
         quantize_half(dom0_mx, dom0_high, halves[1])
+        windows.append(new_window(3, clear=nc.gpsimd, tag="dom0_high"))
         place(out_1, 0, 1, banks[4], dom0_mx, pw0_mx, q0_raw[:, 1, :])
 
         p1 = weights(1, q1_mx, k1_mx)

@@ -58,36 +58,36 @@ def tile_attend_gat_lse_kv_kernel(
             nc.sync.dma_start(out=col[:], in_=vec.rearrange("b (p t) o -> p b (t o)", t=PACK))
             return col
 
+        halves = (slice(0, 256), slice(256, 512))
         lse_sb = load_per_query(lse, "lse_sb")
+        rw_sb = load_per_query(rw, "rw_sb")
         k_pool_scales, v_pool_scales = new_scales("k_pool_scales"), new_scales("v_pool_scales")
         load_scales(k_pool_scales, k_scales, range(4))
-        load_scales(v_pool_scales, v_scales, range(1))
-        q0_raw = load_rows(qT[0], "q0_raw")
-        load_scales(v_pool_scales, v_scales, range(1, 4))
-        rw_sb = load_per_query(rw, "rw_sb")
-        dom0_low_raw = load_rows(dom[0][:, :256], "dom0_low_raw")
+        load_scales(v_pool_scales, v_scales, range(4))
+        q0_low_raw = load_rows(qT[0][:, halves[0]], "q0_low_raw")
+        q0_high_raw = load_rows(qT[0][:, halves[1]], "q0_high_raw")
         k_pool_words = load_words(k_words, "k_pool_words")
-        q1_raw = load_rows(qT[1], "q1_raw")
-        v_pool_words = load_words(v_words, "v_pool_words")
-        dom0_high_raw = load_rows(dom[0][:, 256:], "dom0_high_raw")
-        dom1_raw = load_rows(dom[1], "dom1_raw")
+        dom0_first_raw = load_rows(dom[0][:, :P], "dom0_first_raw")
+        dom0_rest_raw = load_rows(dom[0][:, P:], "dom0_rest_raw")
         delta_sb = load_per_query(delta, "delta_sb")
+        v_pool_words = load_words(v_words, "v_pool_words")
         do0_raw = load_rows(doT[0], "do0_raw")
         qm0_raw = load_rows(qm[0], "qm0_raw")
+        q1_raw = load_rows(qT[1], "q1_raw")
+        dom1_raw = load_rows(dom[1], "dom1_raw")
         do1_raw = load_rows(doT[1], "do1_raw")
         qm1_raw = load_rows(qm[1], "qm1_raw")
 
         neg_lse = held.tile([P, B, PACK], F32, name="neg_lse")
         nc.scalar.mul(neg_lse[:], lse_sb[:], -1.0)
 
-        def new_window(c, clear=nc.vector, tag=None):
-            window = held.tile([P, T], F32, name=f"window{c}", tag=tag or f"window{c}", align_bytes=64)
+        def new_window(name, clear=nc.vector, tag=None):
+            window = held.tile([P, T], F32, name=name, tag=tag or name, align_bytes=64)
             clear.memset(window[:].bitcast(I32), 0)
             return window
 
-        windows = [new_window(c) for c in range(2)]
-        ones = held.tile([P, N], F32, name="ones")
-        nc.vector.memset(ones[:], 1.0)
+        dv_windows = [new_window(f"dv_window{c}") for c in range(2)]
+        dk_windows = []
 
         def gather(pool_tile, b, dtype, name, tag=None, parts=1):
             picked = held.tile([P, N], dtype, name=name, tag=tag or name, align_bytes=64)
@@ -134,8 +134,8 @@ def tile_attend_gat_lse_kv_kernel(
             fours = slice(cols.start // 4, cols.stop // 4)
             nc.scalar.copy(interleaved(grouped)[:, fours], by_fours(raw)[:, fours])
 
-        def cast_plain(raw):
-            grouped = new_grouped()
+        def cast_plain(raw, tag=None):
+            grouped = new_grouped(tag)
             cast_plain_cols(grouped, raw, slice(0, 512))
             return grouped
 
@@ -163,7 +163,7 @@ def tile_attend_gat_lse_kv_kernel(
             )
 
         def weights(b, q_mx, k_mx):
-            p = held.tile([P, PACK, N], F32, name=f"p{b}")
+            p = held.tile([P, PACK, N], F32, name=f"p{b}", tag="v_pool_words", align_bytes=64)
             for t in range(PACK):
                 product(banks[t], q_mx, t, k_mx)
                 nc.scalar.activation(p[:, t, :], banks[t][:], ACT.Exp, bias=neg_lse[:, b, t : t + 1])
@@ -181,28 +181,30 @@ def tile_attend_gat_lse_kv_kernel(
             nc.vector.tensor_tensor(p[:], p[:], g[:], ALU.mult)
             return p
 
-        def place(out, b, c, bank, stationary, moving, staged, two_inputs=False):
+        def place(out, b, c, bank, stationary, moving, staged, window):
             product(bank, stationary, c, moving)
             nc.scalar.copy(staged, bank[:])
-            listed = windows[c][:].indirect(offsets[:, b * LIST_COLS : (b + 1) * LIST_COLS])
-            if two_inputs:
-                nc.vector.tensor_tensor(listed, staged, ones[:], ALU.mult)
-            else:
-                nc.vector.tensor_copy(listed, staged)
+            nc.vector.tensor_copy(window[:].indirect(offsets[:, b * LIST_COLS : (b + 1) * LIST_COLS]), staged)
             if b == B - 1:
-                nc.sync.dma_start(out=out[c * P : (c + 1) * P, :], in_=windows[c][:])
+                nc.sync.dma_start(out=out[c * P : (c + 1) * P, :], in_=window[:])
 
         k_picked_scales = gather_scales(k_pool_scales, "k_scales")
         v_picked_scales = gather_scales(v_pool_scales, "v_scales")
-        q0_mx = quantize(cast_by_query(q0_raw), E4M3, "q0")
+        q0 = new_grouped()
+        for h, raw in enumerate((q0_low_raw, q0_high_raw)):
+            nc.scalar.copy(
+                q0[:].rearrange("p (t m j) -> p m j t", t=PACK, j=PACK)[:, h * P // 2 : (h + 1) * P // 2],
+                raw[:].rearrange("p j (m t) -> p m j t", t=PACK),
+            )
+        q0_mx = quantize(q0, E4M3, "q0")
         k0_mx = gather(k_pool_words, 0, U32, "k0_codes", parts=2), k_picked_scales[0], E4M3
         k1_mx = gather(k_pool_words, 1, U32, "k1_codes"), k_picked_scales[1], E4M3
-        halves = (slice(0, 256), slice(256, 512))
-        dom0_mx = new_mx("dom0", E5M2, tag="k_pool_words")
-        dom0_low = held.tile([P, 256 * PACK], BF16, name="dom0_low", align_bytes=64)
-        nc.scalar.copy(interleaved(dom0_low), by_fours(dom0_low_raw))
-        quantize_half(dom0_mx, dom0_low, halves[0])
-        p0 = held.tile([P, PACK, N], F32, name="p0")
+        dom0_mx = new_mx("dom0", E5M2)
+        dom0_first = held.tile([P, P * PACK], BF16, name="dom0_first", align_bytes=64)
+        nc.scalar.copy(interleaved(dom0_first), by_fours(dom0_first_raw))
+        quantize_half(dom0_mx, dom0_first, slice(0, P))
+        dv_windows.append(new_window("dv_window2", clear=nc.gpsimd, tag="dom0_first"))
+        p0 = held.tile([P, PACK, N], F32, name="p0", align_bytes=64)
         pw0 = new_grouped()
         gate = rw_sb[:, 0, :].unsqueeze(1).unsqueeze(3).broadcast_to([P, N // 8, PACK, 4])
         for h, slots in enumerate(halves):
@@ -213,52 +215,50 @@ def tile_attend_gat_lse_kv_kernel(
             nc.vector.tensor_tensor(interleaved(pw0)[:, fours], by_fours(p0)[:, fours], gate, ALU.mult)
         pw0_mx = quantize(pw0, E4M3, "pw0")
         v0_mx = gather(v_pool_words, 0, U32, "v0_codes"), v_picked_scales[0], E4M3
-        q1_mx = quantize(cast_by_query(q1_raw, "q1_grouped"), E4M3, "q1")
-        windows.append(new_window(2, clear=nc.gpsimd, tag="q1_grouped"))
-        place(out_1, 0, 0, banks[4], dom0_mx, pw0_mx, q0_raw[:, 0, :], two_inputs=True)
-        dom0_high = held.tile([P, 256 * PACK], BF16, name="dom0_high", align_bytes=64)
-        nc.scalar.copy(interleaved(dom0_high), by_fours(dom0_high_raw))
-        quantize_half(dom0_mx, dom0_high, halves[1])
-        windows.append(new_window(3, clear=nc.gpsimd, tag="dom0_high"))
-        place(out_1, 0, 1, banks[4], dom0_mx, pw0_mx, q0_raw[:, 1, :])
-
-        p1 = weights(1, q1_mx, k1_mx)
-        place(out_1, 0, 2, banks[0], dom0_mx, pw0_mx, q0_raw[:, 2, :])
-        pw1_planes = held.tile([P, PACK, N], F32, name="pw1_planes")
-        for t in range(PACK):
-            nc.scalar.activation(pw1_planes[:, t, :], p1[:, t, :], ACT.Copy, scale=rw_sb[:, 1, t : t + 1])
-        place(out_1, 0, 3, banks[1], dom0_mx, pw0_mx, q0_raw[:, 3, :])
-        dom1, dom1_mx = new_grouped("dom1_grouped"), new_mx("dom1", E5M2)
-        cast_plain_cols(dom1, dom1_raw, halves[0])
-        quantize_cols(dom1_mx, dom1, halves[0])
-        pw1 = new_grouped("pw1_grouped")
-        cast_plain_cols(pw1, pw1_planes, slice(0, 512))
-        pw1_mx = quantize(pw1, E4M3, "pw1")
-        v1_mx = gather(v_pool_words, 1, U32, "v1_codes", tag="pw1_grouped"), v_picked_scales[1], E4M3
-        do0_mx = quantize(cast_by_query(do0_raw), E5M2, "do0")
+        v1_mx = gather(v_pool_words, 1, U32, "v1_codes"), v_picked_scales[1], E4M3
+        dom0_rest = held.tile([P, 3 * P * PACK], BF16, name="dom0_rest", align_bytes=64)
+        nc.scalar.copy(interleaved(dom0_rest), by_fours(dom0_rest_raw))
+        for cols in (slice(P, 2 * P), halves[1]):
+            nc.vector.quantize_mx(
+                out=dom0_mx[0][:, cols].bitcast(E5M2),
+                scales=dom0_mx[1][:, cols],
+                in_=dom0_rest[:, PACK * (cols.start - P) : PACK * (cols.stop - P)],
+            )
+        dv_windows.append(new_window("dv_window3", clear=nc.gpsimd, tag="dom0_rest"))
         neg_rw_delta = held.tile([P, B, PACK], F32, name="neg_rw_delta")
         nc.vector.scalar_tensor_tensor(neg_rw_delta[:], delta_sb[:], -1.0, rw_sb[:], ALU.mult, ALU.mult)
-        place(out_1, 1, 0, banks[1], dom1_mx, pw1_mx, q1_raw[:, 0, :])
-        cast_plain_cols(dom1, dom1_raw, halves[1])
-        quantize_cols(dom1_mx, dom1, halves[1])
-        place(out_1, 1, 1, banks[1], dom1_mx, pw1_mx, q1_raw[:, 1, :])
-
-        g0 = gated_dp(0, do0_mx, v0_mx, banks[4:8], held.tile([P, PACK, N], F32, name="g0"))
-        ds0 = score_grad(p0, g0)
-        do1_mx = quantize(cast_by_query(do1_raw), E5M2, "do1")
+        place(out_1, 0, 0, banks[0], dom0_mx, pw0_mx, dom0_rest_raw[:].rearrange("p j w -> p (j w)")[:, :N], dv_windows[0])
+        do0_mx = quantize(cast_by_query(do0_raw, "do0_grouped"), E5M2, "do0")
+        dk_windows.append(new_window("dk_window0", clear=nc.gpsimd, tag="do0_grouped"))
+        place(out_1, 0, 1, banks[1], dom0_mx, pw0_mx, do0_raw[:, 0, :], dv_windows[1])
         qm0_mx = quantize(cast_plain(qm0_raw), E4M3, "qm0")
-        place(out_1, 1, 2, banks[0], dom1_mx, pw1_mx, g0[:, 2, :])
-        ds0_mx = quantize(cast_plain(ds0), E5M2, "ds0")
-        place(out_1, 1, 3, banks[0], dom1_mx, pw1_mx, ds0[:, 3, :])
+        g0 = held.tile([P, PACK, N], F32, name="g0", tag="k_pool_words", align_bytes=64)
+        ds0 = score_grad(p0, gated_dp(0, do0_mx, v0_mx, banks[4:8], g0))
+        place(out_1, 0, 2, banks[6], dom0_mx, pw0_mx, do0_raw[:, 1, :], dv_windows[2])
+        q1_mx = quantize(cast_by_query(q1_raw, "q1_grouped"), E4M3, "q1")
+        dk_windows.append(new_window("dk_window1", clear=nc.gpsimd, tag="q1_grouped"))
+        ds0_mx = quantize(cast_plain(ds0, "ds0_grouped"), E5M2, "ds0")
+        dk_windows.append(new_window("dk_window2", clear=nc.gpsimd, tag="ds0_grouped"))
+        place(out_1, 0, 3, banks[7], dom0_mx, pw0_mx, ds0[:, 3, :], dv_windows[3])
+        dk_windows.append(new_window("dk_window3", clear=nc.gpsimd, tag="p0"))
 
-        g1 = gated_dp(1, do1_mx, v1_mx, banks[4:8], do0_raw)
-        place(out_0, 0, 0, banks[7], qm0_mx, ds0_mx, g0[:, 0, :])
+        place(out_0, 0, 0, banks[4], qm0_mx, ds0_mx, qm0_raw[:, 0, :], dk_windows[0])
+        p1 = weights(1, q1_mx, k1_mx)
+        place(out_0, 0, 1, banks[5], qm0_mx, ds0_mx, qm0_raw[:, 1, :], dk_windows[1])
+        pw1_planes = held.tile([P, PACK, N], F32, name="pw1_planes", tag="k_pool_words", align_bytes=64)
+        for t in range(PACK):
+            nc.scalar.activation(pw1_planes[:, t, :], p1[:, t, :], ACT.Copy, scale=rw_sb[:, 1, t : t + 1])
+        place(out_0, 0, 2, banks[6], qm0_mx, ds0_mx, qm0_raw[:, 2, :], dk_windows[2])
+        pw1_mx = quantize(cast_plain(pw1_planes), E4M3, "pw1")
+        dom1_mx = quantize(cast_plain(dom1_raw), E5M2, "dom1")
+        place(out_0, 0, 3, banks[7], qm0_mx, ds0_mx, dom1_raw[:, 3, :], dk_windows[3])
+        do1_mx = quantize(cast_by_query(do1_raw), E5M2, "do1")
+        place(out_1, 1, 0, banks[0], dom1_mx, pw1_mx, do1_raw[:, 0, :], dv_windows[0])
+        place(out_1, 1, 1, banks[1], dom1_mx, pw1_mx, do1_raw[:, 1, :], dv_windows[1])
         qm1_mx = quantize(cast_plain(qm1_raw), E4M3, "qm1")
-        ds1 = score_grad(p1, g1)
-        place(out_0, 0, 1, banks[0], qm0_mx, ds0_mx, g1[:, 1, :])
-        ds1 = cast_plain(ds1)
-        place(out_0, 0, 2, banks[1], qm0_mx, ds0_mx, g1[:, 2, :])
-        ds1_mx = quantize(ds1, E5M2, "ds1")
-        place(out_0, 0, 3, banks[2], qm0_mx, ds0_mx, p1[:, 3, :])
+        ds1 = score_grad(p1, gated_dp(1, do1_mx, v1_mx, banks[4:8], q1_raw))
+        place(out_1, 1, 2, banks[6], dom1_mx, pw1_mx, do1_raw[:, 2, :], dv_windows[2])
+        ds1_mx = quantize(cast_plain(ds1), E5M2, "ds1")
+        place(out_1, 1, 3, banks[7], dom1_mx, pw1_mx, ds1[:, 3, :], dv_windows[3])
         for c in range(4):
-            place(out_0, 1, c, banks[4 + c], qm1_mx, ds1_mx, q0_raw[:, c, :])
+            place(out_0, 1, c, banks[c], qm1_mx, ds1_mx, qm1_raw[:, c, :], dk_windows[c])

@@ -35,7 +35,7 @@ def tile_attend_gat_lse_kv_kernel(
         nc.sync.dma_start(offsets[:], offs)
 
         def load_rows(rows, name):
-            raw = held.tile([P, PACK, rows.shape[1]], F32, name=name)
+            raw = held.tile([P, PACK, rows.shape[1]], F32, name=name, align_bytes=64)
             nc.sync.dma_start(out=raw[:], in_=rows.rearrange("(p j) w -> p j w", j=PACK))
             return raw
 
@@ -61,6 +61,7 @@ def tile_attend_gat_lse_kv_kernel(
         halves = (slice(0, 256), slice(256, 512))
         lse_sb = load_per_query(lse, "lse_sb")
         rw_sb = load_per_query(rw, "rw_sb")
+        delta_sb = load_per_query(delta, "delta_sb")
         k_pool_scales, v_pool_scales = new_scales("k_pool_scales"), new_scales("v_pool_scales")
         load_scales(k_pool_scales, k_scales, range(4))
         load_scales(v_pool_scales, v_scales, range(4))
@@ -69,17 +70,18 @@ def tile_attend_gat_lse_kv_kernel(
         k_pool_words = load_words(k_words, "k_pool_words")
         dom0_first_raw = load_rows(dom[0][:, :P], "dom0_first_raw")
         dom0_rest_raw = load_rows(dom[0][:, P:], "dom0_rest_raw")
-        delta_sb = load_per_query(delta, "delta_sb")
         v_pool_words = load_words(v_words, "v_pool_words")
         do0_raw = load_rows(doT[0], "do0_raw")
         qm0_raw = load_rows(qm[0], "qm0_raw")
         q1_raw = load_rows(qT[1], "q1_raw")
         dom1_raw = load_rows(dom[1], "dom1_raw")
-        do1_raw = load_rows(doT[1], "do1_raw")
         qm1_raw = load_rows(qm[1], "qm1_raw")
+        do1_raw = load_rows(doT[1], "do1_raw")
 
         neg_lse = held.tile([P, B, PACK], F32, name="neg_lse")
         nc.scalar.mul(neg_lse[:], lse_sb[:], -1.0)
+        neg_delta = held.tile([P, B, PACK], F32, name="neg_delta")
+        nc.gpsimd.tensor_scalar(neg_delta[:], delta_sb[:], -1.0, 0.0, ALU.mult, ALU.add)
 
         def new_window(name, clear=nc.vector, tag=None):
             window = held.tile([P, T], F32, name=name, tag=tag or name, align_bytes=64)
@@ -169,17 +171,24 @@ def tile_attend_gat_lse_kv_kernel(
                 nc.scalar.activation(p[:, t, :], banks[t][:], ACT.Exp, bias=neg_lse[:, b, t : t + 1])
             return p
 
-        def gated_dp(b, do_mx, v_mx, dp_banks, g):
-            for t, bank in enumerate(dp_banks):
-                product(bank, do_mx, t, v_mx)
-                nc.scalar.activation(
-                    g[:, t, :], bank[:], ACT.Identity, bias=neg_rw_delta[:, b, t : t + 1], scale=rw_sb[:, b, t : t + 1]
-                )
-            return g
+        def gated_weights(b, p, tag):
+            pw = held.tile([P, PACK, N], F32, name=f"pw{b}_planes", tag=tag, align_bytes=64)
+            for t in range(PACK):
+                nc.scalar.activation(pw[:, t, :], p[:, t, :], ACT.Copy, scale=rw_sb[:, b, t : t + 1])
+            return pw
 
-        def score_grad(p, g):
-            nc.vector.tensor_tensor(p[:], p[:], g[:], ALU.mult)
-            return p
+        def score_grad(b, do_mx, v_mx, pw, ds):
+            last = PACK - 1
+            shifted = held.tile([P, N], F32, name=f"shifted{b}")
+            product(banks[4 + last], do_mx, last, v_mx)
+            nc.scalar.activation(shifted[:], banks[4 + last][:], ACT.Identity, bias=neg_delta[:, b, last : last + 1])
+            nc.gpsimd.tensor_tensor(ds[:, last, :], shifted[:], pw[:, last, :], ALU.mult)
+            for t in range(last):
+                product(banks[4 + t], do_mx, t, v_mx)
+                nc.vector.scalar_tensor_tensor(
+                    ds[:, t, :], banks[4 + t][:], delta_sb[:, b, t : t + 1], pw[:, t, :], ALU.subtract, ALU.mult
+                )
+            return ds
 
         def place(out, b, c, bank, stationary, moving, staged, window):
             product(bank, stationary, c, moving)
@@ -225,40 +234,35 @@ def tile_attend_gat_lse_kv_kernel(
                 in_=dom0_rest[:, PACK * (cols.start - P) : PACK * (cols.stop - P)],
             )
         dv_windows.append(new_window("dv_window3", clear=nc.gpsimd, tag="dom0_rest"))
-        neg_rw_delta = held.tile([P, B, PACK], F32, name="neg_rw_delta")
-        nc.vector.scalar_tensor_tensor(neg_rw_delta[:], delta_sb[:], -1.0, rw_sb[:], ALU.mult, ALU.mult)
         place(out_1, 0, 0, banks[0], dom0_mx, pw0_mx, dom0_rest_raw[:].rearrange("p j w -> p (j w)")[:, :N], dv_windows[0])
         do0_mx = quantize(cast_by_query(do0_raw, "do0_grouped"), E5M2, "do0")
         dk_windows.append(new_window("dk_window0", clear=nc.gpsimd, tag="do0_grouped"))
-        place(out_1, 0, 1, banks[1], dom0_mx, pw0_mx, do0_raw[:, 0, :], dv_windows[1])
+        place(out_1, 0, 1, banks[4], dom0_mx, pw0_mx, do0_raw[:, 3, :], dv_windows[1])
         qm0_mx = quantize(cast_plain(qm0_raw), E4M3, "qm0")
-        g0 = held.tile([P, PACK, N], F32, name="g0", tag="k_pool_words", align_bytes=64)
-        ds0 = score_grad(p0, gated_dp(0, do0_mx, v0_mx, banks[4:8], g0))
-        place(out_1, 0, 2, banks[6], dom0_mx, pw0_mx, do0_raw[:, 1, :], dv_windows[2])
+        ds0 = score_grad(0, do0_mx, v0_mx, gated_weights(0, p0, "k_pool_words"), do0_raw)
+        place(out_1, 0, 2, banks[7], dom0_mx, pw0_mx, q0_low_raw[:].rearrange("p j w -> p (j w)")[:, :N], dv_windows[2])
         q1_mx = quantize(cast_by_query(q1_raw, "q1_grouped"), E4M3, "q1")
         dk_windows.append(new_window("dk_window1", clear=nc.gpsimd, tag="q1_grouped"))
         ds0_mx = quantize(cast_plain(ds0, "ds0_grouped"), E5M2, "ds0")
         dk_windows.append(new_window("dk_window2", clear=nc.gpsimd, tag="ds0_grouped"))
-        place(out_1, 0, 3, banks[7], dom0_mx, pw0_mx, ds0[:, 3, :], dv_windows[3])
-        dk_windows.append(new_window("dk_window3", clear=nc.gpsimd, tag="p0"))
+        place(out_1, 0, 3, banks[1], dom0_mx, pw0_mx, ds0[:, 3, :], dv_windows[3])
+        dk_windows.append(new_window("dk_window3", clear=nc.gpsimd, tag="do0_raw"))
 
         place(out_0, 0, 0, banks[4], qm0_mx, ds0_mx, qm0_raw[:, 0, :], dk_windows[0])
         p1 = weights(1, q1_mx, k1_mx)
         place(out_0, 0, 1, banks[5], qm0_mx, ds0_mx, qm0_raw[:, 1, :], dk_windows[1])
-        pw1_planes = held.tile([P, PACK, N], F32, name="pw1_planes", tag="k_pool_words", align_bytes=64)
-        for t in range(PACK):
-            nc.scalar.activation(pw1_planes[:, t, :], p1[:, t, :], ACT.Copy, scale=rw_sb[:, 1, t : t + 1])
+        pw1_planes = gated_weights(1, p1, "p0")
         place(out_0, 0, 2, banks[6], qm0_mx, ds0_mx, qm0_raw[:, 2, :], dk_windows[2])
         pw1_mx = quantize(cast_plain(pw1_planes), E4M3, "pw1")
         dom1_mx = quantize(cast_plain(dom1_raw), E5M2, "dom1")
         place(out_0, 0, 3, banks[7], qm0_mx, ds0_mx, dom1_raw[:, 3, :], dk_windows[3])
-        do1_mx = quantize(cast_by_query(do1_raw), E5M2, "do1")
-        place(out_1, 1, 0, banks[0], dom1_mx, pw1_mx, do1_raw[:, 0, :], dv_windows[0])
-        place(out_1, 1, 1, banks[1], dom1_mx, pw1_mx, do1_raw[:, 1, :], dv_windows[1])
         qm1_mx = quantize(cast_plain(qm1_raw), E4M3, "qm1")
-        ds1 = score_grad(p1, gated_dp(1, do1_mx, v1_mx, banks[4:8], q1_raw))
-        place(out_1, 1, 2, banks[6], dom1_mx, pw1_mx, do1_raw[:, 2, :], dv_windows[2])
+        place(out_1, 1, 0, banks[0], dom1_mx, pw1_mx, q1_raw[:, 0, :], dv_windows[0])
+        do1_mx = quantize(cast_by_query(do1_raw), E5M2, "do1")
+        place(out_1, 1, 1, banks[4], dom1_mx, pw1_mx, do1_raw[:, 3, :], dv_windows[1])
+        ds1 = score_grad(1, do1_mx, v1_mx, pw1_planes, do1_raw)
+        place(out_1, 1, 2, banks[7], dom1_mx, pw1_mx, q1_raw[:, 2, :], dv_windows[2])
         ds1_mx = quantize(cast_plain(ds1), E5M2, "ds1")
-        place(out_1, 1, 3, banks[7], dom1_mx, pw1_mx, ds1[:, 3, :], dv_windows[3])
+        place(out_1, 1, 3, banks[1], dom1_mx, pw1_mx, ds1[:, 3, :], dv_windows[3])
         for c in range(4):
             place(out_0, 1, c, banks[c], qm1_mx, ds1_mx, qm1_raw[:, c, :], dk_windows[c])

@@ -59,18 +59,18 @@ def tile_attend_gat_lse_kv_kernel(
             return col
 
         halves = (slice(0, 256), slice(256, 512))
-        lse_sb = load_per_query(lse, "lse_sb")
-        rw_sb = load_per_query(rw, "rw_sb")
-        delta_sb = load_per_query(delta, "delta_sb")
         k_pool_scales, v_pool_scales = new_scales("k_pool_scales"), new_scales("v_pool_scales")
-        load_scales(k_pool_scales, k_scales, range(4))
-        load_scales(v_pool_scales, v_scales, range(4))
-        q0_low_raw = load_rows(qT[0][:, halves[0]], "q0_low_raw")
-        q0_high_raw = load_rows(qT[0][:, halves[1]], "q0_high_raw")
         k_pool_words = load_words(k_words, "k_pool_words")
+        load_scales(k_pool_scales, k_scales, range(4))
+        q0_parts = (slice(0, 192), slice(192, 384), slice(384, 512))
+        q0_raws = [load_rows(qT[0][:, cols], f"q0_raw{cols.start}") for cols in q0_parts]
+        lse_sb = load_per_query(lse, "lse_sb")
+        load_scales(v_pool_scales, v_scales, range(4))
+        rw_sb = load_per_query(rw, "rw_sb")
         dom0_first_raw = load_rows(dom[0][:, :P], "dom0_first_raw")
-        dom0_rest_raw = load_rows(dom[0][:, P:], "dom0_rest_raw")
         v_pool_words = load_words(v_words, "v_pool_words")
+        delta_sb = load_per_query(delta, "delta_sb")
+        dom0_rest_raw = load_rows(dom[0][:, P:], "dom0_rest_raw")
         do0_raw = load_rows(doT[0], "do0_raw")
         qm0_raw = load_rows(qm[0], "qm0_raw")
         q1_raw = load_rows(qT[1], "q1_raw")
@@ -78,10 +78,8 @@ def tile_attend_gat_lse_kv_kernel(
         qm1_raw = load_rows(qm[1], "qm1_raw")
         do1_raw = load_rows(doT[1], "do1_raw")
 
-        neg_lse = held.tile([P, B, PACK], F32, name="neg_lse")
-        nc.scalar.mul(neg_lse[:], lse_sb[:], -1.0)
-        neg_delta = held.tile([P, B, PACK], F32, name="neg_delta")
-        nc.gpsimd.tensor_scalar(neg_delta[:], delta_sb[:], -1.0, 0.0, ALU.mult, ALU.add)
+        minus_one = held.tile([P, 1], F32, name="minus_one")
+        nc.gpsimd.iota(minus_one[:], pattern=[[0, 1]], base=-1, channel_multiplier=0, allow_small_or_imprecise_dtypes=True)
 
         def new_window(name, clear=nc.vector, tag=None):
             window = held.tile([P, T], F32, name=name, tag=tag or name, align_bytes=64)
@@ -98,9 +96,9 @@ def tile_attend_gat_lse_kv_kernel(
                 nc.vector.tensor_copy(picked[:, h * N // parts : (h + 1) * N // parts], pool_tile[:].indirect(offsets[:, entries]))
             return picked
 
-        def gather_scales(pool_scales, name):
-            picked = held.tile([P, B * N], U8, name=name, align_bytes=64)
-            nc.vector.tensor_copy(picked[:], pool_scales[:].indirect(offsets[:]))
+        def gather_all(pool_tile, dtype, name):
+            picked = held.tile([P, B * N], dtype, name=name, align_bytes=64)
+            nc.vector.tensor_copy(picked[:], pool_tile[:].indirect(offsets[:]))
             return [picked[:, b * N : (b + 1) * N] for b in range(B)]
 
         def new_mx(name, fmt, tag=None):
@@ -171,10 +169,9 @@ def tile_attend_gat_lse_kv_kernel(
                 nc.scalar.activation(p[:, t, :], banks[t][:], ACT.Exp, bias=neg_lse[:, b, t : t + 1])
             return p
 
-        def gated_weights(b, p, tag):
-            pw = held.tile([P, PACK, N], F32, name=f"pw{b}_planes", tag=tag, align_bytes=64)
+        def gated_weights(b, p, pw):
             for t in range(PACK):
-                nc.scalar.activation(pw[:, t, :], p[:, t, :], ACT.Copy, scale=rw_sb[:, b, t : t + 1])
+                nc.scalar.activation(pw[t], p[:, t, :], ACT.Copy, scale=rw_sb[:, b, t : t + 1])
             return pw
 
         def score_grad(b, do_mx, v_mx, pw, ds):
@@ -182,11 +179,11 @@ def tile_attend_gat_lse_kv_kernel(
             shifted = held.tile([P, N], F32, name=f"shifted{b}")
             product(banks[4 + last], do_mx, last, v_mx)
             nc.scalar.activation(shifted[:], banks[4 + last][:], ACT.Identity, bias=neg_delta[:, b, last : last + 1])
-            nc.gpsimd.tensor_tensor(ds[:, last, :], shifted[:], pw[:, last, :], ALU.mult)
+            nc.gpsimd.tensor_tensor(ds[:, last, :], shifted[:], pw[last], ALU.mult)
             for t in range(last):
                 product(banks[4 + t], do_mx, t, v_mx)
                 nc.vector.scalar_tensor_tensor(
-                    ds[:, t, :], banks[4 + t][:], delta_sb[:, b, t : t + 1], pw[:, t, :], ALU.subtract, ALU.mult
+                    ds[:, t, :], banks[4 + t][:], delta_sb[:, b, t : t + 1], pw[t], ALU.subtract, ALU.mult
                 )
             return ds
 
@@ -197,22 +194,21 @@ def tile_attend_gat_lse_kv_kernel(
             if b == B - 1:
                 nc.sync.dma_start(out=out[c * P : (c + 1) * P, :], in_=window[:])
 
-        k_picked_scales = gather_scales(k_pool_scales, "k_scales")
-        v_picked_scales = gather_scales(v_pool_scales, "v_scales")
+        k_picked_words = gather_all(k_pool_words, U32, "k_codes")
+        k_picked_scales = gather_all(k_pool_scales, U8, "k_scales")
+        k0_mx, k1_mx = [(k_picked_words[b], k_picked_scales[b], E4M3) for b in range(B)]
         q0 = new_grouped()
-        for h, raw in enumerate((q0_low_raw, q0_high_raw)):
+        for cols, raw in zip(q0_parts, q0_raws):
             nc.scalar.copy(
-                q0[:].rearrange("p (t m j) -> p m j t", t=PACK, j=PACK)[:, h * P // 2 : (h + 1) * P // 2],
+                q0[:].rearrange("p (t m j) -> p m j t", t=PACK, j=PACK)[:, cols.start // PACK : cols.stop // PACK],
                 raw[:].rearrange("p j (m t) -> p m j t", t=PACK),
             )
         q0_mx = quantize(q0, E4M3, "q0")
-        k0_mx = gather(k_pool_words, 0, U32, "k0_codes", parts=2), k_picked_scales[0], E4M3
-        k1_mx = gather(k_pool_words, 1, U32, "k1_codes"), k_picked_scales[1], E4M3
-        dom0_mx = new_mx("dom0", E5M2)
-        dom0_first = held.tile([P, P * PACK], BF16, name="dom0_first", align_bytes=64)
-        nc.scalar.copy(interleaved(dom0_first), by_fours(dom0_first_raw))
-        quantize_half(dom0_mx, dom0_first, slice(0, P))
-        dv_windows.append(new_window("dv_window2", clear=nc.gpsimd, tag="dom0_first"))
+        neg_lse = held.tile([P, B, PACK], F32, name="neg_lse")
+        nc.scalar.mul(neg_lse[:], lse_sb[:], -1.0)
+        neg_delta = held.tile([P, B, PACK], F32, name="neg_delta")
+        nc.scalar.activation(neg_delta[:], delta_sb[:], ACT.Copy, scale=minus_one[:])
+        v_picked_scales = gather_all(v_pool_scales, U8, "v_scales")
         p0 = held.tile([P, PACK, N], F32, name="p0", align_bytes=64)
         pw0 = new_grouped()
         gate = rw_sb[:, 0, :].unsqueeze(1).unsqueeze(3).broadcast_to([P, N // 8, PACK, 4])
@@ -222,6 +218,10 @@ def tile_attend_gat_lse_kv_kernel(
                 nc.scalar.activation(p0[:, t, slots], banks[4 * h + t][:, slots], ACT.Exp, bias=neg_lse[:, 0, t : t + 1])
             fours = slice(slots.start // 4, slots.stop // 4)
             nc.vector.tensor_tensor(interleaved(pw0)[:, fours], by_fours(p0)[:, fours], gate, ALU.mult)
+        dom0_mx = new_mx("dom0", E5M2)
+        dom0_first = held.tile([P, P * PACK], BF16, name="dom0_first", align_bytes=64)
+        nc.scalar.copy(interleaved(dom0_first), by_fours(dom0_first_raw))
+        quantize_half(dom0_mx, dom0_first, slice(0, P))
         pw0_mx = quantize(pw0, E4M3, "pw0")
         v0_mx = gather(v_pool_words, 0, U32, "v0_codes"), v_picked_scales[0], E4M3
         v1_mx = gather(v_pool_words, 1, U32, "v1_codes"), v_picked_scales[1], E4M3
@@ -233,27 +233,33 @@ def tile_attend_gat_lse_kv_kernel(
                 scales=dom0_mx[1][:, cols],
                 in_=dom0_rest[:, PACK * (cols.start - P) : PACK * (cols.stop - P)],
             )
-        dv_windows.append(new_window("dv_window3", clear=nc.gpsimd, tag="dom0_rest"))
-        place(out_1, 0, 0, banks[0], dom0_mx, pw0_mx, dom0_rest_raw[:].rearrange("p j w -> p (j w)")[:, :N], dv_windows[0])
+        dv_windows.append(new_window("dv_window2", clear=nc.gpsimd, tag="dom0_rest"))
+        pw0_early = held.tile([P, 2, N], F32, name="pw0_early")
+        pw0_late = held.tile([P, 3, N], F32, name="pw0_late", tag="dom0_rest_raw", align_bytes=64)
+        pw0_planes = [pw0_early[:, 0, :], pw0_early[:, 1, :], pw0_late[:, 0, :], pw0_late[:, 1, :]]
+        place(out_1, 0, 0, banks[0], dom0_mx, pw0_mx, pw0_late[:, 2, :], dv_windows[0])
         do0_mx = quantize(cast_by_query(do0_raw, "do0_grouped"), E5M2, "do0")
-        dk_windows.append(new_window("dk_window0", clear=nc.gpsimd, tag="do0_grouped"))
+        dv_windows.append(new_window("dv_window3", clear=nc.gpsimd, tag="do0_grouped"))
         place(out_1, 0, 1, banks[4], dom0_mx, pw0_mx, do0_raw[:, 3, :], dv_windows[1])
-        qm0_mx = quantize(cast_plain(qm0_raw), E4M3, "qm0")
-        ds0 = score_grad(0, do0_mx, v0_mx, gated_weights(0, p0, "k_pool_words"), do0_raw)
-        place(out_1, 0, 2, banks[7], dom0_mx, pw0_mx, q0_low_raw[:].rearrange("p j w -> p (j w)")[:, :N], dv_windows[2])
+        qm0 = cast_plain(qm0_raw)
+        ds0 = score_grad(0, do0_mx, v0_mx, gated_weights(0, p0, pw0_planes), do0_raw)
+        qm0_mx = quantize(qm0, E4M3, "qm0")
+        place(out_1, 0, 2, banks[7], dom0_mx, pw0_mx, q0_raws[0][:].rearrange("p j w -> p (j w)")[:, :N], dv_windows[2])
         q1_mx = quantize(cast_by_query(q1_raw, "q1_grouped"), E4M3, "q1")
-        dk_windows.append(new_window("dk_window1", clear=nc.gpsimd, tag="q1_grouped"))
+        dk_windows.append(new_window("dk_window0", clear=nc.gpsimd, tag="q1_grouped"))
         ds0_mx = quantize(cast_plain(ds0, "ds0_grouped"), E5M2, "ds0")
-        dk_windows.append(new_window("dk_window2", clear=nc.gpsimd, tag="ds0_grouped"))
+        dk_windows.append(new_window("dk_window1", clear=nc.gpsimd, tag="ds0_grouped"))
         place(out_1, 0, 3, banks[1], dom0_mx, pw0_mx, ds0[:, 3, :], dv_windows[3])
-        dk_windows.append(new_window("dk_window3", clear=nc.gpsimd, tag="do0_raw"))
+        dk_windows.append(new_window("dk_window2", clear=nc.gpsimd, tag="do0_raw"))
 
-        place(out_0, 0, 0, banks[4], qm0_mx, ds0_mx, qm0_raw[:, 0, :], dk_windows[0])
+        place(out_0, 0, 0, banks[4], qm0_mx, ds0_mx, q0_raws[1][:].rearrange("p j w -> p (j w)")[:, :N], dk_windows[0])
+        dk_windows.append(new_window("dk_window3", clear=nc.gpsimd, tag="q0_raw192"))
         p1 = weights(1, q1_mx, k1_mx)
         place(out_0, 0, 1, banks[5], qm0_mx, ds0_mx, qm0_raw[:, 1, :], dk_windows[1])
-        pw1_planes = gated_weights(1, p1, "p0")
+        pw1_tile = held.tile([P, PACK, N], F32, name="pw1_tile", tag="p0", align_bytes=64)
+        pw1_planes = gated_weights(1, p1, [pw1_tile[:, t, :] for t in range(PACK)])
         place(out_0, 0, 2, banks[6], qm0_mx, ds0_mx, qm0_raw[:, 2, :], dk_windows[2])
-        pw1_mx = quantize(cast_plain(pw1_planes), E4M3, "pw1")
+        pw1_mx = quantize(cast_plain(pw1_tile), E4M3, "pw1")
         dom1_mx = quantize(cast_plain(dom1_raw), E5M2, "dom1")
         place(out_0, 0, 3, banks[7], qm0_mx, ds0_mx, dom1_raw[:, 3, :], dk_windows[3])
         qm1_mx = quantize(cast_plain(qm1_raw), E4M3, "qm1")

@@ -59,25 +59,25 @@ def tile_attend_gat_lse_kv_kernel(
             return col
 
         halves = (slice(0, 256), slice(256, 512))
-        k_pool_scales, v_pool_scales = new_scales("k_pool_scales"), new_scales("v_pool_scales")
-        k_pool_words = load_words(k_words, "k_pool_words")
-        load_scales(k_pool_scales, k_scales, range(4))
-        q0_parts = (slice(0, 192), slice(192, 384), slice(384, 512))
-        q0_raws = [load_rows(qT[0][:, cols], f"q0_raw{cols.start}") for cols in q0_parts]
         lse_sb = load_per_query(lse, "lse_sb")
-        load_scales(v_pool_scales, v_scales, range(4))
         rw_sb = load_per_query(rw, "rw_sb")
-        dom0_first_raw = load_rows(dom[0][:, :P], "dom0_first_raw")
+        k_pool_scales, v_pool_scales = new_scales("k_pool_scales"), new_scales("v_pool_scales")
+        load_scales(k_pool_scales, k_scales, range(4))
+        load_scales(v_pool_scales, v_scales, range(4))
+        q0_raw = load_rows(qT[0], "q0_raw")
+        k_pool_words = load_words(k_words, "k_pool_words")
+        dom0_raw = load_rows(dom[0], "dom0_raw")
         v_pool_words = load_words(v_words, "v_pool_words")
         delta_sb = load_per_query(delta, "delta_sb")
-        dom0_rest_raw = load_rows(dom[0][:, P:], "dom0_rest_raw")
         do0_raw = load_rows(doT[0], "do0_raw")
         qm0_raw = load_rows(qm[0], "qm0_raw")
         q1_raw = load_rows(qT[1], "q1_raw")
         dom1_raw = load_rows(dom[1], "dom1_raw")
-        qm1_raw = load_rows(qm[1], "qm1_raw")
         do1_raw = load_rows(doT[1], "do1_raw")
+        qm1_raw = load_rows(qm[1], "qm1_raw")
 
+        neg_lse = held.tile([P, B, PACK], F32, name="neg_lse")
+        nc.scalar.mul(neg_lse[:], lse_sb[:], -1.0)
         minus_one = held.tile([P, 1], F32, name="minus_one")
         nc.gpsimd.iota(minus_one[:], pattern=[[0, 1]], base=-1, channel_multiplier=0, allow_small_or_imprecise_dtypes=True)
 
@@ -121,7 +121,7 @@ def tile_attend_gat_lse_kv_kernel(
 
         def new_grouped(tag=None):
             if tag:
-                return held.tile([P, 512 * PACK], BF16, name=tag, align_bytes=64)
+                return held.tile([P, 512 * PACK], BF16, name="grouped_on_" + tag, tag=tag, align_bytes=64)
             return groups.tile([P, 512 * PACK], BF16, name="grouped", align_bytes=64)
 
         def interleaved(grouped):
@@ -174,11 +174,15 @@ def tile_attend_gat_lse_kv_kernel(
                 nc.scalar.activation(pw[t], p[:, t, :], ACT.Copy, scale=rw_sb[:, b, t : t + 1])
             return pw
 
-        def score_grad(b, do_mx, v_mx, pw, ds):
-            last = PACK - 1
-            shifted = held.tile([P, N], F32, name=f"shifted{b}")
+        last = PACK - 1
+
+        def shifted_last(b, do_mx, v_mx):
+            shifted = held.tile([P, N], F32, name=f"shifted{b}", align_bytes=64)
             product(banks[4 + last], do_mx, last, v_mx)
             nc.scalar.activation(shifted[:], banks[4 + last][:], ACT.Identity, bias=neg_delta[:, b, last : last + 1])
+            return shifted
+
+        def score_grad(b, do_mx, v_mx, shifted, pw, ds):
             nc.gpsimd.tensor_tensor(ds[:, last, :], shifted[:], pw[last], ALU.mult)
             for t in range(last):
                 product(banks[4 + t], do_mx, t, v_mx)
@@ -194,21 +198,16 @@ def tile_attend_gat_lse_kv_kernel(
             if b == B - 1:
                 nc.sync.dma_start(out=out[c * P : (c + 1) * P, :], in_=window[:])
 
-        k_picked_words = gather_all(k_pool_words, U32, "k_codes")
         k_picked_scales = gather_all(k_pool_scales, U8, "k_scales")
-        k0_mx, k1_mx = [(k_picked_words[b], k_picked_scales[b], E4M3) for b in range(B)]
-        q0 = new_grouped()
-        for cols, raw in zip(q0_parts, q0_raws):
-            nc.scalar.copy(
-                q0[:].rearrange("p (t m j) -> p m j t", t=PACK, j=PACK)[:, cols.start // PACK : cols.stop // PACK],
-                raw[:].rearrange("p j (m t) -> p m j t", t=PACK),
-            )
-        q0_mx = quantize(q0, E4M3, "q0")
-        neg_lse = held.tile([P, B, PACK], F32, name="neg_lse")
-        nc.scalar.mul(neg_lse[:], lse_sb[:], -1.0)
-        neg_delta = held.tile([P, B, PACK], F32, name="neg_delta")
-        nc.scalar.activation(neg_delta[:], delta_sb[:], ACT.Copy, scale=minus_one[:])
         v_picked_scales = gather_all(v_pool_scales, U8, "v_scales")
+        q0 = new_grouped()
+        q0_dealt = q0[:].rearrange("p (t m j) -> p m j t", t=PACK, j=PACK)
+        q0_rows = q0_raw[:].rearrange("p j (m t) -> p m j t", t=PACK)
+        nc.scalar.copy(q0_dealt[:, :, :, :2], q0_rows[:, :, :, :2])
+        nc.vector.tensor_copy(q0_dealt[:, :, :, 2:], q0_rows[:, :, :, 2:])
+        q0_mx = quantize(q0, E4M3, "q0")
+        k0_mx = gather(k_pool_words, 0, U32, "k0_codes", parts=2), k_picked_scales[0], E4M3
+        k1_mx = gather(k_pool_words, 1, U32, "k1_codes"), k_picked_scales[1], E4M3
         p0 = held.tile([P, PACK, N], F32, name="p0", align_bytes=64)
         pw0 = new_grouped()
         gate = rw_sb[:, 0, :].unsqueeze(1).unsqueeze(3).broadcast_to([P, N // 8, PACK, 4])
@@ -220,13 +219,13 @@ def tile_attend_gat_lse_kv_kernel(
             nc.vector.tensor_tensor(interleaved(pw0)[:, fours], by_fours(p0)[:, fours], gate, ALU.mult)
         dom0_mx = new_mx("dom0", E5M2)
         dom0_first = held.tile([P, P * PACK], BF16, name="dom0_first", align_bytes=64)
-        nc.scalar.copy(interleaved(dom0_first), by_fours(dom0_first_raw))
+        nc.scalar.copy(interleaved(dom0_first), by_fours(dom0_raw)[:, : P // 4])
         quantize_half(dom0_mx, dom0_first, slice(0, P))
         pw0_mx = quantize(pw0, E4M3, "pw0")
         v0_mx = gather(v_pool_words, 0, U32, "v0_codes"), v_picked_scales[0], E4M3
         v1_mx = gather(v_pool_words, 1, U32, "v1_codes"), v_picked_scales[1], E4M3
         dom0_rest = held.tile([P, 3 * P * PACK], BF16, name="dom0_rest", align_bytes=64)
-        nc.scalar.copy(interleaved(dom0_rest), by_fours(dom0_rest_raw))
+        nc.scalar.copy(interleaved(dom0_rest), by_fours(dom0_raw)[:, P // 4 :])
         for cols in (slice(P, 2 * P), halves[1]):
             nc.vector.quantize_mx(
                 out=dom0_mx[0][:, cols].bitcast(E5M2),
@@ -234,39 +233,42 @@ def tile_attend_gat_lse_kv_kernel(
                 in_=dom0_rest[:, PACK * (cols.start - P) : PACK * (cols.stop - P)],
             )
         dv_windows.append(new_window("dv_window2", clear=nc.gpsimd, tag="dom0_rest"))
-        pw0_early = held.tile([P, 2, N], F32, name="pw0_early")
-        pw0_late = held.tile([P, 3, N], F32, name="pw0_late", tag="dom0_rest_raw", align_bytes=64)
-        pw0_planes = [pw0_early[:, 0, :], pw0_early[:, 1, :], pw0_late[:, 0, :], pw0_late[:, 1, :]]
-        place(out_1, 0, 0, banks[0], dom0_mx, pw0_mx, pw0_late[:, 2, :], dv_windows[0])
+        after_dom0 = held.tile([P, 3, N], F32, name="after_dom0", tag="dom0_raw", align_bytes=64)
+        pw0_planes = [do0_raw[:, t, :] for t in range(PACK - 1)] + [after_dom0[:, 1, :]]
+        place(out_1, 0, 0, banks[0], dom0_mx, pw0_mx, after_dom0[:, 0, :], dv_windows[0])
+        neg_delta = held.tile([P, B, PACK], F32, name="neg_delta")
+        nc.scalar.activation(neg_delta[:], delta_sb[:], ACT.Copy, scale=minus_one[:])
         do0_mx = quantize(cast_by_query(do0_raw, "do0_grouped"), E5M2, "do0")
         dv_windows.append(new_window("dv_window3", clear=nc.gpsimd, tag="do0_grouped"))
         place(out_1, 0, 1, banks[4], dom0_mx, pw0_mx, do0_raw[:, 3, :], dv_windows[1])
         qm0 = cast_plain(qm0_raw)
-        ds0 = score_grad(0, do0_mx, v0_mx, gated_weights(0, p0, pw0_planes), do0_raw)
+        shifted0 = shifted_last(0, do0_mx, v0_mx)
+        ds0 = score_grad(0, do0_mx, v0_mx, shifted0, gated_weights(0, p0, pw0_planes), do0_raw)
+        dk_windows.append(new_window("dk_window0", clear=nc.gpsimd, tag="shifted0"))
         qm0_mx = quantize(qm0, E4M3, "qm0")
-        place(out_1, 0, 2, banks[7], dom0_mx, pw0_mx, q0_raws[0][:].rearrange("p j w -> p (j w)")[:, :N], dv_windows[2])
-        q1_mx = quantize(cast_by_query(q1_raw, "q1_grouped"), E4M3, "q1")
-        dk_windows.append(new_window("dk_window0", clear=nc.gpsimd, tag="q1_grouped"))
+        place(out_1, 0, 2, banks[7], dom0_mx, pw0_mx, q0_raw[:, 1, :], dv_windows[2])
+        q1_mx = quantize(cast_by_query(q1_raw), E4M3, "q1")
         ds0_mx = quantize(cast_plain(ds0, "ds0_grouped"), E5M2, "ds0")
         dk_windows.append(new_window("dk_window1", clear=nc.gpsimd, tag="ds0_grouped"))
-        place(out_1, 0, 3, banks[1], dom0_mx, pw0_mx, ds0[:, 3, :], dv_windows[3])
-        dk_windows.append(new_window("dk_window2", clear=nc.gpsimd, tag="do0_raw"))
+        place(out_1, 0, 3, banks[6], dom0_mx, pw0_mx, after_dom0[:, 2, :], dv_windows[3])
+        dk_windows.append(new_window("dk_window2", clear=nc.gpsimd, tag="dom0_raw"))
 
-        place(out_0, 0, 0, banks[4], qm0_mx, ds0_mx, q0_raws[1][:].rearrange("p j w -> p (j w)")[:, :N], dk_windows[0])
-        dk_windows.append(new_window("dk_window3", clear=nc.gpsimd, tag="q0_raw192"))
+        place(out_0, 0, 0, banks[4], qm0_mx, ds0_mx, q0_raw[:, 0, :], dk_windows[0])
+        dk_windows.append(new_window("dk_window3", clear=nc.gpsimd, tag="q0_raw"))
         p1 = weights(1, q1_mx, k1_mx)
         place(out_0, 0, 1, banks[5], qm0_mx, ds0_mx, qm0_raw[:, 1, :], dk_windows[1])
         pw1_tile = held.tile([P, PACK, N], F32, name="pw1_tile", tag="p0", align_bytes=64)
         pw1_planes = gated_weights(1, p1, [pw1_tile[:, t, :] for t in range(PACK)])
         place(out_0, 0, 2, banks[6], qm0_mx, ds0_mx, qm0_raw[:, 2, :], dk_windows[2])
         pw1_mx = quantize(cast_plain(pw1_tile), E4M3, "pw1")
-        dom1_mx = quantize(cast_plain(dom1_raw), E5M2, "dom1")
+        dom1_mx = quantize(cast_plain(dom1_raw, "in_turn"), E5M2, "dom1")
         place(out_0, 0, 3, banks[7], qm0_mx, ds0_mx, dom1_raw[:, 3, :], dk_windows[3])
-        qm1_mx = quantize(cast_plain(qm1_raw), E4M3, "qm1")
+        do1_mx = quantize(cast_by_query(do1_raw, "in_turn"), E5M2, "do1")
         place(out_1, 1, 0, banks[0], dom1_mx, pw1_mx, q1_raw[:, 0, :], dv_windows[0])
-        do1_mx = quantize(cast_by_query(do1_raw), E5M2, "do1")
         place(out_1, 1, 1, banks[4], dom1_mx, pw1_mx, do1_raw[:, 3, :], dv_windows[1])
-        ds1 = score_grad(1, do1_mx, v1_mx, pw1_planes, do1_raw)
+        qm1 = cast_plain(qm1_raw, "in_turn")
+        ds1 = score_grad(1, do1_mx, v1_mx, shifted_last(1, do1_mx, v1_mx), pw1_planes, do1_raw)
+        qm1_mx = quantize(qm1, E4M3, "qm1")
         place(out_1, 1, 2, banks[7], dom1_mx, pw1_mx, q1_raw[:, 2, :], dv_windows[2])
         ds1_mx = quantize(cast_plain(ds1), E5M2, "ds1")
         place(out_1, 1, 3, banks[1], dom1_mx, pw1_mx, ds1[:, 3, :], dv_windows[3])

@@ -176,10 +176,10 @@ def tile_attend_gat_lse_kv_kernel(
 
         last = PACK - 1
 
-        def shifted_last(b, do_mx, v_mx):
+        def shifted_last(b, do_mx, v_mx, neg_delta):
             shifted = held.tile([P, N], F32, name=f"shifted{b}", align_bytes=64)
             product(banks[4 + last], do_mx, last, v_mx)
-            nc.scalar.activation(shifted[:], banks[4 + last][:], ACT.Identity, bias=neg_delta[:, b, last : last + 1])
+            nc.scalar.activation(shifted[:], banks[4 + last][:], ACT.Identity, bias=neg_delta[:])
             return shifted
 
         def score_grad(b, do_mx, v_mx, shifted, pw, ds):
@@ -236,13 +236,13 @@ def tile_attend_gat_lse_kv_kernel(
         after_dom0 = held.tile([P, 3, N], F32, name="after_dom0", tag="dom0_raw", align_bytes=64)
         pw0_planes = [do0_raw[:, t, :] for t in range(PACK - 1)] + [after_dom0[:, 1, :]]
         place(out_1, 0, 0, banks[0], dom0_mx, pw0_mx, after_dom0[:, 0, :], dv_windows[0])
-        neg_delta = held.tile([P, B, PACK], F32, name="neg_delta")
-        nc.scalar.activation(neg_delta[:], delta_sb[:], ACT.Copy, scale=minus_one[:])
+        neg_delta0 = held.tile([P, 1], F32, name="neg_delta0")
+        nc.scalar.mul(neg_delta0[:], delta_sb[:, 0, last:], -1.0)
         do0_mx = quantize(cast_by_query(do0_raw, "do0_grouped"), E5M2, "do0")
         dv_windows.append(new_window("dv_window3", clear=nc.gpsimd, tag="do0_grouped"))
         place(out_1, 0, 1, banks[4], dom0_mx, pw0_mx, do0_raw[:, 3, :], dv_windows[1])
         qm0 = cast_plain(qm0_raw)
-        shifted0 = shifted_last(0, do0_mx, v0_mx)
+        shifted0 = shifted_last(0, do0_mx, v0_mx, neg_delta0)
         ds0 = score_grad(0, do0_mx, v0_mx, shifted0, gated_weights(0, p0, pw0_planes), do0_raw)
         dk_windows.append(new_window("dk_window0", clear=nc.gpsimd, tag="shifted0"))
         qm0_mx = quantize(qm0, E4M3, "qm0")
@@ -266,8 +266,10 @@ def tile_attend_gat_lse_kv_kernel(
         do1_mx = quantize(cast_by_query(do1_raw, "in_turn"), E5M2, "do1")
         place(out_1, 1, 0, banks[0], dom1_mx, pw1_mx, q1_raw[:, 0, :], dv_windows[0])
         place(out_1, 1, 1, banks[4], dom1_mx, pw1_mx, do1_raw[:, 3, :], dv_windows[1])
+        neg_delta1 = held.tile([P, 1], F32, name="neg_delta1", tag="dom0_codes", align_bytes=64)
+        nc.scalar.activation(neg_delta1[:], delta_sb[:, 1, last:], ACT.Copy, scale=minus_one[:])
         qm1 = cast_plain(qm1_raw, "in_turn")
-        ds1 = score_grad(1, do1_mx, v1_mx, shifted_last(1, do1_mx, v1_mx), pw1_planes, do1_raw)
+        ds1 = score_grad(1, do1_mx, v1_mx, shifted_last(1, do1_mx, v1_mx, neg_delta1), pw1_planes, do1_raw)
         qm1_mx = quantize(qm1, E4M3, "qm1")
         place(out_1, 1, 2, banks[7], dom1_mx, pw1_mx, q1_raw[:, 2, :], dv_windows[2])
         ds1_mx = quantize(cast_plain(ds1), E5M2, "ds1")

@@ -78,8 +78,6 @@ def tile_attend_gat_lse_kv_kernel(
 
         neg_lse = held.tile([P, B, PACK], F32, name="neg_lse")
         nc.scalar.mul(neg_lse[:], lse_sb[:], -1.0)
-        minus_one = held.tile([P, 1], F32, name="minus_one")
-        nc.gpsimd.iota(minus_one[:], pattern=[[0, 1]], base=-1, channel_multiplier=0, allow_small_or_imprecise_dtypes=True)
 
         def new_window(name, clear=nc.vector, tag=None):
             window = held.tile([P, T], F32, name=name, tag=tag or name, align_bytes=64)
@@ -208,6 +206,7 @@ def tile_attend_gat_lse_kv_kernel(
         q0_mx = quantize(q0, E4M3, "q0")
         k0_mx = gather(k_pool_words, 0, U32, "k0_codes", parts=2), k_picked_scales[0], E4M3
         k1_mx = gather(k_pool_words, 1, U32, "k1_codes"), k_picked_scales[1], E4M3
+        dv_windows.append(new_window("dv_window2", clear=nc.gpsimd, tag="k_pool_words"))
         p0 = held.tile([P, PACK, N], F32, name="p0", align_bytes=64)
         pw0 = new_grouped()
         gate = rw_sb[:, 0, :].unsqueeze(1).unsqueeze(3).broadcast_to([P, N // 8, PACK, 4])
@@ -217,6 +216,8 @@ def tile_attend_gat_lse_kv_kernel(
                 nc.scalar.activation(p0[:, t, slots], banks[4 * h + t][:, slots], ACT.Exp, bias=neg_lse[:, 0, t : t + 1])
             fours = slice(slots.start // 4, slots.stop // 4)
             nc.vector.tensor_tensor(interleaved(pw0)[:, fours], by_fours(p0)[:, fours], gate, ALU.mult)
+        minus_one = held.tile([P, 1], F32, name="minus_one", tag="q0_codes", align_bytes=64)
+        nc.gpsimd.iota(minus_one[:], pattern=[[0, 1]], base=-1, channel_multiplier=0, allow_small_or_imprecise_dtypes=True)
         dom0_mx = new_mx("dom0", E5M2)
         dom0_first = held.tile([P, P * PACK], BF16, name="dom0_first", align_bytes=64)
         nc.scalar.copy(interleaved(dom0_first), by_fours(dom0_raw)[:, : P // 4])
@@ -232,34 +233,33 @@ def tile_attend_gat_lse_kv_kernel(
                 scales=dom0_mx[1][:, cols],
                 in_=dom0_rest[:, PACK * (cols.start - P) : PACK * (cols.stop - P)],
             )
-        dv_windows.append(new_window("dv_window2", clear=nc.gpsimd, tag="dom0_rest"))
         after_dom0 = held.tile([P, 3, N], F32, name="after_dom0", tag="dom0_raw", align_bytes=64)
         pw0_planes = [do0_raw[:, t, :] for t in range(PACK - 1)] + [after_dom0[:, 1, :]]
         place(out_1, 0, 0, banks[0], dom0_mx, pw0_mx, after_dom0[:, 0, :], dv_windows[0])
         neg_delta0 = held.tile([P, 1], F32, name="neg_delta0")
         nc.scalar.mul(neg_delta0[:], delta_sb[:, 0, last:], -1.0)
-        do0_mx = quantize(cast_by_query(do0_raw, "do0_grouped"), E5M2, "do0")
-        dv_windows.append(new_window("dv_window3", clear=nc.gpsimd, tag="do0_grouped"))
+        do0_mx = quantize(cast_by_query(do0_raw), E5M2, "do0")
         place(out_1, 0, 1, banks[4], dom0_mx, pw0_mx, do0_raw[:, 3, :], dv_windows[1])
         qm0 = cast_plain(qm0_raw)
         shifted0 = shifted_last(0, do0_mx, v0_mx, neg_delta0)
         ds0 = score_grad(0, do0_mx, v0_mx, shifted0, gated_weights(0, p0, pw0_planes), do0_raw)
-        dk_windows.append(new_window("dk_window0", clear=nc.gpsimd, tag="shifted0"))
+        dv_windows.append(new_window("dv_window3", clear=nc.gpsimd, tag="shifted0"))
         qm0_mx = quantize(qm0, E4M3, "qm0")
         place(out_1, 0, 2, banks[7], dom0_mx, pw0_mx, q0_raw[:, 1, :], dv_windows[2])
         q1_mx = quantize(cast_by_query(q1_raw), E4M3, "q1")
         ds0_mx = quantize(cast_plain(ds0, "ds0_grouped"), E5M2, "ds0")
-        dk_windows.append(new_window("dk_window1", clear=nc.gpsimd, tag="ds0_grouped"))
+        dk_windows.append(new_window("dk_window0", clear=nc.gpsimd, tag="ds0_grouped"))
         place(out_1, 0, 3, banks[6], dom0_mx, pw0_mx, after_dom0[:, 2, :], dv_windows[3])
-        dk_windows.append(new_window("dk_window2", clear=nc.gpsimd, tag="dom0_raw"))
+        dk_windows.append(new_window("dk_window1", clear=nc.gpsimd, tag="dom0_raw"))
 
         place(out_0, 0, 0, banks[4], qm0_mx, ds0_mx, q0_raw[:, 0, :], dk_windows[0])
-        dk_windows.append(new_window("dk_window3", clear=nc.gpsimd, tag="q0_raw"))
+        dk_windows.append(new_window("dk_window2", clear=nc.gpsimd, tag="q0_raw"))
         p1 = weights(1, q1_mx, k1_mx)
         place(out_0, 0, 1, banks[5], qm0_mx, ds0_mx, qm0_raw[:, 1, :], dk_windows[1])
+        dk_windows.append(new_window("dk_window3", clear=nc.gpsimd, tag="qm0_raw"))
         pw1_tile = held.tile([P, PACK, N], F32, name="pw1_tile", tag="p0", align_bytes=64)
         pw1_planes = gated_weights(1, p1, [pw1_tile[:, t, :] for t in range(PACK)])
-        place(out_0, 0, 2, banks[6], qm0_mx, ds0_mx, qm0_raw[:, 2, :], dk_windows[2])
+        place(out_0, 0, 2, banks[6], qm0_mx, ds0_mx, do0_raw[:, 2, :], dk_windows[2])
         pw1_mx = quantize(cast_plain(pw1_tile), E4M3, "pw1")
         dom1_mx = quantize(cast_plain(dom1_raw, "in_turn"), E5M2, "dom1")
         place(out_0, 0, 3, banks[7], qm0_mx, ds0_mx, dom1_raw[:, 3, :], dk_windows[3])

@@ -137,6 +137,21 @@ def tile_attend_gat_lse_kv_kernel(
             cast_plain_cols(grouped, raw, slice(0, 512))
             return grouped
 
+        def first_columns(mx, raw, name, tag=None):
+            first = held.tile([P, P * PACK], BF16, name=name, tag=tag or name, align_bytes=64)
+            nc.scalar.copy(interleaved(first), by_fours(raw)[:, : P // 4])
+            quantize_half(mx, first, slice(0, P))
+
+        def other_columns(mx, raw, name, tag=None):
+            rest = held.tile([P, 3 * P * PACK], BF16, name=name, tag=tag or name, align_bytes=64)
+            nc.scalar.copy(interleaved(rest), by_fours(raw)[:, P // 4 :])
+            for cols in (slice(P, 2 * P), slice(2 * P, 4 * P)):
+                nc.vector.quantize_mx(
+                    out=mx[0][:, cols].bitcast(mx[2]),
+                    scales=mx[1][:, cols],
+                    in_=rest[:, PACK * (cols.start - P) : PACK * (cols.stop - P)],
+                )
+
         def cast_by_query_rows(grouped, raw, rows):
             nc.scalar.copy(
                 grouped[:].rearrange("p (t m j) -> p m j t", t=PACK, j=PACK)[:, rows],
@@ -219,20 +234,11 @@ def tile_attend_gat_lse_kv_kernel(
         minus_one = held.tile([P, 1], F32, name="minus_one", tag="q0_codes", align_bytes=64)
         nc.gpsimd.iota(minus_one[:], pattern=[[0, 1]], base=-1, channel_multiplier=0, allow_small_or_imprecise_dtypes=True)
         dom0_mx = new_mx("dom0", E5M2)
-        dom0_first = held.tile([P, P * PACK], BF16, name="dom0_first", align_bytes=64)
-        nc.scalar.copy(interleaved(dom0_first), by_fours(dom0_raw)[:, : P // 4])
-        quantize_half(dom0_mx, dom0_first, slice(0, P))
+        first_columns(dom0_mx, dom0_raw, "dom0_first")
         pw0_mx = quantize(pw0, E4M3, "pw0")
         v0_mx = gather(v_pool_words, 0, U32, "v0_codes"), v_picked_scales[0], E4M3
         v1_mx = gather(v_pool_words, 1, U32, "v1_codes"), v_picked_scales[1], E4M3
-        dom0_rest = held.tile([P, 3 * P * PACK], BF16, name="dom0_rest", align_bytes=64)
-        nc.scalar.copy(interleaved(dom0_rest), by_fours(dom0_raw)[:, P // 4 :])
-        for cols in (slice(P, 2 * P), halves[1]):
-            nc.vector.quantize_mx(
-                out=dom0_mx[0][:, cols].bitcast(E5M2),
-                scales=dom0_mx[1][:, cols],
-                in_=dom0_rest[:, PACK * (cols.start - P) : PACK * (cols.stop - P)],
-            )
+        other_columns(dom0_mx, dom0_raw, "dom0_rest")
         after_dom0 = held.tile([P, 3, N], F32, name="after_dom0", tag="dom0_raw", align_bytes=64)
         pw0_planes = [do0_raw[:, t, :] for t in range(PACK - 1)] + [after_dom0[:, 1, :]]
         place(out_1, 0, 0, banks[0], dom0_mx, pw0_mx, after_dom0[:, 0, :], dv_windows[0])
@@ -245,31 +251,36 @@ def tile_attend_gat_lse_kv_kernel(
         ds0 = score_grad(0, do0_mx, v0_mx, shifted0, gated_weights(0, p0, pw0_planes), do0_raw)
         dv_windows.append(new_window("dv_window3", clear=nc.gpsimd, tag="shifted0"))
         qm0_mx = quantize(qm0, E4M3, "qm0")
-        place(out_1, 0, 2, banks[7], dom0_mx, pw0_mx, q0_raw[:, 1, :], dv_windows[2])
-        q1_mx = quantize(cast_by_query(q1_raw), E4M3, "q1")
+        place(out_1, 0, 2, banks[7], dom0_mx, pw0_mx, after_dom0[:, 2, :], dv_windows[2])
         ds0_mx = quantize(cast_plain(ds0, "ds0_grouped"), E5M2, "ds0")
         dk_windows.append(new_window("dk_window0", clear=nc.gpsimd, tag="ds0_grouped"))
-        place(out_1, 0, 3, banks[6], dom0_mx, pw0_mx, after_dom0[:, 2, :], dv_windows[3])
+        place(out_1, 0, 3, banks[6], dom0_mx, pw0_mx, q0_raw[:, 1, :], dv_windows[3])
+        q1_mx = quantize(cast_by_query(q1_raw, "dom0_raw"), E4M3, "q1")
         dk_windows.append(new_window("dk_window1", clear=nc.gpsimd, tag="dom0_raw"))
 
         place(out_0, 0, 0, banks[4], qm0_mx, ds0_mx, q0_raw[:, 0, :], dk_windows[0])
         dk_windows.append(new_window("dk_window2", clear=nc.gpsimd, tag="q0_raw"))
-        p1 = weights(1, q1_mx, k1_mx)
         place(out_0, 0, 1, banks[5], qm0_mx, ds0_mx, qm0_raw[:, 1, :], dk_windows[1])
         dk_windows.append(new_window("dk_window3", clear=nc.gpsimd, tag="qm0_raw"))
+        p1 = weights(1, q1_mx, k1_mx)
         pw1_tile = held.tile([P, PACK, N], F32, name="pw1_tile", tag="p0", align_bytes=64)
         pw1_planes = gated_weights(1, p1, [pw1_tile[:, t, :] for t in range(PACK)])
-        place(out_0, 0, 2, banks[6], qm0_mx, ds0_mx, do0_raw[:, 2, :], dk_windows[2])
-        pw1_mx = quantize(cast_plain(pw1_tile), E4M3, "pw1")
-        dom1_mx = quantize(cast_plain(dom1_raw, "in_turn"), E5M2, "dom1")
-        place(out_0, 0, 3, banks[7], qm0_mx, ds0_mx, dom1_raw[:, 3, :], dk_windows[3])
-        do1_mx = quantize(cast_by_query(do1_raw, "in_turn"), E5M2, "do1")
+        place(out_0, 0, 2, banks[2], qm0_mx, ds0_mx, do0_raw[:, 2, :], dk_windows[2])
+        pw1_mx = quantize(cast_plain(pw1_tile, "pw1_grouped"), E4M3, "pw1")
+        dom1_mx = new_mx("dom1", E5M2)
+        first_columns(dom1_mx, dom1_raw, "dom1_first", "k1_codes")
+        place(out_0, 0, 3, banks[3], qm0_mx, ds0_mx, do0_raw[:, 3, :], dk_windows[3])
+        other_columns(dom1_mx, dom1_raw, "dom1_rest", "pw1_grouped")
         place(out_1, 1, 0, banks[0], dom1_mx, pw1_mx, q1_raw[:, 0, :], dv_windows[0])
+        do1_mx = quantize(cast_by_query(do1_raw, "k1_codes"), E5M2, "do1")
         place(out_1, 1, 1, banks[4], dom1_mx, pw1_mx, do1_raw[:, 3, :], dv_windows[1])
         neg_delta1 = held.tile([P, 1], F32, name="neg_delta1", tag="dom0_codes", align_bytes=64)
         nc.scalar.activation(neg_delta1[:], delta_sb[:, 1, last:], ACT.Copy, scale=minus_one[:])
-        qm1 = cast_plain(qm1_raw, "in_turn")
-        ds1 = score_grad(1, do1_mx, v1_mx, shifted_last(1, do1_mx, v1_mx, neg_delta1), pw1_planes, do1_raw)
+        qm1 = new_grouped("k1_codes")
+        cast_plain_cols(qm1, qm1_raw, halves[0])
+        shifted1 = shifted_last(1, do1_mx, v1_mx, neg_delta1)
+        cast_plain_cols(qm1, qm1_raw, halves[1])
+        ds1 = score_grad(1, do1_mx, v1_mx, shifted1, pw1_planes, do1_raw)
         qm1_mx = quantize(qm1, E4M3, "qm1")
         place(out_1, 1, 2, banks[7], dom1_mx, pw1_mx, q1_raw[:, 2, :], dv_windows[2])
         ds1_mx = quantize(cast_plain(ds1), E5M2, "ds1")

@@ -54,7 +54,7 @@ def tile_attend_gat_lse_kv_kernel(
                 nc.sync.dma_start(out=pool_scales[row:P:32, :].bitcast(I32), in_=scales[0, row:16:4, :].bitcast(I32))
 
         def load_per_query(vec, name):
-            col = held.tile([P, B, PACK], F32, name=name)
+            col = held.tile([P, B, PACK], F32, name=name, align_bytes=64)
             nc.sync.dma_start(out=col[:], in_=vec.rearrange("b (p t) o -> p b (t o)", t=PACK))
             return col
 
@@ -85,6 +85,7 @@ def tile_attend_gat_lse_kv_kernel(
             return window
 
         dv_windows = [new_window(f"dv_window{c}") for c in range(2)]
+        dv_windows.append(new_window("dv_window2", clear=nc.gpsimd, tag="lse_sb"))
         dk_windows = []
 
         def gather(pool_tile, b, dtype, name, tag=None, parts=1):
@@ -213,15 +214,16 @@ def tile_attend_gat_lse_kv_kernel(
 
         k_picked_scales = gather_all(k_pool_scales, U8, "k_scales")
         v_picked_scales = gather_all(v_pool_scales, U8, "v_scales")
-        q0 = new_grouped()
+        q0 = new_grouped("q0_grouped")
         q0_dealt = q0[:].rearrange("p (t m j) -> p m j t", t=PACK, j=PACK)
         q0_rows = q0_raw[:].rearrange("p j (m t) -> p m j t", t=PACK)
         nc.scalar.copy(q0_dealt[:, :, :, :2], q0_rows[:, :, :, :2])
         nc.vector.tensor_copy(q0_dealt[:, :, :, 2:], q0_rows[:, :, :, 2:])
         q0_mx = quantize(q0, E4M3, "q0")
+        dv_windows.append(new_window("dv_window3", clear=nc.gpsimd, tag="q0_grouped"))
         k0_mx = gather(k_pool_words, 0, U32, "k0_codes", parts=2), k_picked_scales[0], E4M3
         k1_mx = gather(k_pool_words, 1, U32, "k1_codes"), k_picked_scales[1], E4M3
-        dv_windows.append(new_window("dv_window2", clear=nc.gpsimd, tag="k_pool_words"))
+        dk_windows.append(new_window("dk_window0", clear=nc.gpsimd, tag="k_pool_words"))
         p0 = held.tile([P, PACK, N], F32, name="p0", align_bytes=64)
         pw0 = new_grouped()
         gate = rw_sb[:, 0, :].unsqueeze(1).unsqueeze(3).broadcast_to([P, N // 8, PACK, 4])
@@ -249,19 +251,17 @@ def tile_attend_gat_lse_kv_kernel(
         qm0 = cast_plain(qm0_raw)
         shifted0 = shifted_last(0, do0_mx, v0_mx, neg_delta0)
         ds0 = score_grad(0, do0_mx, v0_mx, shifted0, gated_weights(0, p0, pw0_planes), do0_raw)
-        dv_windows.append(new_window("dv_window3", clear=nc.gpsimd, tag="shifted0"))
+        dk_windows.append(new_window("dk_window1", clear=nc.gpsimd, tag="shifted0"))
         qm0_mx = quantize(qm0, E4M3, "qm0")
         place(out_1, 0, 2, banks[7], dom0_mx, pw0_mx, after_dom0[:, 2, :], dv_windows[2])
         ds0_mx = quantize(cast_plain(ds0, "ds0_grouped"), E5M2, "ds0")
-        dk_windows.append(new_window("dk_window0", clear=nc.gpsimd, tag="ds0_grouped"))
+        dk_windows.append(new_window("dk_window2", clear=nc.gpsimd, tag="ds0_grouped"))
         place(out_1, 0, 3, banks[6], dom0_mx, pw0_mx, q0_raw[:, 1, :], dv_windows[3])
         q1_mx = quantize(cast_by_query(q1_raw, "dom0_raw"), E4M3, "q1")
-        dk_windows.append(new_window("dk_window1", clear=nc.gpsimd, tag="dom0_raw"))
+        dk_windows.append(new_window("dk_window3", clear=nc.gpsimd, tag="dom0_raw"))
 
         place(out_0, 0, 0, banks[4], qm0_mx, ds0_mx, q0_raw[:, 0, :], dk_windows[0])
-        dk_windows.append(new_window("dk_window2", clear=nc.gpsimd, tag="q0_raw"))
         place(out_0, 0, 1, banks[5], qm0_mx, ds0_mx, qm0_raw[:, 1, :], dk_windows[1])
-        dk_windows.append(new_window("dk_window3", clear=nc.gpsimd, tag="qm0_raw"))
         p1 = weights(1, q1_mx, k1_mx)
         pw1_tile = held.tile([P, PACK, N], F32, name="pw1_tile", tag="p0", align_bytes=64)
         pw1_planes = gated_weights(1, p1, [pw1_tile[:, t, :] for t in range(PACK)])

@@ -71,8 +71,8 @@ def tile_attend_gat_lse_kv_kernel(
         delta_sb = load_per_query(delta, "delta_sb")
         do0_raw = load_rows(doT[0], "do0_raw")
         qm0_raw = load_rows(qm[0], "qm0_raw")
-        q1_raw = load_rows(qT[1], "q1_raw")
         dom1_raw = load_rows(dom[1], "dom1_raw")
+        q1_raw = load_rows(qT[1], "q1_raw")
         do1_raw = load_rows(doT[1], "do1_raw")
         qm1_raw = load_rows(qm[1], "qm1_raw")
 
@@ -254,6 +254,7 @@ def tile_attend_gat_lse_kv_kernel(
         dk_windows.append(new_window("dk_window1", clear=nc.gpsimd, tag="shifted0"))
         qm0_mx = quantize(qm0, E4M3, "qm0")
         place(out_1, 0, 2, banks[7], dom0_mx, pw0_mx, after_dom0[:, 2, :], dv_windows[2])
+        dom1_mx = quantize(cast_plain(dom1_raw), E5M2, "dom1")
         ds0_mx = quantize(cast_plain(ds0, "ds0_grouped"), E5M2, "ds0")
         dk_windows.append(new_window("dk_window2", clear=nc.gpsimd, tag="ds0_grouped"))
         place(out_1, 0, 3, banks[6], dom0_mx, pw0_mx, q0_raw[:, 1, :], dv_windows[3])
@@ -262,27 +263,27 @@ def tile_attend_gat_lse_kv_kernel(
 
         place(out_0, 0, 0, banks[4], qm0_mx, ds0_mx, q0_raw[:, 0, :], dk_windows[0])
         place(out_0, 0, 1, banks[5], qm0_mx, ds0_mx, qm0_raw[:, 1, :], dk_windows[1])
+        do1 = new_grouped("k0_codes")
+        cast_by_query_rows(do1, do1_raw, slice(0, P // 2))
         p1 = weights(1, q1_mx, k1_mx)
         pw1_tile = held.tile([P, PACK, N], F32, name="pw1_tile", tag="p0", align_bytes=64)
         pw1_planes = gated_weights(1, p1, [pw1_tile[:, t, :] for t in range(PACK)])
         place(out_0, 0, 2, banks[2], qm0_mx, ds0_mx, do0_raw[:, 2, :], dk_windows[2])
         pw1_mx = quantize(cast_plain(pw1_tile, "pw1_grouped"), E4M3, "pw1")
-        dom1_mx = new_mx("dom1", E5M2)
-        first_columns(dom1_mx, dom1_raw, "dom1_first", "k1_codes")
         place(out_0, 0, 3, banks[3], qm0_mx, ds0_mx, do0_raw[:, 3, :], dk_windows[3])
-        other_columns(dom1_mx, dom1_raw, "dom1_rest", "pw1_grouped")
-        place(out_1, 1, 0, banks[0], dom1_mx, pw1_mx, q1_raw[:, 0, :], dv_windows[0])
-        do1_mx = quantize(cast_by_query(do1_raw, "k1_codes"), E5M2, "do1")
-        place(out_1, 1, 1, banks[4], dom1_mx, pw1_mx, do1_raw[:, 3, :], dv_windows[1])
-        neg_delta1 = held.tile([P, 1], F32, name="neg_delta1", tag="dom0_codes", align_bytes=64)
-        nc.scalar.activation(neg_delta1[:], delta_sb[:, 1, last:], ACT.Copy, scale=minus_one[:])
-        qm1 = new_grouped("k1_codes")
-        cast_plain_cols(qm1, qm1_raw, halves[0])
-        shifted1 = shifted_last(1, do1_mx, v1_mx, neg_delta1)
-        cast_plain_cols(qm1, qm1_raw, halves[1])
-        ds1 = score_grad(1, do1_mx, v1_mx, shifted1, pw1_planes, do1_raw)
-        qm1_mx = quantize(qm1, E4M3, "qm1")
-        place(out_1, 1, 2, banks[7], dom1_mx, pw1_mx, q1_raw[:, 2, :], dv_windows[2])
+        cast_by_query_rows(do1, do1_raw, slice(P // 2, P))
+        do1_mx = quantize(do1, E5M2, "do1")
+        place(out_1, 1, 0, banks[0], dom1_mx, pw1_mx, do1_raw[:, 0, :], dv_windows[0])
+        place(out_1, 1, 1, banks[1], dom1_mx, pw1_mx, do1_raw[:, 1, :], dv_windows[1])
+        neg_delta1 = held.tile([P, PACK], F32, name="neg_delta1", tag="dom0_codes", align_bytes=64)
+        nc.scalar.activation(neg_delta1[:], delta_sb[:, 1, :], ACT.Copy, scale=minus_one[:])
+        qm1_mx = quantize(cast_plain(qm1_raw, "pw1_grouped"), E4M3, "qm1")
+        ds1 = q1_raw
+        for t in range(PACK):
+            product(banks[4 + t], do1_mx, t, v1_mx)
+            nc.scalar.activation(dom1_raw[:, t, :], banks[4 + t][:], ACT.Identity, bias=neg_delta1[:, t : t + 1])
+            nc.gpsimd.tensor_tensor(ds1[:, t, :], dom1_raw[:, t, :], pw1_planes[t], ALU.mult)
+        place(out_1, 1, 2, banks[7], dom1_mx, pw1_mx, do1_raw[:, 2, :], dv_windows[2])
         ds1_mx = quantize(cast_plain(ds1), E5M2, "ds1")
         place(out_1, 1, 3, banks[1], dom1_mx, pw1_mx, ds1[:, 3, :], dv_windows[3])
         for c in range(4):

@@ -39,10 +39,10 @@ def tile_attend_gat_lse_kv_kernel(
             nc.sync.dma_start(out=raw[:], in_=rows.rearrange("(p j) w -> p j w", j=PACK))
             return raw
 
-        def load_words(words, name):
-            pool_words = held.tile([P, T], U32, name=name, align_bytes=64)
-            nc.sync.dma_start(out=pool_words[:].bitcast(I32), in_=words[0].rearrange("p n t -> p (n t)").bitcast(I32))
-            return pool_words
+        def load_words(pool_words, words, tokens):
+            nc.sync.dma_start(
+                out=pool_words[:, tokens].bitcast(I32), in_=words[0].rearrange("p n t -> p (n t)").bitcast(I32)[:, tokens]
+            )
 
         def new_scales(name):
             pool_scales = held.tile([P, T], U8, name=name, align_bytes=64)
@@ -63,30 +63,34 @@ def tile_attend_gat_lse_kv_kernel(
         rw_sb = load_per_query(rw, "rw_sb")
         k_pool_scales, v_pool_scales = new_scales("k_pool_scales"), new_scales("v_pool_scales")
         load_scales(k_pool_scales, k_scales, range(4))
-        load_scales(v_pool_scales, v_scales, range(4))
+        k_pool_words = held.tile([P, T], U32, name="k_pool_words", align_bytes=64)
+        v_pool_words = held.tile([P, T], U32, name="v_pool_words", align_bytes=64)
+        load_words(k_pool_words, k_words, slice(0, T))
         q0_raw = load_rows(qT[0], "q0_raw")
-        k_pool_words = load_words(k_words, "k_pool_words")
+        load_scales(v_pool_scales, v_scales, range(4))
         dom0_raw = load_rows(dom[0], "dom0_raw")
-        v_pool_words = load_words(v_words, "v_pool_words")
-        delta_sb = load_per_query(delta, "delta_sb")
-        do0_raw = load_rows(doT[0], "do0_raw")
-        qm0_raw = load_rows(qm[0], "qm0_raw")
-        dom1_raw = load_rows(dom[1], "dom1_raw")
+        load_words(v_pool_words, v_words, slice(0, T // 2))
         q1_raw = load_rows(qT[1], "q1_raw")
+        load_words(v_pool_words, v_words, slice(T // 2, T))
+        dom1_raw = load_rows(dom[1], "dom1_raw")
+        do0_raw = load_rows(doT[0], "do0_raw")
+        delta_sb = load_per_query(delta, "delta_sb")
+        qm0_raw = load_rows(qm[0], "qm0_raw")
         do1_raw = load_rows(doT[1], "do1_raw")
         qm1_raw = load_rows(qm[1], "qm1_raw")
 
         neg_lse = held.tile([P, B, PACK], F32, name="neg_lse")
         nc.scalar.mul(neg_lse[:], lse_sb[:], -1.0)
+        neg_rw0 = held.tile([P, PACK], F32, name="neg_rw0")
+        nc.scalar.mul(neg_rw0[:], rw_sb[:, 0, :], -1.0)
 
         def new_window(name, clear=nc.vector, tag=None):
             window = held.tile([P, T], F32, name=name, tag=tag or name, align_bytes=64)
             clear.memset(window[:].bitcast(I32), 0)
             return window
 
-        dv_windows = [new_window(f"dv_window{c}") for c in range(2)]
-        dv_windows.append(new_window("dv_window2", clear=nc.gpsimd, tag="lse_sb"))
-        dk_windows = []
+        windows = [new_window(f"window{c}") for c in range(2)]
+        windows.append(new_window("window2", clear=nc.gpsimd, tag="lse_sb"))
 
         def gather(pool_tile, b, dtype, name, tag=None, parts=1):
             picked = held.tile([P, N], dtype, name=name, tag=tag or name, align_bytes=64)
@@ -176,115 +180,108 @@ def tile_attend_gat_lse_kv_kernel(
                 stop=True,
             )
 
-        def weights(b, q_mx, k_mx):
-            p = held.tile([P, PACK, N], F32, name=f"p{b}", tag="v_pool_words", align_bytes=64)
-            for t in range(PACK):
-                product(banks[t], q_mx, t, k_mx)
-                nc.scalar.activation(p[:, t, :], banks[t][:], ACT.Exp, bias=neg_lse[:, b, t : t + 1])
-            return p
+        def half_columns(mx, raw, cols, tag):
+            half = held.tile([P, 256 * PACK], BF16, name="half_on_" + tag, tag=tag, align_bytes=64)
+            nc.scalar.copy(interleaved(half), by_fours(raw)[:, cols.start // 4 : cols.stop // 4])
+            quantize_half(mx, half, cols)
 
-        def gated_weights(b, p, pw):
-            for t in range(PACK):
-                nc.scalar.activation(pw[t], p[:, t, :], ACT.Copy, scale=rw_sb[:, b, t : t + 1])
-            return pw
-
-        last = PACK - 1
-
-        def shifted_last(b, do_mx, v_mx, neg_delta):
-            shifted = held.tile([P, N], F32, name=f"shifted{b}", align_bytes=64)
-            product(banks[4 + last], do_mx, last, v_mx)
-            nc.scalar.activation(shifted[:], banks[4 + last][:], ACT.Identity, bias=neg_delta[:])
-            return shifted
-
-        def score_grad(b, do_mx, v_mx, shifted, pw, ds):
-            nc.gpsimd.tensor_tensor(ds[:, last, :], shifted[:], pw[last], ALU.mult)
-            for t in range(last):
-                product(banks[4 + t], do_mx, t, v_mx)
-                nc.vector.scalar_tensor_tensor(
-                    ds[:, t, :], banks[4 + t][:], delta_sb[:, b, t : t + 1], pw[t], ALU.subtract, ALU.mult
-                )
-            return ds
+        def scatter(b, bank, staged, window, slots=slice(0, N)):
+            entries = slice((b * N + slots.start) // 16, (b * N + slots.stop) // 16)
+            nc.scalar.copy(staged[:, slots], bank[:, slots])
+            nc.vector.tensor_copy(window[:].indirect(offsets[:, entries]), staged[:, slots])
 
         def place(out, b, c, bank, stationary, moving, staged, window):
             product(bank, stationary, c, moving)
-            nc.scalar.copy(staged, bank[:])
-            nc.vector.tensor_copy(window[:].indirect(offsets[:, b * LIST_COLS : (b + 1) * LIST_COLS]), staged)
+            scatter(b, bank, staged, window)
             if b == B - 1:
                 nc.sync.dma_start(out=out[c * P : (c + 1) * P, :], in_=window[:])
 
         k_picked_scales = gather_all(k_pool_scales, U8, "k_scales")
-        v_picked_scales = gather_all(v_pool_scales, U8, "v_scales")
-        q0 = new_grouped("q0_grouped")
-        q0_dealt = q0[:].rearrange("p (t m j) -> p m j t", t=PACK, j=PACK)
+        k_picked_words = gather_all(k_pool_words, U32, "k_codes")
+        k0_mx = k_picked_words[0], k_picked_scales[0], E4M3
+        k1_mx = k_picked_words[1], k_picked_scales[1], E4M3
+
+        q0_mx = new_mx("q0", E4M3)
         q0_rows = q0_raw[:].rearrange("p j (m t) -> p m j t", t=PACK)
-        nc.scalar.copy(q0_dealt[:, :, :, :2], q0_rows[:, :, :, :2])
-        nc.vector.tensor_copy(q0_dealt[:, :, :, 2:], q0_rows[:, :, :, 2:])
-        q0_mx = quantize(q0, E4M3, "q0")
-        dv_windows.append(new_window("dv_window3", clear=nc.gpsimd, tag="q0_grouped"))
-        k0_mx = gather(k_pool_words, 0, U32, "k0_codes", parts=2), k_picked_scales[0], E4M3
-        k1_mx = gather(k_pool_words, 1, U32, "k1_codes"), k_picked_scales[1], E4M3
-        dk_windows.append(new_window("dk_window0", clear=nc.gpsimd, tag="k_pool_words"))
+        for h, copy in ((1, nc.vector.tensor_copy), (0, nc.scalar.copy)):
+            part = held.tile([P, 256 * PACK], BF16, name=f"q0_part{h}", align_bytes=64)
+            copy(part[:].rearrange("p (t m j) -> p m j t", t=2, j=PACK), q0_rows[:, :, :, 2 * h : 2 * h + 2])
+            quantize_half(q0_mx, part, halves[h])
+        windows.append(new_window("window3", clear=nc.gpsimd, tag="q0_part0"))
+        v_picked_scales = gather_all(v_pool_scales, U8, "v_scales")
         p0 = held.tile([P, PACK, N], F32, name="p0", align_bytes=64)
         pw0 = new_grouped()
         gate = rw_sb[:, 0, :].unsqueeze(1).unsqueeze(3).broadcast_to([P, N // 8, PACK, 4])
         for h, slots in enumerate(halves):
-            for t in range(PACK):
-                product(banks[4 * h + t], q0_mx, t, k0_mx, slots)
-                nc.scalar.activation(p0[:, t, slots], banks[4 * h + t][:, slots], ACT.Exp, bias=neg_lse[:, 0, t : t + 1])
+            for t in ((2, 3, 0, 1), (0, 1, 2, 3))[h]:
+                bank = banks[t if t >= 2 else 4 * h + t]
+                product(bank, q0_mx, t, k0_mx, slots)
+                nc.scalar.activation(p0[:, t, slots], bank[:, slots], ACT.Exp, bias=neg_lse[:, 0, t : t + 1])
             fours = slice(slots.start // 4, slots.stop // 4)
             nc.vector.tensor_tensor(interleaved(pw0)[:, fours], by_fours(p0)[:, fours], gate, ALU.mult)
-        minus_one = held.tile([P, 1], F32, name="minus_one", tag="q0_codes", align_bytes=64)
-        nc.gpsimd.iota(minus_one[:], pattern=[[0, 1]], base=-1, channel_multiplier=0, allow_small_or_imprecise_dtypes=True)
         dom0_mx = new_mx("dom0", E5M2)
         first_columns(dom0_mx, dom0_raw, "dom0_first")
         pw0_mx = quantize(pw0, E4M3, "pw0")
-        v0_mx = gather(v_pool_words, 0, U32, "v0_codes"), v_picked_scales[0], E4M3
-        v1_mx = gather(v_pool_words, 1, U32, "v1_codes"), v_picked_scales[1], E4M3
         other_columns(dom0_mx, dom0_raw, "dom0_rest")
-        after_dom0 = held.tile([P, 3, N], F32, name="after_dom0", tag="dom0_raw", align_bytes=64)
-        pw0_planes = [do0_raw[:, t, :] for t in range(PACK - 1)] + [after_dom0[:, 1, :]]
-        place(out_1, 0, 0, banks[0], dom0_mx, pw0_mx, after_dom0[:, 0, :], dv_windows[0])
-        neg_delta0 = held.tile([P, 1], F32, name="neg_delta0")
-        nc.scalar.mul(neg_delta0[:], delta_sb[:, 0, last:], -1.0)
-        do0_mx = quantize(cast_by_query(do0_raw), E5M2, "do0")
-        place(out_1, 0, 1, banks[4], dom0_mx, pw0_mx, do0_raw[:, 3, :], dv_windows[1])
-        qm0 = cast_plain(qm0_raw)
-        shifted0 = shifted_last(0, do0_mx, v0_mx, neg_delta0)
-        ds0 = score_grad(0, do0_mx, v0_mx, shifted0, gated_weights(0, p0, pw0_planes), do0_raw)
-        dk_windows.append(new_window("dk_window1", clear=nc.gpsimd, tag="shifted0"))
-        qm0_mx = quantize(qm0, E4M3, "qm0")
-        place(out_1, 0, 2, banks[7], dom0_mx, pw0_mx, after_dom0[:, 2, :], dv_windows[2])
-        dom1_mx = quantize(cast_plain(dom1_raw), E5M2, "dom1")
-        ds0_mx = quantize(cast_plain(ds0, "ds0_grouped"), E5M2, "ds0")
-        dk_windows.append(new_window("dk_window2", clear=nc.gpsimd, tag="ds0_grouped"))
-        place(out_1, 0, 3, banks[6], dom0_mx, pw0_mx, q0_raw[:, 1, :], dv_windows[3])
-        q1_mx = quantize(cast_by_query(q1_raw, "dom0_raw"), E4M3, "q1")
-        dk_windows.append(new_window("dk_window3", clear=nc.gpsimd, tag="dom0_raw"))
+        v_picked_words = gather_all(v_pool_words, U32, "v_codes")
+        v0_mx = v_picked_words[0], v_picked_scales[0], E4M3
+        v1_mx = v_picked_words[1], v_picked_scales[1], E4M3
 
-        place(out_0, 0, 0, banks[4], qm0_mx, ds0_mx, q0_raw[:, 0, :], dk_windows[0])
-        place(out_0, 0, 1, banks[5], qm0_mx, ds0_mx, qm0_raw[:, 1, :], dk_windows[1])
-        do1 = new_grouped("k0_codes")
-        cast_by_query_rows(do1, do1_raw, slice(0, P // 2))
-        p1 = weights(1, q1_mx, k1_mx)
-        pw1_tile = held.tile([P, PACK, N], F32, name="pw1_tile", tag="p0", align_bytes=64)
-        pw1_planes = gated_weights(1, p1, [pw1_tile[:, t, :] for t in range(PACK)])
-        place(out_0, 0, 2, banks[2], qm0_mx, ds0_mx, do0_raw[:, 2, :], dk_windows[2])
-        pw1_mx = quantize(cast_plain(pw1_tile, "pw1_grouped"), E4M3, "pw1")
-        place(out_0, 0, 3, banks[3], qm0_mx, ds0_mx, do0_raw[:, 3, :], dk_windows[3])
-        cast_by_query_rows(do1, do1_raw, slice(P // 2, P))
+        q1_mx = quantize(cast_by_query(q1_raw), E4M3, "q1")
+        place(out_1, 0, 0, banks[0], dom0_mx, pw0_mx, q1_raw[:, 0, :], windows[0])
+        place(out_1, 0, 1, banks[1], dom0_mx, pw0_mx, q1_raw[:, 1, :], windows[1])
+        place(out_1, 0, 2, banks[2], dom0_mx, pw0_mx, q1_raw[:, 2, :], windows[2])
+        p1 = held.tile([P, PACK, N], F32, name="p1", tag="k_pool_words", align_bytes=64)
+        for t in range(PACK):
+            product(banks[4 + t], q1_mx, t, k1_mx)
+            nc.scalar.activation(p1[:, t, :], banks[4 + t][:], ACT.Exp, bias=neg_lse[:, 1, t : t + 1])
+        pw1 = held.tile([P, PACK, N], F32, name="pw1", tag="v_pool_words", align_bytes=64)
+        for slots in halves:
+            for t in range(PACK):
+                nc.scalar.activation(pw1[:, t, slots], p1[:, t, slots], ACT.Copy, scale=rw_sb[:, 1, t : t + 1])
+        pw1_grouped = new_grouped()
+        for slots in halves:
+            cast_plain_cols(pw1_grouped, pw1, slots)
+        pw1_mx = quantize(pw1_grouped, E4M3, "pw1")
+        dom1_mx = new_mx("dom1", E5M2)
+        half_columns(dom1_mx, dom1_raw, halves[0], "dom0_raw")
+        place(out_1, 0, 3, banks[5], dom0_mx, pw0_mx, p1[:, 3, :], windows[3])
+        do0_mx = quantize(cast_by_query(do0_raw, "do0_grouped"), E5M2, "do0")
+        shift0 = held.tile([P, PACK], F32, name="shift0")
+        for t in range(PACK):
+            nc.scalar.activation(shift0[:, t : t + 1], delta_sb[:, 0, t : t + 1], ACT.Copy, scale=neg_rw0[:, t : t + 1])
+        neg_delta1 = held.tile([P, PACK], F32, name="neg_delta1")
+        nc.scalar.mul(neg_delta1[:], delta_sb[:, 1, :], -1.0)
+        half_columns(dom1_mx, dom1_raw, halves[1], "dom1_high")
+        place(out_1, 1, 0, banks[0], dom1_mx, pw1_mx, p1[:, 0, :], windows[0])
+        place(out_1, 1, 1, banks[1], dom1_mx, pw1_mx, p1[:, 1, :], windows[1])
+        ds0 = held.tile([P, PACK, N], F32, name="ds0", tag="dom1_high", align_bytes=64)
+        for t in range(PACK):
+            product(banks[4 + t], do0_mx, t, v0_mx)
+            nc.scalar.activation(
+                q0_raw[:, t, :], banks[4 + t][:], ACT.Identity, bias=shift0[:, t : t + 1], scale=rw_sb[:, 0, t : t + 1]
+            )
+            nc.gpsimd.tensor_tensor(ds0[:, t, :], q0_raw[:, t, :], p0[:, t, :], ALU.mult)
+        place(out_1, 1, 2, banks[4], dom1_mx, pw1_mx, p1[:, 2, :], windows[2])
+        qm0_mx = quantize(cast_plain(qm0_raw), E4M3, "qm0")
+        do1 = new_grouped()
+        cast_by_query_rows(do1, do1_raw, slice(0, P // 4))
+        ds0_mx = quantize(cast_plain(ds0), E5M2, "ds0")
+        place(out_1, 1, 3, banks[5], dom1_mx, pw1_mx, q0_raw[:, 3, :], windows[3])
+        do1_rest = slice(P // 4, P)
+        cast_by_query_rows(do1, do1_raw, do1_rest)
         do1_mx = quantize(do1, E5M2, "do1")
-        place(out_1, 1, 0, banks[0], dom1_mx, pw1_mx, do1_raw[:, 0, :], dv_windows[0])
-        place(out_1, 1, 1, banks[1], dom1_mx, pw1_mx, do1_raw[:, 1, :], dv_windows[1])
-        neg_delta1 = held.tile([P, PACK], F32, name="neg_delta1", tag="dom0_codes", align_bytes=64)
-        nc.scalar.activation(neg_delta1[:], delta_sb[:, 1, :], ACT.Copy, scale=minus_one[:])
-        qm1_mx = quantize(cast_plain(qm1_raw, "pw1_grouped"), E4M3, "qm1")
-        ds1 = q1_raw
+        qm1_mx = quantize(cast_plain(qm1_raw, "p0"), E4M3, "qm1")
+        place(out_0, 0, 0, banks[0], qm0_mx, ds0_mx, q0_raw[:, 0, :], windows[0])
+        place(out_0, 0, 1, banks[1], qm0_mx, ds0_mx, q0_raw[:, 1, :], windows[1])
+        place(out_0, 0, 2, banks[2], qm0_mx, ds0_mx, q0_raw[:, 2, :], windows[2])
+        ds1 = held.tile([P, PACK, N], F32, name="ds1", tag="p0", align_bytes=64)
+        shifted1 = qm0_raw
         for t in range(PACK):
             product(banks[4 + t], do1_mx, t, v1_mx)
-            nc.scalar.activation(dom1_raw[:, t, :], banks[4 + t][:], ACT.Identity, bias=neg_delta1[:, t : t + 1])
-            nc.gpsimd.tensor_tensor(ds1[:, t, :], dom1_raw[:, t, :], pw1_planes[t], ALU.mult)
-        place(out_1, 1, 2, banks[7], dom1_mx, pw1_mx, do1_raw[:, 2, :], dv_windows[2])
+            nc.scalar.activation(shifted1[:, t, :], banks[4 + t][:], ACT.Identity, bias=neg_delta1[:, t : t + 1])
+            nc.gpsimd.tensor_tensor(ds1[:, t, :], shifted1[:, t, :], pw1[:, t, :], ALU.mult)
         ds1_mx = quantize(cast_plain(ds1), E5M2, "ds1")
-        place(out_1, 1, 3, banks[1], dom1_mx, pw1_mx, ds1[:, 3, :], dv_windows[3])
+        place(out_0, 0, 3, banks[3], qm0_mx, ds0_mx, shifted1[:, 3, :], windows[3])
         for c in range(4):
-            place(out_0, 1, c, banks[c], qm1_mx, ds1_mx, qm1_raw[:, c, :], dk_windows[c])
+            place(out_0, 1, c, banks[4 + c], qm1_mx, ds1_mx, qm1_raw[:, c, :], windows[c])

@@ -157,15 +157,12 @@ def tile_attend_gat_lse_kv_kernel(
                     in_=rest[:, PACK * (cols.start - P) : PACK * (cols.stop - P)],
                 )
 
-        def cast_by_query_rows(grouped, raw, rows):
-            nc.scalar.copy(
-                grouped[:].rearrange("p (t m j) -> p m j t", t=PACK, j=PACK)[:, rows],
-                raw[:].rearrange("p j (m t) -> p m j t", t=PACK)[:, rows],
-            )
-
         def cast_by_query(raw, tag=None):
             grouped = new_grouped(tag)
-            cast_by_query_rows(grouped, raw, slice(0, P))
+            nc.scalar.copy(
+                grouped[:].rearrange("p (t m j) -> p m j t", t=PACK, j=PACK),
+                raw[:].rearrange("p j (m t) -> p m j t", t=PACK),
+            )
             return grouped
 
         def product(bank, stationary, c, moving, slots=slice(0, N)):
@@ -185,10 +182,23 @@ def tile_attend_gat_lse_kv_kernel(
             nc.scalar.copy(interleaved(half), by_fours(raw)[:, cols.start // 4 : cols.stop // 4])
             quantize_half(mx, half, cols)
 
+        def as_grouped(planes):
+            return planes.rearrange("p t w -> p (t w)").bitcast(BF16)
+
+        def half_into(mx, raw, cols, plane):
+            half = as_grouped(plane)
+            nc.scalar.copy(half.rearrange("p (c i t) -> p c t i", i=4, t=PACK), by_fours(raw)[:, cols.start // 4 : cols.stop // 4])
+            nc.vector.quantize_mx(out=mx[0][:, cols].bitcast(mx[2]), scales=mx[1][:, cols], in_=half)
+
         def scatter(b, bank, staged, window, slots=slice(0, N)):
             entries = slice((b * N + slots.start) // 16, (b * N + slots.stop) // 16)
             nc.scalar.copy(staged[:, slots], bank[:, slots])
             nc.vector.tensor_copy(window[:].indirect(offsets[:, entries]), staged[:, slots])
+
+        def scatter_from(b, bank, staged, window, slots):
+            entries = slice((b * N + slots.start) // 16, (b * N + slots.stop) // 16)
+            nc.scalar.copy(staged, bank[:, slots])
+            nc.vector.tensor_copy(window[:].indirect(offsets[:, entries]), staged)
 
         def place(out, b, c, bank, stationary, moving, staged, window):
             product(bank, stationary, c, moving)
@@ -254,7 +264,6 @@ def tile_attend_gat_lse_kv_kernel(
         nc.scalar.mul(neg_delta1[:], delta_sb[:, 1, :], -1.0)
         half_columns(dom1_mx, dom1_raw, halves[1], "dom1_high")
         place(out_1, 1, 0, banks[0], dom1_mx, pw1_mx, p1[:, 0, :], windows[0])
-        place(out_1, 1, 1, banks[1], dom1_mx, pw1_mx, p1[:, 1, :], windows[1])
         ds0 = held.tile([P, PACK, N], F32, name="ds0", tag="dom1_high", align_bytes=64)
         for t in range(PACK):
             product(banks[4 + t], do0_mx, t, v0_mx)
@@ -262,26 +271,45 @@ def tile_attend_gat_lse_kv_kernel(
                 q0_raw[:, t, :], banks[4 + t][:], ACT.Identity, bias=shift0[:, t : t + 1], scale=rw_sb[:, 0, t : t + 1]
             )
             nc.gpsimd.tensor_tensor(ds0[:, t, :], q0_raw[:, t, :], p0[:, t, :], ALU.mult)
+            if t == 1:
+                place(out_1, 1, 1, banks[1], dom1_mx, pw1_mx, p1[:, 1, :], windows[1])
         place(out_1, 1, 2, banks[4], dom1_mx, pw1_mx, p1[:, 2, :], windows[2])
-        qm0_mx = quantize(cast_plain(qm0_raw), E4M3, "qm0")
-        do1 = new_grouped()
-        cast_by_query_rows(do1, do1_raw, slice(0, P // 4))
-        ds0_mx = quantize(cast_plain(ds0), E5M2, "ds0")
-        place(out_1, 1, 3, banks[5], dom1_mx, pw1_mx, q0_raw[:, 3, :], windows[3])
-        do1_rest = slice(P // 4, P)
-        cast_by_query_rows(do1, do1_raw, do1_rest)
-        do1_mx = quantize(do1, E5M2, "do1")
-        qm1_mx = quantize(cast_plain(qm1_raw, "p0"), E4M3, "qm1")
-        place(out_0, 0, 0, banks[0], qm0_mx, ds0_mx, q0_raw[:, 0, :], windows[0])
-        place(out_0, 0, 1, banks[1], qm0_mx, ds0_mx, q0_raw[:, 1, :], windows[1])
-        place(out_0, 0, 2, banks[2], qm0_mx, ds0_mx, q0_raw[:, 2, :], windows[2])
+        ds0_grouped = new_grouped()
+        for slots in halves:
+            cast_plain_cols(ds0_grouped, ds0, slots)
+        ds0_mx = quantize(ds0_grouped, E5M2, "ds0")
+        product(banks[5], dom1_mx, 3, pw1_mx)
+        scatter(1, banks[5], ds0[:, 3, :], windows[3], halves[0])
+        qm0 = as_grouped(ds0[:, :2, :])
+        for part in (slice(0, 96), slice(96, P)):
+            nc.scalar.copy(qm0.rearrange("p (c i t) -> p c t i", i=4, t=PACK)[:, part], by_fours(qm0_raw)[:, part])
+        qm0_mx = new_mx("qm0", E4M3)
+        quantize_cols(qm0_mx, qm0, slice(0, 512))
+        scatter_from(1, banks[5], qm0_raw[:, 3, halves[0]], windows[3], halves[1])
+        nc.sync.dma_start(out=out_1[3 * P :, :], in_=windows[3][:])
+        do1 = as_grouped(qm0_raw[:, :2, :])
+        nc.scalar.copy(
+            do1.rearrange("p (t m j) -> p m j t", t=PACK, j=PACK), do1_raw[:].rearrange("p j (m t) -> p m j t", t=PACK)
+        )
+        do1_mx = new_mx("do1", E5M2)
+        quantize_cols(do1_mx, do1, slice(0, 512))
+        for c in range(3):
+            place(out_0, 0, c, banks[c], qm0_mx, ds0_mx, q0_raw[:, c, :], windows[c])
+        product(banks[3], qm0_mx, 3, ds0_mx)
+        qm1_mx = new_mx("qm1", E4M3)
+        half_into(qm1_mx, qm1_raw, halves[0], do1_raw[:, 3:, :])
+        scatter(0, banks[3], qm1_raw[:, 3, :], windows[3], halves[0])
         ds1 = held.tile([P, PACK, N], F32, name="ds1", tag="p0", align_bytes=64)
         shifted1 = qm0_raw
         for t in range(PACK):
             product(banks[4 + t], do1_mx, t, v1_mx)
             nc.scalar.activation(shifted1[:, t, :], banks[4 + t][:], ACT.Identity, bias=neg_delta1[:, t : t + 1])
             nc.gpsimd.tensor_tensor(ds1[:, t, :], shifted1[:, t, :], pw1[:, t, :], ALU.mult)
-        ds1_mx = quantize(cast_plain(ds1), E5M2, "ds1")
-        place(out_0, 0, 3, banks[3], qm0_mx, ds0_mx, shifted1[:, 3, :], windows[3])
+        ds1_grouped = new_grouped()
+        for slots in halves:
+            cast_plain_cols(ds1_grouped, ds1, slots)
+        ds1_mx = quantize(ds1_grouped, E5M2, "ds1")
+        scatter_from(0, banks[3], ds1[:, 3, halves[0]], windows[3], halves[1])
+        half_into(qm1_mx, qm1_raw, halves[1], ds1[:, :1, :])
         for c in range(4):
-            place(out_0, 1, c, banks[4 + c], qm1_mx, ds1_mx, qm1_raw[:, c, :], windows[c])
+            place(out_0, 1, c, banks[4 + c], qm1_mx, ds1_mx, shifted1[:, c, :], windows[c])

@@ -182,11 +182,8 @@ def tile_attend_gat_lse_kv_kernel(
             nc.scalar.copy(interleaved(half), by_fours(raw)[:, cols.start // 4 : cols.stop // 4])
             quantize_half(mx, half, cols)
 
-        def as_grouped(planes):
-            return planes.rearrange("p t w -> p (t w)").bitcast(BF16)
-
         def half_into(mx, raw, cols, plane):
-            half = as_grouped(plane)
+            half = plane.rearrange("p t w -> p (t w)").bitcast(BF16)
             nc.scalar.copy(half.rearrange("p (c i t) -> p c t i", i=4, t=PACK), by_fours(raw)[:, cols.start // 4 : cols.stop // 4])
             nc.vector.quantize_mx(out=mx[0][:, cols].bitcast(mx[2]), scales=mx[1][:, cols], in_=half)
 
@@ -274,37 +271,31 @@ def tile_attend_gat_lse_kv_kernel(
             if t == 1:
                 place(out_1, 1, 1, banks[1], dom1_mx, pw1_mx, p1[:, 1, :], windows[1])
         place(out_1, 1, 2, banks[4], dom1_mx, pw1_mx, p1[:, 2, :], windows[2])
-        ds0_grouped = new_grouped()
+        qm0_mx = quantize(cast_plain(qm0_raw), E4M3, "qm0")
+        product(banks[5], dom1_mx, 3, pw1_mx)
+        scatter(1, banks[5], p1[:, 3, :], windows[3], halves[0])
+        do1 = cast_by_query(do1_raw)
+        ds0_grouped = new_grouped("ds0_grouped")
         for slots in halves:
             cast_plain_cols(ds0_grouped, ds0, slots)
         ds0_mx = quantize(ds0_grouped, E5M2, "ds0")
-        product(banks[5], dom1_mx, 3, pw1_mx)
-        scatter(1, banks[5], ds0[:, 3, :], windows[3], halves[0])
-        qm0 = as_grouped(ds0[:, :2, :])
-        for part in (slice(0, 96), slice(96, P)):
-            nc.scalar.copy(qm0.rearrange("p (c i t) -> p c t i", i=4, t=PACK)[:, part], by_fours(qm0_raw)[:, part])
-        qm0_mx = new_mx("qm0", E4M3)
-        quantize_cols(qm0_mx, qm0, slice(0, 512))
-        scatter_from(1, banks[5], qm0_raw[:, 3, halves[0]], windows[3], halves[1])
+        scatter_from(1, banks[5], ds0[:, 3, halves[0]], windows[3], halves[1])
         nc.sync.dma_start(out=out_1[3 * P :, :], in_=windows[3][:])
-        do1 = as_grouped(qm0_raw[:, :2, :])
-        nc.scalar.copy(
-            do1.rearrange("p (t m j) -> p m j t", t=PACK, j=PACK), do1_raw[:].rearrange("p j (m t) -> p m j t", t=PACK)
-        )
-        do1_mx = new_mx("do1", E5M2)
-        quantize_cols(do1_mx, do1, slice(0, 512))
-        for c in range(3):
-            place(out_0, 0, c, banks[c], qm0_mx, ds0_mx, q0_raw[:, c, :], windows[c])
-        product(banks[3], qm0_mx, 3, ds0_mx)
+        do1_mx = quantize(do1, E5M2, "do1", "ds0_grouped")
         qm1_mx = new_mx("qm1", E4M3)
-        half_into(qm1_mx, qm1_raw, halves[0], do1_raw[:, 3:, :])
-        scatter(0, banks[3], qm1_raw[:, 3, :], windows[3], halves[0])
-        ds1 = held.tile([P, PACK, N], F32, name="ds1", tag="p0", align_bytes=64)
+        half_into(qm1_mx, qm1_raw, halves[0], ds0[:, :1, :])
+        place(out_0, 0, 0, banks[0], qm0_mx, ds0_mx, do1_raw[:, 0, :], windows[0])
+        ds1 = held.tile([P, PACK, N], F32, name="ds1", tag="dom1_high", align_bytes=64)
         shifted1 = qm0_raw
         for t in range(PACK):
             product(banks[4 + t], do1_mx, t, v1_mx)
             nc.scalar.activation(shifted1[:, t, :], banks[4 + t][:], ACT.Identity, bias=neg_delta1[:, t : t + 1])
             nc.gpsimd.tensor_tensor(ds1[:, t, :], shifted1[:, t, :], pw1[:, t, :], ALU.mult)
+            if t == 1:
+                place(out_0, 0, 1, banks[1], qm0_mx, ds0_mx, do1_raw[:, 1, :], windows[1])
+        place(out_0, 0, 2, banks[2], qm0_mx, ds0_mx, do1_raw[:, 2, :], windows[2])
+        product(banks[3], qm0_mx, 3, ds0_mx)
+        scatter(0, banks[3], do1_raw[:, 3, :], windows[3], halves[0])
         ds1_grouped = new_grouped()
         for slots in halves:
             cast_plain_cols(ds1_grouped, ds1, slots)

@@ -182,20 +182,10 @@ def tile_attend_gat_lse_kv_kernel(
             nc.scalar.copy(interleaved(half), by_fours(raw)[:, cols.start // 4 : cols.stop // 4])
             quantize_half(mx, half, cols)
 
-        def half_into(mx, raw, cols, plane):
-            half = plane.rearrange("p t w -> p (t w)").bitcast(BF16)
-            nc.scalar.copy(half.rearrange("p (c i t) -> p c t i", i=4, t=PACK), by_fours(raw)[:, cols.start // 4 : cols.stop // 4])
-            nc.vector.quantize_mx(out=mx[0][:, cols].bitcast(mx[2]), scales=mx[1][:, cols], in_=half)
-
         def scatter(b, bank, staged, window, slots=slice(0, N)):
             entries = slice((b * N + slots.start) // 16, (b * N + slots.stop) // 16)
             nc.scalar.copy(staged[:, slots], bank[:, slots])
             nc.vector.tensor_copy(window[:].indirect(offsets[:, entries]), staged[:, slots])
-
-        def scatter_from(b, bank, staged, window, slots):
-            entries = slice((b * N + slots.start) // 16, (b * N + slots.stop) // 16)
-            nc.scalar.copy(staged, bank[:, slots])
-            nc.vector.tensor_copy(window[:].indirect(offsets[:, entries]), staged)
 
         def place(out, b, c, bank, stationary, moving, staged, window):
             product(bank, stationary, c, moving)
@@ -254,13 +244,13 @@ def tile_attend_gat_lse_kv_kernel(
         half_columns(dom1_mx, dom1_raw, halves[0], "dom0_raw")
         place(out_1, 0, 3, banks[5], dom0_mx, pw0_mx, p1[:, 3, :], windows[3])
         do0_mx = quantize(cast_by_query(do0_raw, "do0_grouped"), E5M2, "do0")
+        half_columns(dom1_mx, dom1_raw, halves[1], "dom1_high")
+        place(out_1, 1, 0, banks[0], dom1_mx, pw1_mx, p1[:, 0, :], windows[0])
         shift0 = held.tile([P, PACK], F32, name="shift0")
         for t in range(PACK):
             nc.scalar.activation(shift0[:, t : t + 1], delta_sb[:, 0, t : t + 1], ACT.Copy, scale=neg_rw0[:, t : t + 1])
         neg_delta1 = held.tile([P, PACK], F32, name="neg_delta1")
         nc.scalar.mul(neg_delta1[:], delta_sb[:, 1, :], -1.0)
-        half_columns(dom1_mx, dom1_raw, halves[1], "dom1_high")
-        place(out_1, 1, 0, banks[0], dom1_mx, pw1_mx, p1[:, 0, :], windows[0])
         ds0 = held.tile([P, PACK, N], F32, name="ds0", tag="dom1_high", align_bytes=64)
         for t in range(PACK):
             product(banks[4 + t], do0_mx, t, v0_mx)
@@ -272,35 +262,21 @@ def tile_attend_gat_lse_kv_kernel(
                 place(out_1, 1, 1, banks[1], dom1_mx, pw1_mx, p1[:, 1, :], windows[1])
         place(out_1, 1, 2, banks[4], dom1_mx, pw1_mx, p1[:, 2, :], windows[2])
         qm0_mx = quantize(cast_plain(qm0_raw), E4M3, "qm0")
-        product(banks[5], dom1_mx, 3, pw1_mx)
-        scatter(1, banks[5], p1[:, 3, :], windows[3], halves[0])
-        do1 = cast_by_query(do1_raw)
-        ds0_grouped = new_grouped("ds0_grouped")
-        for slots in halves:
-            cast_plain_cols(ds0_grouped, ds0, slots)
-        ds0_mx = quantize(ds0_grouped, E5M2, "ds0")
-        scatter_from(1, banks[5], ds0[:, 3, halves[0]], windows[3], halves[1])
-        nc.sync.dma_start(out=out_1[3 * P :, :], in_=windows[3][:])
-        do1_mx = quantize(do1, E5M2, "do1", "ds0_grouped")
-        qm1_mx = new_mx("qm1", E4M3)
-        half_into(qm1_mx, qm1_raw, halves[0], ds0[:, :1, :])
-        place(out_0, 0, 0, banks[0], qm0_mx, ds0_mx, do1_raw[:, 0, :], windows[0])
-        ds1 = held.tile([P, PACK, N], F32, name="ds1", tag="dom1_high", align_bytes=64)
-        shifted1 = qm0_raw
+        do1_mx = quantize(cast_by_query(do1_raw), E5M2, "do1")
+        ds0_mx = quantize(cast_plain(ds0, "ds0_grouped"), E5M2, "ds0")
+        place(out_1, 1, 3, banks[5], dom1_mx, pw1_mx, q0_raw[:, 3, :], windows[3])
+        ds1 = held.tile([P, PACK, N], F32, name="ds1", tag="p0", align_bytes=64)
+        shifted1 = ds0
         for t in range(PACK):
             product(banks[4 + t], do1_mx, t, v1_mx)
             nc.scalar.activation(shifted1[:, t, :], banks[4 + t][:], ACT.Identity, bias=neg_delta1[:, t : t + 1])
             nc.gpsimd.tensor_tensor(ds1[:, t, :], shifted1[:, t, :], pw1[:, t, :], ALU.mult)
             if t == 1:
-                place(out_0, 0, 1, banks[1], qm0_mx, ds0_mx, do1_raw[:, 1, :], windows[1])
+                place(out_0, 0, 0, banks[0], qm0_mx, ds0_mx, do1_raw[:, 0, :], windows[0])
+        place(out_0, 0, 1, banks[1], qm0_mx, ds0_mx, do1_raw[:, 1, :], windows[1])
         place(out_0, 0, 2, banks[2], qm0_mx, ds0_mx, do1_raw[:, 2, :], windows[2])
-        product(banks[3], qm0_mx, 3, ds0_mx)
-        scatter(0, banks[3], do1_raw[:, 3, :], windows[3], halves[0])
-        ds1_grouped = new_grouped()
-        for slots in halves:
-            cast_plain_cols(ds1_grouped, ds1, slots)
-        ds1_mx = quantize(ds1_grouped, E5M2, "ds1")
-        scatter_from(0, banks[3], ds1[:, 3, halves[0]], windows[3], halves[1])
-        half_into(qm1_mx, qm1_raw, halves[1], ds1[:, :1, :])
+        qm1_mx = quantize(cast_plain(qm1_raw, "ds0_grouped"), E4M3, "qm1")
+        ds1_mx = quantize(cast_plain(ds1), E5M2, "ds1")
+        place(out_0, 0, 3, banks[3], qm0_mx, ds0_mx, shifted1[:, 3, :], windows[3])
         for c in range(4):
-            place(out_0, 1, c, banks[4 + c], qm1_mx, ds1_mx, shifted1[:, c, :], windows[c])
+            place(out_0, 1, c, banks[4 + c], qm1_mx, ds1_mx, qm1_raw[:, c, :], windows[c])

@@ -147,15 +147,10 @@ def tile_attend_gat_lse_kv_kernel(
             nc.scalar.copy(interleaved(first), by_fours(raw)[:, : P // 4])
             quantize_half(mx, first, slice(0, P))
 
-        def other_columns(mx, raw, name, tag=None):
-            rest = held.tile([P, 3 * P * PACK], BF16, name=name, tag=tag or name, align_bytes=64)
-            nc.scalar.copy(interleaved(rest), by_fours(raw)[:, P // 4 :])
-            for cols in (slice(P, 2 * P), slice(2 * P, 4 * P)):
-                nc.vector.quantize_mx(
-                    out=mx[0][:, cols].bitcast(mx[2]),
-                    scales=mx[1][:, cols],
-                    in_=rest[:, PACK * (cols.start - P) : PACK * (cols.stop - P)],
-                )
+        def some_columns(mx, raw, cols, name):
+            part = held.tile([P, P * PACK], BF16, name=name, align_bytes=64)
+            nc.scalar.copy(interleaved(part), by_fours(raw)[:, cols.start // 4 : cols.stop // 4])
+            quantize_half(mx, part, cols)
 
         def cast_by_query(raw, tag=None):
             grouped = new_grouped(tag)
@@ -219,15 +214,17 @@ def tile_attend_gat_lse_kv_kernel(
         dom0_mx = new_mx("dom0", E5M2)
         first_columns(dom0_mx, dom0_raw, "dom0_first")
         pw0_mx = quantize(pw0, E4M3, "pw0")
-        other_columns(dom0_mx, dom0_raw, "dom0_rest")
+        some_columns(dom0_mx, dom0_raw, slice(P, 2 * P), "dom0_second")
         v_picked_words = gather_all(v_pool_words, U32, "v_codes")
         v0_mx = v_picked_words[0], v_picked_scales[0], E4M3
         v1_mx = v_picked_words[1], v_picked_scales[1], E4M3
 
         q1_mx = quantize(cast_by_query(q1_raw), E4M3, "q1")
         place(out_1, 0, 0, banks[0], dom0_mx, pw0_mx, q1_raw[:, 0, :], windows[0])
+        dom0_high = q1_raw[:, 3, :].bitcast(BF16)
+        nc.scalar.copy(dom0_high.rearrange("p (c i t) -> p c t i", i=4, t=PACK), by_fours(dom0_raw)[:, 64:])
+        nc.vector.quantize_mx(out=dom0_mx[0][:, halves[1]].bitcast(E5M2), scales=dom0_mx[1][:, halves[1]], in_=dom0_high)
         place(out_1, 0, 1, banks[1], dom0_mx, pw0_mx, q1_raw[:, 1, :], windows[1])
-        place(out_1, 0, 2, banks[2], dom0_mx, pw0_mx, q1_raw[:, 2, :], windows[2])
         p1 = held.tile([P, PACK, N], F32, name="p1", tag="k_pool_words", align_bytes=64)
         for t in range(PACK):
             product(banks[4 + t], q1_mx, t, k1_mx)
@@ -236,6 +233,8 @@ def tile_attend_gat_lse_kv_kernel(
         for slots in halves:
             for t in range(PACK):
                 nc.scalar.activation(pw1[:, t, slots], p1[:, t, slots], ACT.Copy, scale=rw_sb[:, 1, t : t + 1])
+            if slots == halves[0]:
+                place(out_1, 0, 2, banks[2], dom0_mx, pw0_mx, q1_raw[:, 2, :], windows[2])
         pw1_grouped = new_grouped()
         for slots in halves:
             cast_plain_cols(pw1_grouped, pw1, slots)
@@ -251,6 +250,9 @@ def tile_attend_gat_lse_kv_kernel(
             nc.scalar.activation(shift0[:, t : t + 1], delta_sb[:, 0, t : t + 1], ACT.Copy, scale=neg_rw0[:, t : t + 1])
         neg_delta1 = held.tile([P, PACK], F32, name="neg_delta1")
         nc.scalar.mul(neg_delta1[:], delta_sb[:, 1, :], -1.0)
+        place(out_1, 1, 1, banks[1], dom1_mx, pw1_mx, p1[:, 1, :], windows[1])
+        qm0 = new_grouped()
+        cast_plain_cols(qm0, qm0_raw, slice(0, P))
         ds0 = held.tile([P, PACK, N], F32, name="ds0", tag="dom1_high", align_bytes=64)
         for t in range(PACK):
             product(banks[4 + t], do0_mx, t, v0_mx)
@@ -258,22 +260,21 @@ def tile_attend_gat_lse_kv_kernel(
                 q0_raw[:, t, :], banks[4 + t][:], ACT.Identity, bias=shift0[:, t : t + 1], scale=rw_sb[:, 0, t : t + 1]
             )
             nc.gpsimd.tensor_tensor(ds0[:, t, :], q0_raw[:, t, :], p0[:, t, :], ALU.mult)
-            if t == 1:
-                place(out_1, 1, 1, banks[1], dom1_mx, pw1_mx, p1[:, 1, :], windows[1])
         place(out_1, 1, 2, banks[4], dom1_mx, pw1_mx, p1[:, 2, :], windows[2])
-        qm0_mx = quantize(cast_plain(qm0_raw), E4M3, "qm0")
+        cast_plain_cols(qm0, qm0_raw, slice(P, 4 * P))
+        qm0_mx = quantize(qm0, E4M3, "qm0")
         do1_mx = quantize(cast_by_query(do1_raw), E5M2, "do1")
         ds0_mx = quantize(cast_plain(ds0, "ds0_grouped"), E5M2, "ds0")
         place(out_1, 1, 3, banks[5], dom1_mx, pw1_mx, q0_raw[:, 3, :], windows[3])
         ds1 = held.tile([P, PACK, N], F32, name="ds1", tag="p0", align_bytes=64)
         shifted1 = ds0
         for t in range(PACK):
-            product(banks[4 + t], do1_mx, t, v1_mx)
-            nc.scalar.activation(shifted1[:, t, :], banks[4 + t][:], ACT.Identity, bias=neg_delta1[:, t : t + 1])
+            bank = banks[(4, 6, 0, 1)[t]]
+            if t >= 2:
+                place(out_0, 0, t - 2, bank, qm0_mx, ds0_mx, do1_raw[:, t - 2, :], windows[t - 2])
+            product(bank, do1_mx, t, v1_mx)
+            nc.scalar.activation(shifted1[:, t, :], bank[:], ACT.Identity, bias=neg_delta1[:, t : t + 1])
             nc.gpsimd.tensor_tensor(ds1[:, t, :], shifted1[:, t, :], pw1[:, t, :], ALU.mult)
-            if t == 1:
-                place(out_0, 0, 0, banks[0], qm0_mx, ds0_mx, do1_raw[:, 0, :], windows[0])
-        place(out_0, 0, 1, banks[1], qm0_mx, ds0_mx, do1_raw[:, 1, :], windows[1])
         place(out_0, 0, 2, banks[2], qm0_mx, ds0_mx, do1_raw[:, 2, :], windows[2])
         qm1_mx = quantize(cast_plain(qm1_raw, "ds0_grouped"), E4M3, "qm1")
         ds1_mx = quantize(cast_plain(ds1), E5M2, "ds1")

@@ -199,7 +199,6 @@ def tile_attend_gat_lse_kv_kernel(
             part = held.tile([P, 256 * PACK], BF16, name=f"q0_part{h}", align_bytes=64)
             copy(part[:].rearrange("p (t m j) -> p m j t", t=2, j=PACK), q0_rows[:, :, :, 2 * h : 2 * h + 2])
             quantize_half(q0_mx, part, halves[h])
-        windows.append(new_window("window3", clear=nc.gpsimd, tag="q0_part0"))
         v_picked_scales = gather_all(v_pool_scales, U8, "v_scales")
         p0 = held.tile([P, PACK, N], F32, name="p0", align_bytes=64)
         pw0 = new_grouped()
@@ -213,13 +212,14 @@ def tile_attend_gat_lse_kv_kernel(
             nc.vector.tensor_tensor(interleaved(pw0)[:, fours], by_fours(p0)[:, fours], gate, ALU.mult)
         dom0_mx = new_mx("dom0", E5M2)
         first_columns(dom0_mx, dom0_raw, "dom0_first")
-        pw0_mx = quantize(pw0, E4M3, "pw0")
         some_columns(dom0_mx, dom0_raw, slice(P, 2 * P), "dom0_second")
+        pw0_mx = quantize(pw0, E4M3, "pw0")
         v_picked_words = gather_all(v_pool_words, U32, "v_codes")
         v0_mx = v_picked_words[0], v_picked_scales[0], E4M3
         v1_mx = v_picked_words[1], v_picked_scales[1], E4M3
 
-        q1_mx = quantize(cast_by_query(q1_raw), E4M3, "q1")
+        q1_mx = quantize(cast_by_query(q1_raw, "q1_grouped"), E4M3, "q1")
+        windows.append(new_window("window3", clear=nc.gpsimd, tag="q1_grouped"))
         place(out_1, 0, 0, banks[0], dom0_mx, pw0_mx, q1_raw[:, 0, :], windows[0])
         dom0_high = q1_raw[:, 3, :].bitcast(BF16)
         nc.scalar.copy(dom0_high.rearrange("p (c i t) -> p c t i", i=4, t=PACK), by_fours(dom0_raw)[:, 64:])

@@ -60,37 +60,33 @@ def tile_attend_gat_lse_kv_kernel(
 
         halves = (slice(0, 256), slice(256, 512))
         lse_sb = load_per_query(lse, "lse_sb")
-        rw_sb = load_per_query(rw, "rw_sb")
         k_pool_scales, v_pool_scales = new_scales("k_pool_scales"), new_scales("v_pool_scales")
         load_scales(k_pool_scales, k_scales, range(4))
         k_pool_words = held.tile([P, T], U32, name="k_pool_words", align_bytes=64)
         v_pool_words = held.tile([P, T], U32, name="v_pool_words", align_bytes=64)
-        load_words(k_pool_words, k_words, slice(0, T))
         q0_raw = load_rows(qT[0], "q0_raw")
+        load_words(k_pool_words, k_words, slice(0, T))
+        rw_sb = load_per_query(rw, "rw_sb")
         load_scales(v_pool_scales, v_scales, range(4))
-        dom0_raw = load_rows(dom[0], "dom0_raw")
-        load_words(v_pool_words, v_words, slice(0, T // 2))
         q1_raw = load_rows(qT[1], "q1_raw")
-        load_words(v_pool_words, v_words, slice(T // 2, T))
+        dom0_raw = load_rows(dom[0], "dom0_raw")
         dom1_raw = load_rows(dom[1], "dom1_raw")
+        load_words(v_pool_words, v_words, slice(0, T))
         do0_raw = load_rows(doT[0], "do0_raw")
         delta_sb = load_per_query(delta, "delta_sb")
-        qm0_raw = load_rows(qm[0], "qm0_raw")
         do1_raw = load_rows(doT[1], "do1_raw")
+        qm0_raw = load_rows(qm[0], "qm0_raw")
         qm1_raw = load_rows(qm[1], "qm1_raw")
 
         neg_lse = held.tile([P, B, PACK], F32, name="neg_lse")
         nc.scalar.mul(neg_lse[:], lse_sb[:], -1.0)
-        neg_rw0 = held.tile([P, PACK], F32, name="neg_rw0")
-        nc.scalar.mul(neg_rw0[:], rw_sb[:, 0, :], -1.0)
 
         def new_window(name, clear=nc.vector, tag=None):
             window = held.tile([P, T], F32, name=name, tag=tag or name, align_bytes=64)
             clear.memset(window[:].bitcast(I32), 0)
             return window
 
-        windows = [new_window(f"window{c}") for c in range(2)]
-        windows.append(new_window("window2", clear=nc.gpsimd, tag="lse_sb"))
+        windows = [new_window(f"window{c}") for c in range(3)]
 
         def gather(pool_tile, b, dtype, name, tag=None, parts=1):
             picked = held.tile([P, N], dtype, name=name, tag=tag or name, align_bytes=64)
@@ -177,107 +173,135 @@ def tile_attend_gat_lse_kv_kernel(
             nc.scalar.copy(interleaved(half), by_fours(raw)[:, cols.start // 4 : cols.stop // 4])
             quantize_half(mx, half, cols)
 
-        def scatter(b, bank, staged, window, slots=slice(0, N)):
-            entries = slice((b * N + slots.start) // 16, (b * N + slots.stop) // 16)
-            nc.scalar.copy(staged[:, slots], bank[:, slots])
-            nc.vector.tensor_copy(window[:].indirect(offsets[:, entries]), staged[:, slots])
+        def vector_cast(grouped, raw, cols=slice(0, 512)):
+            fours = slice(cols.start // 4, cols.stop // 4)
+            nc.vector.tensor_copy(interleaved(grouped), by_fours(raw)[:, fours])
+            return grouped
 
-        def place(out, b, c, bank, stationary, moving, staged, window):
-            product(bank, stationary, c, moving)
-            scatter(b, bank, staged, window)
-            if b == B - 1:
-                nc.sync.dma_start(out=out[c * P : (c + 1) * P, :], in_=window[:])
+        def vector_cast_by_query(grouped, raw):
+            nc.vector.tensor_copy(
+                grouped[:].rearrange("p (t m j) -> p m j t", t=PACK, j=PACK),
+                raw[:].rearrange("p j (m t) -> p m j t", t=PACK),
+            )
+            return grouped
+
+        def gated(grouped, planes, b, slots=slice(0, N)):
+            fours = slice(slots.start // 4, slots.stop // 4)
+            gate = rw_sb[:, b, :].unsqueeze(1).unsqueeze(3).broadcast_to([P, fours.stop - fours.start, PACK, 4])
+            nc.vector.tensor_tensor(interleaved(grouped)[:, fours], by_fours(planes)[:, fours], gate, ALU.mult)
+            return grouped
+
+        def listed(window, b, slots):
+            return window[:].indirect(offsets[:, (b * N + slots.start) // 16 : (b * N + slots.stop) // 16])
+
+        def scalar_scatter(window, b, staged):
+            for slots in halves:
+                nc.scalar.activation(listed(window, b, slots), staged[:, slots], ACT.Copy)
+
+        def vector_scatter(window, b, staged):
+            nc.vector.tensor_copy(listed(window, b, slice(0, N)), staged)
+
+        def store(out, c, window):
+            nc.sync.dma_start(out=out[c * P : (c + 1) * P, :], in_=window[:])
+
+        def centred(planes, do_mx, v_mx, probs, b):
+            for t in range(PACK):
+                product(banks[4 + t], do_mx, t, v_mx)
+                nc.vector.scalar_tensor_tensor(
+                    planes[:, t, :], banks[4 + t][:], delta_sb[:, b, t : t + 1], probs[:, t, :], ALU.subtract, ALU.mult
+                )
+
+        def gather_part(picked, pool_tile, entries):
+            nc.vector.tensor_copy(picked[:, entries], pool_tile[:].indirect(offsets[:, entries.start // 16 : entries.stop // 16]))
 
         k_picked_scales = gather_all(k_pool_scales, U8, "k_scales")
-        k_picked_words = gather_all(k_pool_words, U32, "k_codes")
-        k0_mx = k_picked_words[0], k_picked_scales[0], E4M3
-        k1_mx = k_picked_words[1], k_picked_scales[1], E4M3
-
+        windows.append(new_window("window3"))
+        k_codes = held.tile([P, B * N], U32, name="k_codes", align_bytes=64)
+        k0_mx = k_codes[:, :N], k_picked_scales[0], E4M3
+        k1_mx = k_codes[:, N:], k_picked_scales[1], E4M3
+        gather_part(k_codes, k_pool_words, halves[0])
         q0_mx = new_mx("q0", E4M3)
         q0_rows = q0_raw[:].rearrange("p j (m t) -> p m j t", t=PACK)
-        for h, copy in ((1, nc.vector.tensor_copy), (0, nc.scalar.copy)):
+        for h in range(2):
             part = held.tile([P, 256 * PACK], BF16, name=f"q0_part{h}", align_bytes=64)
-            copy(part[:].rearrange("p (t m j) -> p m j t", t=2, j=PACK), q0_rows[:, :, :, 2 * h : 2 * h + 2])
+            nc.scalar.copy(part[:].rearrange("p (t m j) -> p m j t", t=2, j=PACK), q0_rows[:, :, :, 2 * h : 2 * h + 2])
             quantize_half(q0_mx, part, halves[h])
-        v_picked_scales = gather_all(v_pool_scales, U8, "v_scales")
+        gather_part(k_codes, k_pool_words, halves[1])
+        gather_part(k_codes, k_pool_words, slice(N, 2 * N))
         p0 = held.tile([P, PACK, N], F32, name="p0", align_bytes=64)
-        pw0 = new_grouped()
-        gate = rw_sb[:, 0, :].unsqueeze(1).unsqueeze(3).broadcast_to([P, N // 8, PACK, 4])
+        v0_scales = gather(v_pool_scales, 0, U8, "v0_scales")
+        pw0 = new_grouped("pw0_grouped")
         for h, slots in enumerate(halves):
-            for t in ((2, 3, 0, 1), (0, 1, 2, 3))[h]:
-                bank = banks[t if t >= 2 else 4 * h + t]
+            for t in range(PACK):
+                bank = banks[4 * h + t]
                 product(bank, q0_mx, t, k0_mx, slots)
                 nc.scalar.activation(p0[:, t, slots], bank[:, slots], ACT.Exp, bias=neg_lse[:, 0, t : t + 1])
-            fours = slice(slots.start // 4, slots.stop // 4)
-            nc.vector.tensor_tensor(interleaved(pw0)[:, fours], by_fours(p0)[:, fours], gate, ALU.mult)
-        dom0_mx = new_mx("dom0", E5M2)
-        first_columns(dom0_mx, dom0_raw, "dom0_first")
-        some_columns(dom0_mx, dom0_raw, slice(P, 2 * P), "dom0_second")
-        pw0_mx = quantize(pw0, E4M3, "pw0")
-        v_picked_words = gather_all(v_pool_words, U32, "v_codes")
-        v0_mx = v_picked_words[0], v_picked_scales[0], E4M3
-        v1_mx = v_picked_words[1], v_picked_scales[1], E4M3
-
+            gated(pw0, p0, 0, slots)
         q1_mx = quantize(cast_by_query(q1_raw, "q1_grouped"), E4M3, "q1")
-        windows.append(new_window("window3", clear=nc.gpsimd, tag="q1_grouped"))
-        place(out_1, 0, 0, banks[0], dom0_mx, pw0_mx, q1_raw[:, 0, :], windows[0])
-        dom0_high = q1_raw[:, 3, :].bitcast(BF16)
-        nc.scalar.copy(dom0_high.rearrange("p (c i t) -> p c t i", i=4, t=PACK), by_fours(dom0_raw)[:, 64:])
-        nc.vector.quantize_mx(out=dom0_mx[0][:, halves[1]].bitcast(E5M2), scales=dom0_mx[1][:, halves[1]], in_=dom0_high)
-        place(out_1, 0, 1, banks[1], dom0_mx, pw0_mx, q1_raw[:, 1, :], windows[1])
+        pw0_mx = quantize(pw0, E4M3, "pw0", tag="q1_grouped")
+        v1_scales = gather(v_pool_scales, 1, U8, "v1_scales", tag="pw0_grouped")
+        dom1_grouped = held.tile([P, 512 * PACK], BF16, name="dom1_grouped", align_bytes=64)
+        dom0_mx = quantize(cast_plain(dom0_raw), E5M2, "dom0")
+        dom1_mx = quantize(vector_cast(dom1_grouped, dom1_raw), E5M2, "dom1")
+        windows.append(new_window("window4", clear=nc.gpsimd, tag="dom1_grouped"))
+
         p1 = held.tile([P, PACK, N], F32, name="p1", tag="k_pool_words", align_bytes=64)
         for t in range(PACK):
             product(banks[4 + t], q1_mx, t, k1_mx)
             nc.scalar.activation(p1[:, t, :], banks[4 + t][:], ACT.Exp, bias=neg_lse[:, 1, t : t + 1])
-        pw1 = held.tile([P, PACK, N], F32, name="pw1", tag="v_pool_words", align_bytes=64)
-        for slots in halves:
-            for t in range(PACK):
-                nc.scalar.activation(pw1[:, t, slots], p1[:, t, slots], ACT.Copy, scale=rw_sb[:, 1, t : t + 1])
-            if slots == halves[0]:
-                place(out_1, 0, 2, banks[2], dom0_mx, pw0_mx, q1_raw[:, 2, :], windows[2])
-        pw1_grouped = new_grouped()
-        for slots in halves:
-            cast_plain_cols(pw1_grouped, pw1, slots)
-        pw1_mx = quantize(pw1_grouped, E4M3, "pw1")
-        dom1_mx = new_mx("dom1", E5M2)
-        half_columns(dom1_mx, dom1_raw, halves[0], "dom0_raw")
-        place(out_1, 0, 3, banks[5], dom0_mx, pw0_mx, p1[:, 3, :], windows[3])
-        do0_mx = quantize(cast_by_query(do0_raw, "do0_grouped"), E5M2, "do0")
-        half_columns(dom1_mx, dom1_raw, halves[1], "dom1_high")
-        place(out_1, 1, 0, banks[0], dom1_mx, pw1_mx, p1[:, 0, :], windows[0])
-        shift0 = held.tile([P, PACK], F32, name="shift0")
-        for t in range(PACK):
-            nc.scalar.activation(shift0[:, t : t + 1], delta_sb[:, 0, t : t + 1], ACT.Copy, scale=neg_rw0[:, t : t + 1])
-        neg_delta1 = held.tile([P, PACK], F32, name="neg_delta1")
-        nc.scalar.mul(neg_delta1[:], delta_sb[:, 1, :], -1.0)
-        place(out_1, 1, 1, banks[1], dom1_mx, pw1_mx, p1[:, 1, :], windows[1])
-        qm0 = new_grouped()
-        cast_plain_cols(qm0, qm0_raw, slice(0, P))
-        ds0 = held.tile([P, PACK, N], F32, name="ds0", tag="dom1_high", align_bytes=64)
-        for t in range(PACK):
-            product(banks[4 + t], do0_mx, t, v0_mx)
-            nc.scalar.activation(
-                q0_raw[:, t, :], banks[4 + t][:], ACT.Identity, bias=shift0[:, t : t + 1], scale=rw_sb[:, 0, t : t + 1]
-            )
-            nc.gpsimd.tensor_tensor(ds0[:, t, :], q0_raw[:, t, :], p0[:, t, :], ALU.mult)
-        place(out_1, 1, 2, banks[4], dom1_mx, pw1_mx, p1[:, 2, :], windows[2])
-        cast_plain_cols(qm0, qm0_raw, slice(P, 4 * P))
-        qm0_mx = quantize(qm0, E4M3, "qm0")
-        do1_mx = quantize(cast_by_query(do1_raw), E5M2, "do1")
-        ds0_mx = quantize(cast_plain(ds0, "ds0_grouped"), E5M2, "ds0")
-        place(out_1, 1, 3, banks[5], dom1_mx, pw1_mx, q0_raw[:, 3, :], windows[3])
-        ds1 = held.tile([P, PACK, N], F32, name="ds1", tag="p0", align_bytes=64)
-        shifted1 = ds0
-        for t in range(PACK):
-            bank = banks[(4, 6, 0, 1)[t]]
-            if t >= 2:
-                place(out_0, 0, t - 2, bank, qm0_mx, ds0_mx, do1_raw[:, t - 2, :], windows[t - 2])
-            product(bank, do1_mx, t, v1_mx)
-            nc.scalar.activation(shifted1[:, t, :], bank[:], ACT.Identity, bias=neg_delta1[:, t : t + 1])
-            nc.gpsimd.tensor_tensor(ds1[:, t, :], shifted1[:, t, :], pw1[:, t, :], ALU.mult)
-        place(out_0, 0, 2, banks[2], qm0_mx, ds0_mx, do1_raw[:, 2, :], windows[2])
-        qm1_mx = quantize(cast_plain(qm1_raw, "ds0_grouped"), E4M3, "qm1")
-        ds1_mx = quantize(cast_plain(ds1), E5M2, "ds1")
-        place(out_0, 0, 3, banks[3], qm0_mx, ds0_mx, shifted1[:, 3, :], windows[3])
         for c in range(4):
-            place(out_0, 1, c, banks[4 + c], qm1_mx, ds1_mx, qm1_raw[:, c, :], windows[c])
+            product(banks[c], dom0_mx, c, pw0_mx)
+            nc.scalar.copy(q0_raw[:, c, :], banks[c][:])
+        for c in range(4):
+            scalar_scatter(windows[c], 0, q0_raw[:, c, :])
+
+        pw1 = gated(new_grouped(), p1, 1)
+        v0_mx = gather(v_pool_words, 0, U32, "v0_codes"), v0_scales, E4M3
+        pw1_mx = quantize(pw1, E4M3, "pw1")
+        do0_mx = quantize(vector_cast_by_query(new_grouped("do0_grouped"), do0_raw), E5M2, "do0")
+        v1_mx = gather(v_pool_words, 1, U32, "v1_codes", tag="do0_grouped"), v1_scales, E4M3
+        centred(dom0_raw, do0_mx, v0_mx, p0, 0)
+        for c in range(4):
+            product(banks[c], dom1_mx, c, pw1_mx)
+            nc.scalar.copy(q1_raw[:, c, :], banks[c][:])
+        for c in range(4):
+            scalar_scatter(windows[c], 1, q1_raw[:, c, :])
+            store(out_1, c, windows[c])
+
+        do1_grouped = vector_cast_by_query(new_grouped(), do1_raw)
+        ds0 = gated(new_grouped(), dom0_raw, 0)
+        do1_mx = quantize(do1_grouped, E5M2, "do1")
+        ds0_mx = quantize(ds0, E5M2, "ds0")
+        qm0_grouped = vector_cast(new_grouped(), qm0_raw)
+        centred(dom1_raw, do1_mx, v1_mx, p1, 1)
+        qm0_mx = quantize(qm0_grouped, E4M3, "qm0")
+        ds1 = gated(new_grouped(), dom1_raw, 1)
+        qm1_grouped = vector_cast(new_grouped(), qm1_raw)
+        ds1_mx = quantize(ds1, E5M2, "ds1")
+        qm1_mx = quantize(qm1_grouped, E4M3, "qm1")
+
+        key_windows = [windows[4], windows[0], windows[1], windows[2]]
+        for c in range(4):
+            product(banks[c], qm0_mx, c, ds0_mx)
+        for c in range(4):
+            product(banks[4 + c], qm1_mx, c, ds1_mx)
+        nc.vector.tensor_copy(do0_raw[:, 0, :], banks[0][:])
+        vector_scatter(key_windows[0], 0, do0_raw[:, 0, :])
+        nc.vector.tensor_copy(dom1_raw[:, 0, :], banks[4][:])
+        nc.vector.tensor_copy(dom1_raw[:, 1, :], banks[1][:])
+        vector_scatter(key_windows[0], 1, dom1_raw[:, 0, :])
+        store(out_0, 0, key_windows[0])
+        nc.vector.tensor_copy(dom1_raw[:, 2, :], banks[5][:])
+        vector_scatter(key_windows[1], 0, dom1_raw[:, 1, :])
+        nc.vector.tensor_copy(dom1_raw[:, 3, :], banks[6][:])
+        vector_scatter(key_windows[1], 1, dom1_raw[:, 2, :])
+        store(out_0, 1, key_windows[1])
+        nc.scalar.copy(q1_raw[:, 2, :], banks[2][:])
+        nc.scalar.copy(q1_raw[:, 0, :], banks[3][:])
+        scalar_scatter(key_windows[2], 0, q1_raw[:, 2, :])
+        nc.scalar.copy(q1_raw[:, 1, :], banks[7][:])
+        scalar_scatter(key_windows[3], 0, q1_raw[:, 0, :])
+        scalar_scatter(key_windows[3], 1, q1_raw[:, 1, :])
+        store(out_0, 3, key_windows[3])
+        vector_scatter(key_windows[2], 1, dom1_raw[:, 3, :])
+        store(out_0, 2, key_windows[2])

from contextlib import ExitStack

import concourse.mybir as mybir

B, N, T, D, DV, R = 2, 512, 2048, 512, 512, 512
FLOPS = 4 * 2 * B * R * N * D

F32 = mybir.dt.float32
BF16 = mybir.dt.bfloat16
I32 = mybir.dt.int32
U32 = mybir.dt.uint32
U16 = mybir.dt.uint16
U8 = mybir.dt.uint8
E4M3 = mybir.dt.float8_e4m3fn_x4
E5M2 = mybir.dt.float8_e5m2_x4
ACT = mybir.ActivationFunctionType
ALU = mybir.AluOpType

P = 128
PACK = 4
LIST_COLS = N // 16


def tile_attend_gat_lse_kv_kernel(
    tc, qT, k_words, k_scales, v_words, v_scales, doT, lse, delta, rw, qm, dom, offs, out_0, out_1
):
    nc = tc.nc
    with ExitStack() as ctx:
        held = ctx.enter_context(tc.tile_pool(name="held", bufs=1))
        groups = ctx.enter_context(tc.tile_pool(name="groups", bufs=4))
        psum = ctx.enter_context(tc.psum_pool(name="psum", bufs=1))
        banks = [psum.tile([P, 512], F32, name=f"bank{n}") for n in range(8)]

        offsets = held.tile([P, B * LIST_COLS], U16, name="offsets")
        nc.sync.dma_start(offsets[:], offs)

        def load_rows(rows, name):
            raw = held.tile([P, PACK, rows.shape[1]], F32, name=name, align_bytes=64)
            nc.sync.dma_start(out=raw[:], in_=rows.rearrange("(p j) w -> p j w", j=PACK))
            return raw

        def load_words(pool_words, words, tokens):
            nc.sync.dma_start(
                out=pool_words[:, tokens].bitcast(I32), in_=words[0].rearrange("p n t -> p (n t)").bitcast(I32)[:, tokens]
            )

        def new_scales(name):
            pool_scales = held.tile([P, T], U8, name=name, align_bytes=64)
            nc.vector.memset(pool_scales[:].bitcast(I32), 0)
            return pool_scales

        def load_scales(pool_scales, scales, rows):
            for row in rows:
                nc.sync.dma_start(out=pool_scales[row:P:32, :].bitcast(I32), in_=scales[0, row:16:4, :].bitcast(I32))

        def load_per_query(vec, name):
            col = held.tile([P, B, PACK], F32, name=name, align_bytes=64)
            nc.sync.dma_start(out=col[:], in_=vec.rearrange("b (p t) o -> p b (t o)", t=PACK))
            return col

        halves = (slice(0, 256), slice(256, 512))
        lse_sb = load_per_query(lse, "lse_sb")
        k_pool_scales, v_pool_scales = new_scales("k_pool_scales"), new_scales("v_pool_scales")
        load_scales(k_pool_scales, k_scales, range(4))
        k_pool_words = held.tile([P, T], U32, name="k_pool_words", align_bytes=64)
        v_pool_words = held.tile([P, T], U32, name="v_pool_words", align_bytes=64)
        q0_raw = load_rows(qT[0], "q0_raw")
        load_words(k_pool_words, k_words, slice(0, T))
        rw_sb = load_per_query(rw, "rw_sb")
        load_scales(v_pool_scales, v_scales, range(4))
        q1_raw = load_rows(qT[1], "q1_raw")
        dom0_raw = load_rows(dom[0], "dom0_raw")
        dom1_raw = load_rows(dom[1], "dom1_raw")
        load_words(v_pool_words, v_words, slice(0, T))
        do0_raw = load_rows(doT[0], "do0_raw")
        delta_sb = load_per_query(delta, "delta_sb")
        do1_raw = load_rows(doT[1], "do1_raw")
        qm0_raw = load_rows(qm[0], "qm0_raw")
        qm1_raw = load_rows(qm[1], "qm1_raw")

        neg_lse = held.tile([P, B, PACK], F32, name="neg_lse")
        nc.scalar.mul(neg_lse[:], lse_sb[:], -1.0)

        def new_window(name, clear=nc.vector, tag=None):
            window = held.tile([P, T], F32, name=name, tag=tag or name, align_bytes=64)
            clear.memset(window[:].bitcast(I32), 0)
            return window

        windows = [new_window(f"window{c}") for c in range(3)]

        def gather(pool_tile, b, dtype, name, tag=None, parts=1):
            picked = held.tile([P, N], dtype, name=name, tag=tag or name, align_bytes=64)
            for h in range(parts):
                entries = slice((b * parts + h) * LIST_COLS // parts, (b * parts + h + 1) * LIST_COLS // parts)
                nc.vector.tensor_copy(picked[:, h * N // parts : (h + 1) * N // parts], pool_tile[:].indirect(offsets[:, entries]))
            return picked

        def gather_all(pool_tile, dtype, name):
            picked = held.tile([P, B * N], dtype, name=name, align_bytes=64)
            nc.vector.tensor_copy(picked[:], pool_tile[:].indirect(offsets[:]))
            return [picked[:, b * N : (b + 1) * N] for b in range(B)]

        def new_mx(name, fmt, tag=None):
            codes = held.tile([P, 512], U32, name=name + "_codes", tag=tag or name + "_codes", align_bytes=64)
            scales = held.tile([P, 512], U8, name=name + "_scales", align_bytes=64)
            return codes, scales, fmt

        def quantize_cols(mx, grouped, cols):
            nc.vector.quantize_mx(
                out=mx[0][:, cols].bitcast(mx[2]), scales=mx[1][:, cols], in_=grouped[:, PACK * cols.start : PACK * cols.stop]
            )

        def quantize_half(mx, grouped, cols):
            nc.vector.quantize_mx(out=mx[0][:, cols].bitcast(mx[2]), scales=mx[1][:, cols], in_=grouped[:])

        def quantize(grouped, fmt, name, tag=None):
            mx = new_mx(name, fmt, tag)
            quantize_cols(mx, grouped, slice(0, 512))
            return mx

        def new_grouped(tag=None):
            if tag:
                return held.tile([P, 512 * PACK], BF16, name="grouped_on_" + tag, tag=tag, align_bytes=64)
            return groups.tile([P, 512 * PACK], BF16, name="grouped", align_bytes=64)

        def interleaved(grouped):
            return grouped[:].rearrange("p (c i t) -> p c t i", i=4, t=PACK)

        def by_fours(planes):
            return planes[:].rearrange("p t (c i) -> p c t i", i=4)

        def cast_plain_cols(grouped, raw, cols):
            fours = slice(cols.start // 4, cols.stop // 4)
            nc.scalar.copy(interleaved(grouped)[:, fours], by_fours(raw)[:, fours])

        def cast_plain(raw, tag=None):
            grouped = new_grouped(tag)
            cast_plain_cols(grouped, raw, slice(0, 512))
            return grouped

        def first_columns(mx, raw, name, tag=None):
            first = held.tile([P, P * PACK], BF16, name=name, tag=tag or name, align_bytes=64)
            nc.scalar.copy(interleaved(first), by_fours(raw)[:, : P // 4])
            quantize_half(mx, first, slice(0, P))

        def some_columns(mx, raw, cols, name):
            part = held.tile([P, P * PACK], BF16, name=name, align_bytes=64)
            nc.scalar.copy(interleaved(part), by_fours(raw)[:, cols.start // 4 : cols.stop // 4])
            quantize_half(mx, part, cols)

        def cast_by_query(raw, tag=None):
            grouped = new_grouped(tag)
            nc.scalar.copy(
                grouped[:].rearrange("p (t m j) -> p m j t", t=PACK, j=PACK),
                raw[:].rearrange("p j (m t) -> p m j t", t=PACK),
            )
            return grouped

        def product(bank, stationary, c, moving, slots=slice(0, N)):
            cols = slice(c * P, (c + 1) * P)
            nc.tensor.matmul_mx(
                out=bank[:, slots],
                lhsT=stationary[0][:, cols].bitcast(stationary[2]),
                lhsT_scale=stationary[1][:, cols],
                rhs=moving[0][:, slots].bitcast(moving[2]),
                rhs_scale=moving[1][:, slots],
                start=True,
                stop=True,
            )

        def half_columns(mx, raw, cols, tag):
            half = held.tile([P, 256 * PACK], BF16, name="half_on_" + tag, tag=tag, align_bytes=64)
            nc.scalar.copy(interleaved(half), by_fours(raw)[:, cols.start // 4 : cols.stop // 4])
            quantize_half(mx, half, cols)

        def vector_cast(grouped, raw, cols=slice(0, 512)):
            fours = slice(cols.start // 4, cols.stop // 4)
            nc.vector.tensor_copy(interleaved(grouped), by_fours(raw)[:, fours])
            return grouped

        def vector_cast_by_query(grouped, raw):
            nc.vector.tensor_copy(
                grouped[:].rearrange("p (t m j) -> p m j t", t=PACK, j=PACK),
                raw[:].rearrange("p j (m t) -> p m j t", t=PACK),
            )
            return grouped

        def gated(grouped, planes, b, slots=slice(0, N)):
            fours = slice(slots.start // 4, slots.stop // 4)
            gate = rw_sb[:, b, :].unsqueeze(1).unsqueeze(3).broadcast_to([P, fours.stop - fours.start, PACK, 4])
            nc.vector.tensor_tensor(interleaved(grouped)[:, fours], by_fours(planes)[:, fours], gate, ALU.mult)
            return grouped

        def listed(window, b, slots):
            return window[:].indirect(offsets[:, (b * N + slots.start) // 16 : (b * N + slots.stop) // 16])

        def scalar_scatter(window, b, staged):
            for slots in halves:
                nc.scalar.activation(listed(window, b, slots), staged[:, slots], ACT.Copy)

        def vector_scatter(window, b, staged):
            nc.vector.tensor_copy(listed(window, b, slice(0, N)), staged)

        def store(out, c, window):
            nc.sync.dma_start(out=out[c * P : (c + 1) * P, :], in_=window[:])

        def centred(planes, do_mx, v_mx, probs, b):
            for t in range(PACK):
                product(banks[4 + t], do_mx, t, v_mx)
                nc.vector.scalar_tensor_tensor(
                    planes[:, t, :], banks[4 + t][:], delta_sb[:, b, t : t + 1], probs[:, t, :], ALU.subtract, ALU.mult
                )

        def gather_part(picked, pool_tile, entries):
            nc.vector.tensor_copy(picked[:, entries], pool_tile[:].indirect(offsets[:, entries.start // 16 : entries.stop // 16]))

        k_picked_scales = gather_all(k_pool_scales, U8, "k_scales")
        windows.append(new_window("window3"))
        k_codes = held.tile([P, B * N], U32, name="k_codes", align_bytes=64)
        k0_mx = k_codes[:, :N], k_picked_scales[0], E4M3
        k1_mx = k_codes[:, N:], k_picked_scales[1], E4M3
        gather_part(k_codes, k_pool_words, halves[0])
        q0_mx = new_mx("q0", E4M3)
        q0_rows = q0_raw[:].rearrange("p j (m t) -> p m j t", t=PACK)
        for h in range(2):
            part = held.tile([P, 256 * PACK], BF16, name=f"q0_part{h}", align_bytes=64)
            nc.scalar.copy(part[:].rearrange("p (t m j) -> p m j t", t=2, j=PACK), q0_rows[:, :, :, 2 * h : 2 * h + 2])
            quantize_half(q0_mx, part, halves[h])
        gather_part(k_codes, k_pool_words, halves[1])
        gather_part(k_codes, k_pool_words, slice(N, 2 * N))
        p0 = held.tile([P, PACK, N], F32, name="p0", align_bytes=64)
        v0_scales = gather(v_pool_scales, 0, U8, "v0_scales")
        pw0 = new_grouped("pw0_grouped")
        for h, slots in enumerate(halves):
            for t in range(PACK):
                bank = banks[4 * h + t]
                product(bank, q0_mx, t, k0_mx, slots)
                nc.scalar.activation(p0[:, t, slots], bank[:, slots], ACT.Exp, bias=neg_lse[:, 0, t : t + 1])
            gated(pw0, p0, 0, slots)
        q1_mx = quantize(cast_by_query(q1_raw, "q1_grouped"), E4M3, "q1")
        pw0_mx = quantize(pw0, E4M3, "pw0", tag="q1_grouped")
        v1_scales = gather(v_pool_scales, 1, U8, "v1_scales", tag="pw0_grouped")
        dom1_grouped = held.tile([P, 512 * PACK], BF16, name="dom1_grouped", align_bytes=64)
        dom0_mx = quantize(cast_plain(dom0_raw), E5M2, "dom0")
        dom1_mx = quantize(vector_cast(dom1_grouped, dom1_raw), E5M2, "dom1")
        windows.append(new_window("window4", clear=nc.gpsimd, tag="dom1_grouped"))

        p1 = held.tile([P, PACK, N], F32, name="p1", tag="k_pool_words", align_bytes=64)
        for t in range(PACK):
            product(banks[4 + t], q1_mx, t, k1_mx)
            nc.scalar.activation(p1[:, t, :], banks[4 + t][:], ACT.Exp, bias=neg_lse[:, 1, t : t + 1])
        for c in range(4):
            product(banks[c], dom0_mx, c, pw0_mx)
            nc.scalar.copy(q0_raw[:, c, :], banks[c][:])
        for c in range(4):
            scalar_scatter(windows[c], 0, q0_raw[:, c, :])

        pw1 = gated(new_grouped(), p1, 1)
        v0_mx = gather(v_pool_words, 0, U32, "v0_codes"), v0_scales, E4M3
        pw1_mx = quantize(pw1, E4M3, "pw1")
        do0_mx = quantize(vector_cast_by_query(new_grouped("do0_grouped"), do0_raw), E5M2, "do0")
        v1_mx = gather(v_pool_words, 1, U32, "v1_codes", tag="do0_grouped"), v1_scales, E4M3
        centred(dom0_raw, do0_mx, v0_mx, p0, 0)
        for c in range(4):
            product(banks[c], dom1_mx, c, pw1_mx)
            nc.scalar.copy(q1_raw[:, c, :], banks[c][:])
        for c in range(4):
            scalar_scatter(windows[c], 1, q1_raw[:, c, :])
            store(out_1, c, windows[c])

        do1_grouped = vector_cast_by_query(new_grouped(), do1_raw)
        ds0 = gated(new_grouped(), dom0_raw, 0)
        do1_mx = quantize(do1_grouped, E5M2, "do1")
        ds0_mx = quantize(ds0, E5M2, "ds0")
        qm0_grouped = vector_cast(new_grouped(), qm0_raw)
        centred(dom1_raw, do1_mx, v1_mx, p1, 1)
        qm0_mx = quantize(qm0_grouped, E4M3, "qm0")
        ds1 = gated(new_grouped(), dom1_raw, 1)
        qm1_grouped = vector_cast(new_grouped(), qm1_raw)
        ds1_mx = quantize(ds1, E5M2, "ds1")
        qm1_mx = quantize(qm1_grouped, E4M3, "qm1")

        key_windows = [windows[4], windows[0], windows[1], windows[2]]
        for c in range(4):
            product(banks[c], qm0_mx, c, ds0_mx)
        for c in range(4):
            product(banks[4 + c], qm1_mx, c, ds1_mx)
        nc.vector.tensor_copy(do0_raw[:, 0, :], banks[0][:])
        vector_scatter(key_windows[0], 0, do0_raw[:, 0, :])
        nc.vector.tensor_copy(dom1_raw[:, 0, :], banks[4][:])
        nc.vector.tensor_copy(dom1_raw[:, 1, :], banks[1][:])
        vector_scatter(key_windows[0], 1, dom1_raw[:, 0, :])
        store(out_0, 0, key_windows[0])
        nc.vector.tensor_copy(dom1_raw[:, 2, :], banks[5][:])
        vector_scatter(key_windows[1], 0, dom1_raw[:, 1, :])
        nc.vector.tensor_copy(dom1_raw[:, 3, :], banks[6][:])
        vector_scatter(key_windows[1], 1, dom1_raw[:, 2, :])
        store(out_0, 1, key_windows[1])
        nc.scalar.copy(q1_raw[:, 2, :], banks[2][:])
        nc.scalar.copy(q1_raw[:, 0, :], banks[3][:])
        scalar_scatter(key_windows[2], 0, q1_raw[:, 2, :])
        nc.scalar.copy(q1_raw[:, 1, :], banks[7][:])
        scalar_scatter(key_windows[3], 0, q1_raw[:, 0, :])
        scalar_scatter(key_windows[3], 1, q1_raw[:, 1, :])
        store(out_0, 3, key_windows[3])
        vector_scatter(key_windows[2], 1, dom1_raw[:, 3, :])
        store(out_0, 2, key_windows[2])
